import numpy as np, ml_dtypes
CORES = [6,15,38,47]
N = 4
BF = ml_dtypes.bfloat16
def f(rng, *shape):
    return (rng.standard_normal(shape, dtype=np.float32) * np.exp2(rng.integers(-2, 3, shape[:-1] + (1,)))).astype(BF)
def wide(rng, *shape):
    v = f(rng, *shape).astype(np.float32); k = shape[:-2] + (1, shape[-1])
    return (v * np.exp2(rng.integers(-6, 7, k)) * (rng.random(k) > 0.0625)).astype(BF)
def gentries(a):
    return np.ascontiguousarray(a.reshape(8, 16, -1).transpose(0, 2, 1)).reshape(8, -1)
def gtable(e):
    e = np.asarray(e); return np.ascontiguousarray(e.reshape(8, -1, 16).transpose(0, 2, 1)).reshape(128, -1).astype(np.int32)
W, F, U, CAP, SW = 7, 64, 2, 8, 2
C = W * F; Z = C + (W - 1) * N * CAP
def pack(x):
    return np.stack([gtable(v.reshape(8, -1)) for v in x])
def unpack(x):
    return np.stack([gentries(v) for v in x])
def sends(rng, full):
    x = np.argsort(rng.random((N, 8, W - 1, N, F)), axis=-1)[..., :CAP] + F * np.arange(W - 1).reshape(1, 1, W - 1, 1, 1)
    n = rng.integers(0, CAP + 1, (N, 8, W - 1, N, 1)); n[0, :, 0, 1] = CAP
    if full: n[:] = CAP
    keep = (np.argsort(rng.random(x.shape), axis=-1) < n) & (np.arange(N).reshape(N, 1, 1, 1, 1) != np.arange(N).reshape(1, 1, 1, N, 1))
    return np.where(keep, x, Z)
def upwind(rng, far, none):
    s = (N, 8, W, U, F); r = np.arange(N).reshape(N, 1, 1, 1, 1); w = np.arange(W).reshape(1, 1, W, 1, 1)
    v = np.where(rng.random(s) < 0.75, w - 1, (rng.random(s) * w).astype(np.int64))
    near = v * F + rng.integers(0, F, s); away = C + (v * N + (r + 1 + rng.integers(0, N - 1, s)) % N) * CAP + rng.integers(0, CAP, s)
    p = rng.random(s)
    return np.where(w == 0, Z, np.where(p < far, away, np.where(p < far + none, Z, near)))
def draw(rng, o, p, x):
    return {"qs": f(rng, N, 128, C), "rm": (0.5 + 0.5 * rng.random((N, 128, C))).astype(BF), "co": (0.75 * rng.random((N, 128, U * C))).astype(BF),
            "sc": (f(rng, N, 16, 16).astype(np.float32) * np.float32(0.0625)).astype(BF), "seq": pack(o), "up": pack(p), "snd": pack(x)}
def orders(rng):
    return np.argsort(rng.random((N, 8, C)), axis=-1)
def setup_inputs(rng):
    return draw(rng, orders(rng), upwind(rng, 0.5, 0.1), sends(rng, False))
def setup_inputs_full(rng):
    return draw(rng, orders(rng), upwind(rng, 0.9, 0.0), sends(rng, True))
def setup_inputs_chain(rng):
    w = np.arange(W).reshape(1, 1, W, 1, 1); r = np.arange(N).reshape(N, 1, 1, 1, 1); x = sends(rng, True)
    p = np.where(w == 0, Z, C + ((w - 1) * N + (r + 1) % N) * CAP + rng.integers(0, CAP, (N, 8, W, U, F)))
    other = np.arange(N).reshape(N, 1, 1, 1) != np.arange(N).reshape(1, 1, 1, N); a = F * np.arange(W - 1).reshape(1, 1, W - 1, 1)
    x[..., 0] = np.where(other, a, Z); x[..., CAP - 1] = np.where(other, a + F - 1, Z)
    return draw(rng, orders(rng), p, x)
def setup_inputs_alike(rng):
    x = sends(rng, True); x[:] = x[..., :1].copy(); p = upwind(rng, 0.5, 0.1); p = np.repeat(p[:, :, :, :1], U, axis=3)
    o = orders(rng); o[:, 0] = np.arange(C); o[:, 1] = np.arange(C)[::-1]; o[:, 3] = o[:, 2]
    return draw(rng, o, p, x)
def setup_inputs_few(rng):
    x = sends(rng, False); k = int(rng.integers(0, N)); x[k] = Z; x[:, :, :, k] = Z
    d = draw(rng, orders(rng), upwind(rng, 0.08, 0.85), x); d["rm"] = np.where(rng.random(d["rm"].shape) < 0.125, np.float32(0), d["rm"].astype(np.float32)).astype(BF)
    return d
def setup_inputs_spread(rng):
    d = setup_inputs(rng); d["qs"] = wide(rng, N, 128, C); return d
def check_inputs(d):
    bad = []
    if not (np.sort(unpack(d["seq"]), axis=-1) == np.arange(C)).all(): bad.append("seq")
    p = unpack(d["up"]).reshape(N, 8, W, U * F).astype(np.int64); w = np.arange(W).reshape(1, 1, W, 1); r = np.arange(N).reshape(N, 1, 1, 1); s = p - C
    if not ((p == Z) | ((p >= 0) & (p < w * F)) | ((s >= 0) & (s < w * N * CAP) & ((s // CAP) % N != r))).all(): bad.append("up")
    x = unpack(d["snd"]).reshape(N, 8, W - 1, N, CAP).astype(np.int64); w = np.arange(W - 1).reshape(1, 1, W - 1, 1, 1)
    other = np.arange(N).reshape(N, 1, 1, 1, 1) != np.arange(N).reshape(1, 1, 1, N, 1)
    if not ((x == Z) | ((x >= w * F) & (x < w * F + F) & other)).all(): bad.append("snd")
    if not all(np.isfinite(d[k].astype(np.float32)).all() for k in ("qs", "rm", "co", "sc")): bad.append("finite")
    return bad
def reference(qs, rm, co, sc, seq, up, snd):
    o = unpack(seq).astype(np.int64); p = unpack(up).astype(np.int64); x = unpack(snd).astype(np.int64)
    src = qs.astype(np.float64).reshape(N, 8, 16, C); rem = rm.astype(np.float64).reshape(N, 8, 16, C); a = co.astype(np.float64).reshape(N, 8, 16, W, U, F)
    s = sc.astype(np.float64).transpose(0, 2, 1); y = np.zeros((N, 16, C), np.float64)
    for k in range(SW):
        win = np.zeros((N, 8, 16, Z + 1), np.float64)
        for w in range(W):
            c = o[:, :, None, w * F:w * F + F]
            h = np.take_along_axis(win, p[:, :, None, w * U * F:(w + 1) * U * F], 3).reshape(N, 8, 16, U, F)
            v = (np.take_along_axis(src, c, 3) + np.sum(a[:, :, :, w] * h, axis=3)) * np.take_along_axis(rem, c, 3)
            v = np.maximum(v, 0.0)
            win[..., w * F:w * F + F] = v
            if w == W - 1: continue
            for r in range(N):
                for q in range(N):
                    if q == r: continue
                    b = C + (w * N + r) * CAP; e = (w * N + q) * CAP
                    win[q, :, :, b:b + CAP] = np.take_along_axis(win[r], x[r][:, None, e:e + CAP], 2)
        psi = np.zeros((N, 8, 16, C), np.float64); np.put_along_axis(psi, o[:, :, None], win[..., :C], 3)
        flux = np.sum(psi, axis=1); y = y + flux
        src = np.repeat(np.matmul(s, flux)[:, None], 8, axis=1)
    return {"y": y.astype(np.float32)}

@@ -1,0 +1,709 @@
+from concourse.bass import DstId, RemoteDMATransfer
+from concourse.mybir import AluOpType as O, ActivationFunctionType as AF
+
+W, F, U, CAP, SW, NR = 7, 64, 2, 8, 2, 4
+C = W * F
+Z = C + (W - 1) * NR * CAP
+NS = NR * CAP
+BW = 328
+HD = 104
+WIN = HD + BW * (W - 1) + 192
+CR = 136
+BIG = 9.0e29
+OFF = 4096.0
+CELLS = (128, 128, 96, 96)
+KQ = {"v": 8, "s": 8, "t": 2, "g": 2}
+NXS = 108
+FULL = {(0, 2), (0, 4), (1, 0), (1, 2), (1, 4)}
+PLAIN = {(0, 0): CAP, (0, 1): 3 * CAP}
+PAIRS = (3, 5, 1)
+
+
+def own_at(w):
+    return HD + BW * w
+
+
+def slot_at(w):
+    return HD + BW * w + 200
+
+
+SCRATCH = {
+    "seq32": ("sbuf", [128, 28], "int32"), "up32": ("sbuf", [128, 56], "int32"), "snd32": ("sbuf", [128, 12], "int32"),
+    "qsb": ("sbuf", [128, C], "bfloat16"), "rmb": ("sbuf", [128, C], "bfloat16"), "cob": ("sbuf", [128, 2 * C], "bfloat16"),
+    "scb": ("sbuf", [128, 16], "bfloat16"), "scf": ("sbuf", [128, 16], "float32"),
+    "seq16": ("sbuf", [128, 28], "uint16"), "up16": ("sbuf", [128, 56], "uint16"), "upr16": ("sbuf", [128, 56], "uint16"),
+    "rmp": ("sbuf", [128, C], "float32"), "cr": ("sbuf", [128, CR * W], "float32"), "z0": ("sbuf", [128, F], "float32"),
+    "win0": ("sbuf", [128, WIN], "float32"), "win1": ("sbuf", [128, WIN], "float32"),
+    "psic0": ("sbuf", [128, 512], "float32"), "psic1": ("sbuf", [128, 512], "float32"), "src": ("sbuf", [128, 512], "float32"),
+    "dbs": ("sbuf", [128, 200], "float32"), "ebs": ("sbuf", [128, 200], "float32"),
+    "tab": ("sbuf", [128, Z + 8], "float32"), "zer": ("sbuf", [128, 304], "float32"), "neg": ("sbuf", [128, 200], "float32"),
+    "iot": ("sbuf", [128, 128], "int32"), "iam": ("sbuf", [128, 128], "int32"), "mskw": ("sbuf", [128, 128], "float32"),
+    "pi": ("sbuf", [128, 4], "int32"), "p7": ("sbuf", [128, 4], "int32"), "p8": ("sbuf", [128, 4], "int32"),
+    "ph": ("sbuf", [128, 4], "float32"), "pv": ("sbuf", [128, 4], "float32"), "k18": ("sbuf", [128, 18], "float32"),
+    "pa": ("sbuf", [128, 2], "float32"), "pb": ("sbuf", [128, 2], "float32"), "pl": ("sbuf", [128, 2], "uint16"),
+    "uH": ("sbuf", [128, 48], "int32"), "uL": ("sbuf", [128, 48], "int32"), "ut": ("sbuf", [128, 48], "int32"),
+    "s1": ("sbuf", [128, 12], "float32"), "s2": ("sbuf", [128, 12], "float32"), "s3": ("sbuf", [128, 12], "float32"),
+    "s5": ("sbuf", [128, 12], "float32"), "s6": ("sbuf", [128, 12], "float32"), "s7": ("sbuf", [128, 12], "float32"),
+    "l0": ("sbuf", [128, 2], "uint16"), "l1": ("sbuf", [128, 2], "uint16"),
+    "l96f": ("sbuf", [128, 18], "float32"), "l96g": ("sbuf", [128, 18], "float32"), "l96": ("sbuf", [128, 18], "uint16"),
+    "fo": ("sbuf", [128, 64], "float32"), "cum": ("sbuf", [128, 80], "float32"), "r4": ("sbuf", [128, 4], "float32"),
+    "fo2": ("sbuf", [128, 64], "float32"), "cum2": ("sbuf", [128, 80], "float32"), "r42": ("sbuf", [128, 4], "float32"),
+    "screp": ("sbuf", [128, 128], "float32"), "yo": ("sbuf", [128, 128], "float32"),
+    "qa": ("sbuf", [128, 28], "int32"), "qb": ("sbuf", [128, 28], "int32"), "qc": ("sbuf", [128, 28], "int32"),
+    "qd": ("sbuf", [128, 28], "float32"), "qe": ("sbuf", [128, 28], "float32"), "qf": ("sbuf", [128, 28], "float32"),
+    "qg": ("sbuf", [128, 28], "float32"), "seqp": ("sbuf", [128, 28], "uint16"),
+    "ps": ("psum", [128, 2048], "float32"), "pf": ("psum", [128, 2048], "float32"),
+}
+for _n in ("ua", "ub", "uc", "ud", "ue", "uf", "ug", "uh", "ui", "uj", "uk", "um", "un", "uo"):
+    SCRATCH[_n] = ("sbuf", [128, 48], "float32")
+for _i in range(4):
+    SCRATCH["dbl%d" % _i] = ("sbuf", [128, 392], "float32")
+for _k in FULL:
+    SCRATCH["sb%d_%d" % _k] = ("sbuf", [128, 96], "float32")
+for _k in PLAIN:
+    SCRATCH["sb%d_%d" % _k] = ("sbuf", [128, 4 * PLAIN[_k]], "float32")
+for _x in PAIRS:
+    SCRATCH["upf%d" % _x] = ("sbuf", [128, CR], "float32")
+    SCRATCH["ix%d" % _x] = ("sbuf", [128, 4], "uint16")
+    SCRATCH["bx%d" % _x] = ("sbuf", [128, 2], "uint16")
+    SCRATCH["px%d" % _x] = ("sbuf", [128, 4], "uint16")
+    SCRATCH["ex%d" % _x] = ("sbuf", [128, 4], "uint16")
+    SCRATCH["sp%d" % _x] = ("sbuf", [128, 128], "float32")
+    SCRATCH["pk%d" % _x] = ("sbuf", [128, 96], "float32")
+    SCRATCH["lp%d" % _x] = ("sbuf", [128, 128], "float32")
+    SCRATCH["ce%d" % _x] = ("sbuf", [128, 128], "float32")
+SEMAPHORES = (["x%d" % i for i in range(NXS)] + ["arr%d_%d" % k for k in sorted(FULL | set(PLAIN))]
+              + ["pre%d" % x for x in PAIRS] + ["q_%s%d" % (q, i) for q in KQ for i in range(KQ[q])] + ["sent"])
+PSUM = ("ps", "pf")
+
+
+def send_calls(topo, src, dests):
+    far = [d for d in dests if not topo.mates(topo.chip(src), topo.chip(d))]
+    near = [d for d in dests if topo.mates(topo.chip(src), topo.chip(d))]
+    far.sort(key=lambda d: topo.same_plane(topo.chip(src), topo.chip(d)))
+    calls = []
+    if len(far) == 2 and len(near) == 1:
+        e = [topo.engines(src, d) for d in far]
+        h = len(e[0]) // 2
+        calls.append([(far[0], e[0][:h]), (far[1], e[1][h:])])
+        calls.append([(near[0], topo.engines(src, near[0]))])
+    else:
+        for d in far + near:
+            calls.append([(d, topo.engines(src, d))])
+    return calls
+
+
+def engines_to(topo, src, dst, dests):
+    return sum(len(e) for call in send_calls(topo, src, dests) for d, e in call if d == dst)
+
+
+def rank_program(g, core, T, topo):
+    rank = T.rank_of(core)
+    if rank is None:
+        return
+    cores = list(T.cores)
+    others = [c for c in cores if c != core]
+    queues = {"v": g.vector, "s": g.scalar, "t": g.tensor, "g": g, "y": g.sync}
+    ops, group, groups = [], [None], [0]
+
+    def together(on):
+        groups[0] += 1
+        group[0] = groups[0] if on else None
+
+    def reg(name, a, b, step=1):
+        return (name, a, b, step)
+
+    def R(name, a, b, step=1, p=128):
+        t = T[name]
+        ap = t[0:p, a:b] if step == 1 else t[0:p, a:b:step]
+        return (ap, [reg(name, a, b, step)])
+
+    def X(name, b, off, oa, ob, a=0):
+        return (T[name][:, a:b].indirect(T[off][:, oa:ob]), [reg(name, a, b), reg(off, oa, ob)])
+
+    def add_op(q, fn, reads, writes, kind="c", n=1, sem=None):
+        rd, wr = [], []
+        for x in reads:
+            rd += x
+        for x in writes:
+            wr += x
+        ops.append({"q": q, "fn": fn, "r": rd, "w": wr, "kind": kind, "n": n, "sem": sem, "grp": group[0]})
+
+    def split(out):
+        return [out[1][0:1]], [out[1][1:]]
+
+    def tt(out, a, b, op):
+        w, r = split(out)
+        add_op("v", lambda: g.vector.tensor_tensor(out=out[0], in0=a[0], in1=b[0], op=op), [a[1], b[1]] + r, w)
+
+    def ts(out, a, s1, op0, s2=None, op1=None):
+        if op1 is None:
+            add_op("v", lambda: g.vector.tensor_scalar(out=out[0], in0=a[0], scalar1=s1, scalar2=None, op0=op0), [a[1]], [out[1]])
+        else:
+            add_op("v", lambda: g.vector.tensor_scalar(out=out[0], in0=a[0], scalar1=s1, scalar2=s2, op0=op0, op1=op1), [a[1]], [out[1]])
+
+    def cp(out, a):
+        w, r = split(out)
+        add_op("v", lambda: g.vector.tensor_copy(out=out[0], in_=a[0]), [a[1]] + r, w)
+
+    def fill(out, v):
+        add_op("v", lambda: g.vector.memset(out[0], v), [], [out[1]])
+
+    def scan(out, d0, d1, op0, op1):
+        add_op("v", lambda: g.vector.tensor_tensor_scan(out=out[0], data0=d0[0], data1=d1[0], initial=0.0, op0=op0, op1=op1),
+               [d0[1], d1[1]], [out[1]])
+
+    def act(out, a, bias=0.0):
+        add_op("s", lambda: g.scalar.activation(out=out[0], in_=a[0], func=AF.Identity, bias=bias), [a[1]], [out[1]])
+
+    def relu(out, a, bias):
+        add_op("s", lambda: g.scalar.activation(out=out[0], in_=a[0], func=AF.Relu, bias=bias), [a[1]], [out[1]])
+
+    def zeros(name, a, b, step=1):
+        act(R(name, a, b, step), R("zer", 0, len(range(a, b, step))))
+
+    def negs(name, a, b, step=1):
+        act(R(name, a, b, step), R("neg", 0, len(range(a, b, step))))
+
+    def mm(out, lhsT, rhs, start=True, stop=True):
+        add_op("t", lambda: g.tensor.matmul(out=out[0], lhsT=lhsT[0], rhs=rhs[0], start=start, stop=stop), [lhsT[1], rhs[1]], [out[1]])
+
+    def turn(out, a):
+        add_op("v", lambda: g.vector.transpose(out=out[0], in_=a[0]), [a[1]], [out[1]])
+
+    def load(q, name, src, p=128):
+        n = SCRATCH[name][1][1]
+        o = R(name, 0, n, 1, p)
+        add_op(q, lambda: queues[q].dma_start(o[0], src[:, :]), [], [o[1]], "dma", 16)
+
+    def iota(out, pattern, base, cm, flag):
+        if flag:
+            add_op("g", lambda: g.iota(out[0], pattern, base, cm, allow_small_or_imprecise_dtypes=True), [], [out[1]])
+        else:
+            add_op("g", lambda: g.iota(out[0], pattern, base, cm), [], [out[1]])
+
+    def message(sb, width, src_at, dst, dst_at, sem):
+        def one(call):
+            tr = []
+            for d, e in call:
+                rid, pid = topo.addr(d)[:2]
+                k = T.rank_of(d)
+                sa, da, m = src_at(k), dst_at(k), sum(1 << x for x in e)
+                if len(call) == 1:
+                    return g.remote_dma(out_ap=T[dst][:, da:da + width], in_ap=T[sb][:, sa:sa + width], remote_sem=T.sem[sem],
+                                        local_sem=T.sem["sent"], pid=pid, routing_id=rid, dma_engine_mask=m)
+                tr.append(RemoteDMATransfer(dst_ids=[DstId(rid=rid, pnc=pid)], dma_engine_mask=m, remote_sem=T.sem[sem],
+                                            src=T[sb][:, sa:sa + width], dst=T[dst][:, da:da + width]))
+            return g.remote_dma_fused(tr, local_sem=T.sem["sent"])
+
+        n = SCRATCH[sb][1][1]
+        for call in send_calls(topo, core, others):
+            add_op("g", lambda call=call: one(call), [[reg(sb, 0, n)]], [], "remote", sum(len(e) for d, e in call))
+
+    def landing(dst, width, at, sem):
+        n = sum(engines_to(topo, c, core, [d for d in cores if d != c]) for c in others)
+        add_op("ext", None, [], [[reg(dst, at(T.rank_of(c)), at(T.rank_of(c)) + width) for c in others]], "ext", n, sem)
+
+    def index_of(k):
+        return [T.rank_of(c) for c in others].index(k)
+
+    def plain_at(w, s, d):
+        if w % 2 == 0:
+            return slot_at(w) + 32 * s + 8 * d
+        return slot_at(w) + 32 + 24 * s
+
+    def send(s, w):
+        sb, win, sem = "sb%d_%d" % (s, w), "win%d" % s, "arr%d_%d" % (s, w)
+        if (s, w) in FULL:
+            message(sb, NS, lambda k: NS * index_of(k), win, lambda k: slot_at(w) + NS * rank, sem)
+            act(R(win, slot_at(w) + NS * rank, slot_at(w) + NS * rank + NS), R(sb, 0, NS))
+        else:
+            c = PLAIN[(s, w)]
+            message(sb, c, lambda k: c * k, win, lambda k: plain_at(w, rank, k), sem)
+
+    def arrival(s, w):
+        win, sem = "win%d" % s, "arr%d_%d" % (s, w)
+        if (s, w) in FULL:
+            landing(win, NS, lambda k: slot_at(w) + NS * k, sem)
+        else:
+            landing(win, PLAIN[(s, w)], lambda k: plain_at(w, k, rank), sem)
+
+    def own(s, w):
+        return R("win%d" % s, own_at(w) + 2, own_at(w) + 192, 3)
+
+    def chain_gather(s, w):
+        tt(R("dbl%d" % (w % 4), 1, 385, 3), X("win%d" % s, own_at(w), "up16", 8 * w, 8 * w + 8), R("cr", CR * w, CR * w + 128), O.mult)
+
+    def chain_scan(s, w):
+        d = "dbl%d" % (w % 4)
+        scan(R("win%d" % s, own_at(w), own_at(w) + 192), R(d, 0, 192), R(d, 193, 385), O.add, O.max)
+
+    def finish_gather(s, x):
+        w = x - 1
+        act(R("ebs", 2, 98, 3), X("win%d" % s, slot_at(w) + 128, "pl", 0, 2, slot_at(w)))
+        tt(R("ebs", 1, 193, 3), X("win%d" % s, slot_at(w) + 128, "ex%d" % x, 0, 4, slot_at(w) - 8), R("ce%d" % x, 64, 128), O.mult)
+
+    def finish_scan(s, x):
+        a = slot_at(x) + 32
+        scan(R("win%d" % s, a, a + 96), R("ebs", 0, 96), R("ebs", 97, 193), O.add, O.max)
+
+    def partial_base(x):
+        cp(R("dbs", 2, 98, 3), X("dbl%d" % (x % 4), 392, "bx%d" % x, 0, 2))
+
+    def partial(s, w):
+        x, win, i = w + 1, "win%d" % s, w // 2
+        tt(R("dbs", 1, 193, 3), X(win, own_at(w) + 200, "px%d" % x, 0, 4), R("sp%d" % x, 64, 128), O.mult)
+        scan(R(win, 8, 104), R("dbs", 0, 96), R("dbs", 97, 193), O.add, O.max)
+        cp(R("sb%d_%d" % (s, w), 0, 96), X(win, own_at(w) + 200, "l96", 6 * i, 6 * i + 6))
+        send(s, w)
+
+    def base(w, src):
+        x = X("qsb", C, "seq16", 4 * w, 4 * w + 4) if src == "qsb" else X("src", 512, "seqp", 4 * w, 4 * w + 4)
+        tt(R("dbl%d" % (w % 4), 2, 194, 3), x, R("rmp", F * w, F * w + F), O.mult)
+
+    def twice_at(w):
+        return 128 * (w - 2) + 512 if 2 <= w < 6 else 128 * (w == 6) * 8
+
+    def twice(w):
+        for u in range(U):
+            act(R("ps", twice_at(w) + 64 * u, twice_at(w) + 64 * u + F), R("rmp", F * w, F * w + F))
+
+    def coef(w):
+        tt(R("cr", CR * w, CR * w + 128), R("cob", 128 * w, 128 * w + 128), R("ps", twice_at(w), twice_at(w) + 128), O.mult)
+
+    def to_cells(s, w):
+        cp(X("psic%d" % s, 512, "seqp", 4 * w, 4 * w + 4), own(s, w))
+
+    def flux(s, j, start, stop):
+        mm(R("pf", 512 * j, 512 * j + 32, 1, CELLS[j]), R("psic%d" % s, 128 * j, 128 * j + CELLS[j]), R("mskw", 0, 32), start, stop)
+
+    def spread(x):
+        act(R("upf%d" % x, 0, 128), X("tab", Z + 8, "upr16", 8 * x, 8 * x + 8))
+
+    def picks(x):
+        for u in range(U):
+            ts(R("ix%d" % x, 2 * u, 2 * u + 2), R("s2", 2 * x, 2 * x + 2), float(64 * u - 64 * x), O.add, 128.0, O.min)
+        ts(R("bx%d" % x, 0, 2), R("s3", 2 * x, 2 * x + 2), float(2 - 192 * x), O.add, 195.0, O.min)
+
+    def cells_sent(x):
+        act(R("sp%d" % x, 0, 64), X("upf%d" % x, CR, "ix%d" % x, 0, 4))
+        act(R("sp%d" % x, 64, 128), X("cr", CR * x + CR, "ix%d" % x, 0, 4, CR * x))
+
+    def fold(src, out, limit, op, t):
+        tt(R("fo" + t, 0, 64), R(src, 0, 64), R("mskw", 0, 64), O.mult)
+        scan(R("cum" + t, 16, 80), R("fo" + t, 0, 64), R("fo" + t, 0, 64), O.add, O.max)
+        tt(R("r4" + t, 0, 4), R("cum" + t, 31, 80, 16), R("cum" + t, 15, 64, 16), O.subtract)
+        ts(R(out, 0, 4), R("r4" + t, 0, 4), *([limit, O.min] if op == "min" else [limit, O.max, -limit, O.add]))
+
+    def pack(x):
+        together(True)
+        for c in others:
+            k, i = T.rank_of(c), index_of(T.rank_of(c))
+            for j in range(4):
+                act(R("pk%d" % x, 32 * i + 8 * j, 32 * i + 8 * j + 8), R("sp%d" % x, 32 * j + 8 * k, 32 * j + 8 * k + 8))
+        together(False)
+        message("pk%d" % x, NS, lambda k: NS * index_of(k), "lp%d" % x, lambda k: NS * rank, "pre%d" % x)
+
+    def unpack(x):
+        landing("lp%d" % x, NS, lambda k: NS * k, "pre%d" % x)
+        together(True)
+        for c in others:
+            k = T.rank_of(c)
+            for j in range(4):
+                act(R("ce%d" % x, 32 * j + 8 * k, 32 * j + 8 * k + 8), R("lp%d" % x, 32 * k + 8 * j, 32 * k + 8 * j + 8))
+        together(False)
+
+    def known(x):
+        fold("sp%d" % x, "px%d" % x, float(slot_at(x - 1) - 1), "min", "")
+
+    def unknown(x):
+        fold("ce%d" % x, "ex%d" % x, float(slot_at(x - 1) - 8), "max", "2")
+
+    load("y", "seq32", T.seq)
+    load("s", "snd32", T.snd)
+    load("s", "rmb", T.rm)
+    load("y", "qsb", T.qs)
+    load("y", "up32", T.up)
+    load("s", "cob", T.co)
+    load("y", "scb", T.sc, 16)
+    iota(R("pi", 0, 4), [[0, 4]], 0, 1, False)
+    iota(R("iot", 0, 128), [[1, 128]], 1024, -1, False)
+    iota(R("tab", 0, 64), [[3, 64]], own_at(0) + 2, 0, True)
+    iota(R("tab", C, C + 32), [[32, 4], [1, 8]], slot_at(0) + 8 * rank, 0, True)
+    iota(R("tab", C + 32, C + 64), [[3, 32]], slot_at(1) + 34, 0, True)
+    fill(R("zer", 0, 304), 0.0)
+    fill(R("neg", 0, 200), -BIG)
+    together(True)
+    zeros("win0", 0, own_at(0) + 200)
+    for s in range(NR):
+        a = slot_at(0) + NS * s
+        if s == rank:
+            zeros("win0", a, a + NS)
+        else:
+            if rank > 0:
+                zeros("win0", a, a + 8 * rank)
+            if rank < NR - 1:
+                zeros("win0", a + 8 * rank + 8, a + NS)
+    together(False)
+    together(True)
+    zeros("sb0_1", 0, 96)
+    zeros("win0", slot_at(1) - 8, slot_at(1) + 32)
+    zeros("win0", slot_at(1) + 32 + 24 * rank, slot_at(1) + 56 + 24 * rank)
+    for i in (1, 2):
+        negs("dbl%d" % i, 0, 192, 3)
+        negs("dbl%d" % i, 194, 386, 3)
+        zeros("dbl%d" % i, 195, 387, 3)
+    together(False)
+    ts(R("p7", 0, 4), R("pi", 0, 4), 7, O.bitwise_and)
+    ts(R("p8", 0, 4), R("pi", 0, 4), 8, O.bitwise_and)
+    ts(R("iam", 0, 128), R("iot", 0, 128), 15, O.bitwise_and)
+    fill(R("k18", 0, 18), 0.0)
+    ts(R("mskw", 0, 128), R("iam", 0, 128), 0.0, O.is_equal)
+
+    cp(R("seq16", 0, 28), R("seq32", 0, 28))
+    ts(R("s5", 0, 12), R("snd32", 0, 12), float(Z), O.is_ge, -8192.0, O.mult)
+    ts(R("s6", 0, 12), R("snd32", 0, 12), 3.0, O.mult)
+    cp(R("rmp", 0, F), X("rmb", C, "seq16", 0, 4))
+    tt(R("s7", 0, 12), R("s6", 0, 12), R("s5", 0, 12), O.add)
+    tt(R("z0", 0, F), X("qsb", C, "seq16", 0, 4), R("rmp", 0, F), O.mult)
+    ts(R("l0", 0, 2), R("s7", 0, 2), float(own_at(0) + 2), O.add, 0.0, O.max)
+    ts(own(0, 0), R("z0", 0, F), 0.0, O.max)
+    cp(R("sb0_0", 0, NS), X("win0", own_at(0) + 200, "l0", 0, 2))
+    send(0, 0)
+    act(R("rmp", F, C), X("rmb", C, "seq16", 4, 28))
+    together(True)
+    twice(1)
+    together(False)
+    together(True)
+    for w in range(2, W):
+        twice(w)
+    together(False)
+    u, fu = R("up32", 8, 56), (lambda n: R(n, 0, 48))
+    shift = OFF - 266.0
+    ts(fu("uH"), u, 0x3C0, O.bitwise_and)
+    ts(fu("uL"), u, 0x3F, O.bitwise_and)
+    ts(fu("ut"), u, 7, O.bitwise_and)
+    ts(fu("ud"), u, float(C), O.is_ge, -8192.0, O.mult)
+    ts(fu("un"), u, float(Z), O.is_ge, -8192.0, O.mult)
+    ts(fu("ua"), fu("uH"), 5.125, O.mult, float(own_at(0) + 2), O.add)
+    ts(fu("ub"), fu("uL"), 3.0, O.mult)
+    ts(fu("ue"), fu("uH"), 10.25, O.mult, float(slot_at(0)) - 10.25 * C - shift, O.add)
+    ts(fu("uf"), fu("uL"), 4.0, O.mult, 8.0 * rank + shift, O.add)
+    ts(fu("ug"), fu("ut"), 3.0, O.mult)
+    ts(fu("ui"), fu("uL"), 32.0, O.is_ge, OFF, O.mult)
+    tt(fu("uc"), fu("ua"), fu("ub"), O.add)
+    tt(fu("uh"), fu("uf"), fu("ug"), O.subtract)
+    tt(fu("uj"), fu("ub"), fu("ui"), O.add)
+    tt(fu("uo"), fu("ue"), fu("un"), O.add)
+    tt(fu("um"), fu("uc"), fu("ud"), O.add)
+    tt(fu("uk"), fu("uh"), fu("uj"), O.max)
+    base(1, "qsb")
+    tt(fu("ue"), fu("uo"), fu("uk"), O.add)
+    coef(1)
+    tt(fu("ua"), fu("um"), fu("ue"), O.max)
+    ts(R("l1", 0, 2), R("s7", 2, 4), float(own_at(1) + 2 - 192), O.add, 0.0, O.max)
+    cp(R("up16", 8, 56), fu("ua"))
+    ts(R("s1", 0, 12), R("snd32", 0, 12), float(Z), O.is_ge, 1024.0, O.mult)
+    cp(R("upr16", 0, 56), R("up32", 0, 56))
+    tt(R("s2", 0, 12), R("snd32", 0, 12), R("s1", 0, 12), O.add)
+    ts(R("s3", 0, 12), R("s2", 0, 12), 3.0, O.mult)
+    picks(3)
+    together(True)
+    for i in range(3):
+        for j in range(3):
+            a = 6 * i + 2 * j
+            relu(R("l96f", a, a + 2), R("s7", 4 * i, 4 * i + 2), float(own_at(2 * i) + 2 - 384 * i))
+    together(False)
+    together(True)
+    for i in range(1, W):
+        act(R("tab", 64 * i, 64 * i + 64), R("tab", 0, 64), float(BW * i))
+    for i in range(2, W - 1):
+        a, b = C + 32 * i, C + 32 * (i % 2)
+        act(R("tab", a, a + 32), R("tab", b, b + 32), float(BW * (i - i % 2)))
+    zeros("tab", Z, Z + 8)
+    zeros("upf3", 128, CR)
+    zeros("cr", CR * 3 + 128, CR * 4)
+    together(False)
+    together(True)
+    negs("dbl3", 0, 192, 3)
+    negs("dbl3", 194, 386, 3)
+    zeros("dbl3", 195, 387, 3)
+    negs("dbs", 0, 200)
+    zeros("cum", 0, 16)
+    together(False)
+    arrival(0, 0)
+
+    chain_gather(0, 1)
+    chain_scan(0, 1)
+    cp(R("sb0_1", 2, 96, 3), X("win0", own_at(1) + 200, "l1", 0, 2))
+    send(0, 1)
+    coef(3)
+    spread(3)
+    cells_sent(3)
+    pack(3)
+    base(2, "qsb")
+    together(True)
+    negs("dbl0", 0, 192, 3)
+    negs("dbl0", 194, 386, 3)
+    zeros("dbl0", 195, 387, 3)
+    for i in range(2, W - 1):
+        zeros("win0", slot_at(i) - 8, slot_at(i) + (32 if i % 2 else 0))
+    for x in PAIRS:
+        zeros("ce%d" % x, 0, 128)
+    negs("ebs", 0, 97)
+    negs("ebs", 98, 194, 3)
+    zeros("ebs", 99, 195, 3)
+    zeros("cum2", 0, 16)
+    for x in (5, 1):
+        zeros("upf%d" % x, 128, CR)
+        zeros("cr", CR * x + 128, CR * (x + 1))
+    zeros("src", 352, 512)
+    together(False)
+    coef(2)
+    base(3, "qsb")
+    ts(R("ph", 0, 3), R("p8", 0, 3), float(8 * (rank % 2)), O.is_equal)
+    ts(R("pv", 0, 3), R("p7", 0, 3), 3.0, O.mult)
+    ts(R("pa", 0, 2), R("p8", 0, 2), 5.0, O.mult)
+    partial_base(3)
+    for c in others:
+        k, i = T.rank_of(c), index_of(T.rank_of(c))
+        a = 2 * i + rank // 2
+        o, v, h = R("k18", a, a + 13, 6), R("pv", 0, 3), R("ph", 0, 1)
+        add_op("v", lambda o=o, v=v, h=h, k=k: g.vector.tensor_scalar(out=o[0], in0=v[0], scalar1=float(24 * k + 10), scalar2=h[0],
+                                                                      op0=O.add, op1=O.mult), [v[1], h[1]], [o[1]])
+    known(3)
+    tt(R("l96g", 0, 18), R("l96f", 0, 18), R("k18", 0, 18), O.add)
+    tt(R("pb", 0, 2), R("pa", 0, 2), R("p7", 0, 2), O.add)
+    cp(R("l96", 0, 18), R("l96g", 0, 18))
+    ts(R("qa", 0, 28), R("seq32", 0, 28), 0x1F, O.bitwise_and)
+    ts(R("qb", 0, 28), R("seq32", 0, 28), 0x60, O.bitwise_and)
+    ts(R("qc", 0, 28), R("seq32", 0, 28), 0x180, O.bitwise_and)
+    arrival(0, 1)
+
+    chain_gather(0, 2)
+    chain_scan(0, 2)
+    partial(0, 2)
+    spread(5)
+    unpack(3)
+    picks(5)
+    coef(5)
+    cells_sent(5)
+    pack(5)
+    ts(R("pl", 0, 1), R("pb", 0, 1), 0.0, O.add)
+    ts(R("pl", 1, 2), R("pb", 1, 2), 80.0, O.add)
+    base(4, "qsb")
+    coef(4)
+    base(5, "qsb")
+    unknown(3)
+    partial_base(5)
+    known(5)
+    arrival(0, 2)
+
+    finish_gather(0, 3)
+    chain_gather(0, 3)
+    finish_scan(0, 3)
+    chain_scan(0, 3)
+    chain_gather(0, 4)
+    chain_scan(0, 4)
+    partial(0, 4)
+    unpack(5)
+    spread(1)
+    picks(1)
+    cells_sent(1)
+    pack(1)
+    ts(R("qd", 0, 28), R("qb", 0, 28), 4.0, O.mult)
+    ts(R("qe", 0, 28), R("qc", 0, 28), 0.25, O.mult)
+    base(6, "qsb")
+    tt(R("qf", 0, 28), R("qd", 0, 28), R("qa", 0, 28), O.add)
+    coef(6)
+    tt(R("qg", 0, 28), R("qf", 0, 28), R("qe", 0, 28), O.add)
+    unknown(5)
+    cp(R("seqp", 0, 28), R("qg", 0, 28))
+    for x in range(3):
+        to_cells(0, x)
+    zeros("win1", 0, own_at(0) + 200)
+    arrival(0, 4)
+
+    finish_gather(0, 5)
+    chain_gather(0, 5)
+    finish_scan(0, 5)
+    chain_scan(0, 5)
+    chain_gather(0, 6)
+    cp(R("scf", 0, 16, 1, 16), R("scb", 0, 16, 1, 16))
+    mm(R("pf", 0, 16), R("mskw", 0, 128, 1, 16), R("scf", 0, 16, 1, 16))
+    together(True)
+    for i in range(8):
+        act(R("screp", 16 * i, 16 * i + 16), R("pf", 0, 16))
+    together(False)
+    chain_scan(0, 6)
+    for x in (3, 4, 5, 6):
+        to_cells(0, x)
+
+    for i in range(4):
+        mm(R("ps", 512 * i, 512 * i + CELLS[i]), R("screp", 0, 128), R("psic0", 128 * i, 128 * i + CELLS[i]))
+    known(1)
+    for i in range(4):
+        o, a = R("src", 128 * i, 128 * i + CELLS[i]), R("ps", 512 * i, 512 * i + CELLS[i])
+        if i % 2 == 0:
+            act(o, a)
+        else:
+            cp(o, a)
+    tt(R("z0", 0, F), X("src", 512, "seqp", 0, 4), R("rmp", 0, F), O.mult)
+    base(1, "src")
+    ts(own(1, 0), R("z0", 0, F), 0.0, O.max)
+    partial_base(1)
+    partial(1, 0)
+    unpack(1)
+    together(True)
+    for i in range(1, W - 1):
+        zeros("win1", slot_at(i) - 8, slot_at(i) + (32 if i % 2 else 0))
+    together(False)
+    for j in range(4):
+        flux(0, j, True, False)
+    base(2, "src")
+    base(3, "src")
+    to_cells(1, 0)
+    partial_base(3)
+    unknown(1)
+    arrival(1, 0)
+
+    for x in (1, 3, 5):
+        finish_gather(1, x)
+        chain_gather(1, x)
+        finish_scan(1, x)
+        chain_scan(1, x)
+        chain_gather(1, x + 1)
+        chain_scan(1, x + 1)
+        if x < 5:
+            partial(1, x + 1)
+            base(x + 3, "src")
+            if x == 1:
+                base(5, "src")
+                partial_base(5)
+            to_cells(1, x)
+            to_cells(1, x + 1)
+            arrival(1, x + 1)
+        else:
+            to_cells(1, 5)
+            to_cells(1, 6)
+
+    for j in range(4):
+        flux(1, j, False, True)
+    for j in range(4):
+        turn(R("yo", 32 * j, 32 * j + 32, 1, CELLS[j]), R("pf", 512 * j, 512 * j + 32, 1, CELLS[j]))
+    for k in range(4):
+        a, b = 128 * k, min(C, 128 * k + 128)
+        q = "y" if k % 2 == 1 else "s"
+        add_op(q, lambda q=q, a=a, b=b, k=k: queues[q].dma_start(T.y[:, a:b], T.yo[32 * k:32 * k + 16, 0:b - a]),
+               [[("yo", 0, b - a, 1)]], [[("y", a, b, 1)]], "dma", 16)
+
+    emit(g, T, queues, ops)
+
+
+def meets(x, y, same):
+    if x[0] in PSUM and x[0] == y[0] and not same:
+        return x[1] // 512 <= (y[2] - 1) // 512 and y[1] // 512 <= (x[2] - 1) // 512
+    if x[0] != y[0] or x[1] >= y[2] or y[1] >= x[2]:
+        return False
+    return x[3] != y[3] or x[3] == 1 or (x[1] - y[1]) % x[3] == 0
+
+
+def clash(a, b):
+    for x in a["w"]:
+        for y in b["r"] + b["w"]:
+            if meets(x, y, a["q"] == b["q"]):
+                return True
+    for x in a["r"]:
+        for y in b["w"] + (b["r"] if x[0] in PSUM and a["q"] != b["q"] else []):
+            if meets(x, y, a["q"] == b["q"]):
+                return True
+    return False
+
+
+def plan_waits(ops, flagged, members):
+    known, issued, start, waits, new = {}, {}, {}, [], set(flagged)
+    for i, o in enumerate(ops):
+        ws = []
+        q = o["q"]
+        if o["kind"] == "ext":
+            start[i] = 0
+            waits.append(ws)
+            continue
+        k = known.get(q, 0)
+        mine = issued.setdefault(q, [[] for r in range(KQ.get(q, 1))])
+        for j in range(i - 1, -1, -1):
+            if k >> j & 1 or not clash(o, ops[j]):
+                continue
+            p = ops[j]
+            if p["kind"] == "remote":
+                raise ValueError("a call waits for a message's source")
+            if p["q"] == q and p["kind"] == "c" and j not in flagged:
+                r = [n for n in range(len(mine)) if j in mine[n]][0]
+                ws.append(("q", (r, len(mine[r]))))
+                for m in mine[r]:
+                    k |= 1 << m | start[m]
+            else:
+                all_of = members.get(p["grp"], [j])
+                if all_of[-1] >= i:
+                    raise ValueError("a call waits for a group that isn't whole yet")
+                ws.append(("u", all_of[0]))
+                for m in all_of:
+                    k |= 1 << m | start[m]
+                if p["kind"] == "c":
+                    new.update(all_of)
+        start[i] = k
+        known[q] = k
+        if o["kind"] == "c" and i not in flagged:
+            mine[sum(len(m) for m in mine) % len(mine)].append(i)
+        waits.append(ws)
+    return waits, new
+
+
+def emit(g, T, queues, ops):
+    flagged, members, names = set(), {}, {}
+    for i, o in enumerate(ops):
+        if o["grp"] is not None and o["kind"] == "c":
+            members.setdefault(o["grp"], []).append(i)
+    while True:
+        waits, new = plan_waits(ops, flagged, members)
+        if new == flagged:
+            break
+        flagged = new
+    own, total = 0, {}
+    for i, o in enumerate(ops):
+        first = members.get(o["grp"], [i])[0]
+        if o["kind"] == "ext":
+            names[i], total[i] = o["sem"], o["n"]
+        elif first in names:
+            names[i] = names[first]
+        elif o["kind"] == "dma" or i in flagged:
+            names[i], total[i] = "x%d" % own, o["n"] * len(members.get(o["grp"], [i]))
+            own += 1
+    count, done, sent, waited = {}, {}, 0, set()
+    for i, o in enumerate(ops):
+        if o["kind"] == "ext":
+            continue
+        q = o["q"]
+        for kind, v in waits[i]:
+            if kind == "q":
+                queues[q].wait_ge(T.sem["q_%s%d" % (q, v[0])], v[1])
+                done[(q, v[0])] = v[1]
+            else:
+                queues[q].wait_ge(T.sem[names[v]], total[v])
+                waited.add(v)
+        x = o["fn"]()
+        if o["kind"] == "remote":
+            sent += o["n"]
+        elif i in names:
+            x.then_inc(T.sem[names[i]], o["n"])
+        else:
+            r = sum(count.get((q, n), 0) for n in range(KQ[q])) % KQ[q]
+            x.then_inc(T.sem["q_%s%d" % (q, r)], 1)
+            count[(q, r)] = count.get((q, r), 0) + 1
+    for q, r in count:
+        if done.get((q, r), 0) < count[(q, r)]:
+            queues[q].wait_ge(T.sem["q_%s%d" % (q, r)], count[(q, r)])
+    g.wait_ge(T.sem["sent"], sent)
+    for i in total:
+        if i not in waited:
+            queues[ops[i]["q"]].wait_ge(T.sem[names[i]], total[i])

@@ -5,18 +5,20 @@ W, F, U, CAP, SW, NR = 7, 64, 2, 8, 2, 4
 C = W * F
 Z = C + (W - 1) * NR * CAP
 NS = NR * CAP
-BW = 328
-HD = 104
+MW = 48
+BW = 392
+HD = 72
 WIN = HD + BW * (W - 1) + 192
-CR = 136
+LW = 80
+LP = NR * LW
+BASE = (LP + 192, 0)
+DB = 384
 BIG = 9.0e29
 OFF = 4096.0
 CELLS = (128, 128, 96, 96)
-KQ = {"v": 8, "s": 8, "t": 2, "g": 2}
-NXS = 108
-FULL = {(0, 2), (0, 4), (1, 0), (1, 2), (1, 4)}
-PLAIN = {(0, 0): CAP, (0, 1): 3 * CAP}
-PAIRS = (3, 5, 1)
+KQ = {"v": 14, "s": 8, "t": 2, "g": 2}
+NXS = 112
+SENDS = [(s, w) for s in range(SW) for w in (0, 2, 4)]
 
 
 def own_at(w):
@@ -24,56 +26,45 @@ def own_at(w):
 
 
 def slot_at(w):
-    return HD + BW * w + 200
+    return HD + BW * w + 192
+
+
+def f32(n):
+    return ("sbuf", [128, n], "float32")
+
+
+def i32(n):
+    return ("sbuf", [128, n], "int32")
+
+
+def u16(n):
+    return ("sbuf", [128, n], "uint16")
 
 
 SCRATCH = {
-    "seq32": ("sbuf", [128, 28], "int32"), "up32": ("sbuf", [128, 56], "int32"), "snd32": ("sbuf", [128, 12], "int32"),
+    "seq32": i32(28), "up32": i32(56), "snd32": i32(12),
     "qsb": ("sbuf", [128, C], "bfloat16"), "rmb": ("sbuf", [128, C], "bfloat16"), "cob": ("sbuf", [128, 2 * C], "bfloat16"),
-    "scb": ("sbuf", [128, 16], "bfloat16"), "scf": ("sbuf", [128, 16], "float32"),
-    "seq16": ("sbuf", [128, 28], "uint16"), "up16": ("sbuf", [128, 56], "uint16"), "upr16": ("sbuf", [128, 56], "uint16"),
-    "rmp": ("sbuf", [128, C], "float32"), "cr": ("sbuf", [128, CR * W], "float32"), "z0": ("sbuf", [128, F], "float32"),
-    "win0": ("sbuf", [128, WIN], "float32"), "win1": ("sbuf", [128, WIN], "float32"),
-    "psic0": ("sbuf", [128, 512], "float32"), "psic1": ("sbuf", [128, 512], "float32"), "src": ("sbuf", [128, 512], "float32"),
-    "dbs": ("sbuf", [128, 200], "float32"), "ebs": ("sbuf", [128, 200], "float32"),
-    "tab": ("sbuf", [128, Z + 8], "float32"), "zer": ("sbuf", [128, 304], "float32"), "neg": ("sbuf", [128, 200], "float32"),
-    "iot": ("sbuf", [128, 128], "int32"), "iam": ("sbuf", [128, 128], "int32"), "mskw": ("sbuf", [128, 128], "float32"),
-    "pi": ("sbuf", [128, 4], "int32"), "p7": ("sbuf", [128, 4], "int32"), "p8": ("sbuf", [128, 4], "int32"),
-    "ph": ("sbuf", [128, 4], "float32"), "pv": ("sbuf", [128, 4], "float32"), "k18": ("sbuf", [128, 18], "float32"),
-    "pa": ("sbuf", [128, 2], "float32"), "pb": ("sbuf", [128, 2], "float32"), "pl": ("sbuf", [128, 2], "uint16"),
-    "uH": ("sbuf", [128, 48], "int32"), "uL": ("sbuf", [128, 48], "int32"), "ut": ("sbuf", [128, 48], "int32"),
-    "s1": ("sbuf", [128, 12], "float32"), "s2": ("sbuf", [128, 12], "float32"), "s3": ("sbuf", [128, 12], "float32"),
-    "s5": ("sbuf", [128, 12], "float32"), "s6": ("sbuf", [128, 12], "float32"), "s7": ("sbuf", [128, 12], "float32"),
-    "l0": ("sbuf", [128, 2], "uint16"), "l1": ("sbuf", [128, 2], "uint16"),
-    "l96f": ("sbuf", [128, 18], "float32"), "l96g": ("sbuf", [128, 18], "float32"), "l96": ("sbuf", [128, 18], "uint16"),
-    "fo": ("sbuf", [128, 64], "float32"), "cum": ("sbuf", [128, 80], "float32"), "r4": ("sbuf", [128, 4], "float32"),
-    "fo2": ("sbuf", [128, 64], "float32"), "cum2": ("sbuf", [128, 80], "float32"), "r42": ("sbuf", [128, 4], "float32"),
-    "screp": ("sbuf", [128, 128], "float32"), "yo": ("sbuf", [128, 128], "float32"),
-    "qa": ("sbuf", [128, 28], "int32"), "qb": ("sbuf", [128, 28], "int32"), "qc": ("sbuf", [128, 28], "int32"),
-    "qd": ("sbuf", [128, 28], "float32"), "qe": ("sbuf", [128, 28], "float32"), "qf": ("sbuf", [128, 28], "float32"),
-    "qg": ("sbuf", [128, 28], "float32"), "seqp": ("sbuf", [128, 28], "uint16"),
+    "scb": ("sbuf", [128, 16], "bfloat16"), "scf": f32(16),
+    "seq16": u16(28), "up16": u16(56), "upr16": u16(56), "seqp": u16(28),
+    "rmp": f32(C), "cro": f32(392), "cre": f32(384), "z0": f32(F), "win0": f32(BASE[0] + WIN), "win1": f32(WIN),
+    "psic0": f32(512), "psic1": f32(512), "src": f32(512), "dbo": f32(3 * DB), "dbe": f32(DB), "ebs": f32(200),
+    "tab": f32(Z + 8), "zer": f32(192), "iot": i32(192), "iam": i32(192), "mskw": f32(192), "upf": f32(392),
+    "pi": i32(2), "p16i": i32(2), "p16": f32(2), "m8": f32(2), "c16": f32(12), "p4": f32(4), "col": f32(16), "kc": f32(4),
+    "lim": i32(12), "limw": i32(48), "kw": i32(12), "cei": i32(12),
+    "uH": i32(48), "uL": i32(48), "ut": i32(48),
+    "s5": f32(12), "s6": f32(12), "s7": f32(12), "s8": f32(12), "s9": f32(12), "l16f": f32(30), "l0": u16(2), "l16": u16(30), "ix": u16(12), "bx": u16(6),
+    "fo": f32(192), "cum": f32(208), "c12": f32(12), "t1": f32(12), "hx": f32(12), "em": f32(12), "a1": f32(4), "a2": f32(4),
+    "pkf": f32(16), "pk16": u16(16), "pk": f32(3 * LW), "ex": u16(16), "cel": u16(12), "pl": u16(2), "pla": u16(2), "ce": f32(192),
+    "screp": f32(128), "yo": f32(128),
+    "qa": i32(28), "qb": i32(28), "qc": i32(28), "qd": f32(28), "qe": f32(28), "qf": f32(28), "qg": f32(28),
     "ps": ("psum", [128, 2048], "float32"), "pf": ("psum", [128, 2048], "float32"),
 }
-for _n in ("ua", "ub", "uc", "ud", "ue", "uf", "ug", "uh", "ui", "uj", "uk", "um", "un", "uo"):
-    SCRATCH[_n] = ("sbuf", [128, 48], "float32")
-for _i in range(4):
-    SCRATCH["dbl%d" % _i] = ("sbuf", [128, 392], "float32")
-for _k in FULL:
-    SCRATCH["sb%d_%d" % _k] = ("sbuf", [128, 96], "float32")
-for _k in PLAIN:
-    SCRATCH["sb%d_%d" % _k] = ("sbuf", [128, 4 * PLAIN[_k]], "float32")
-for _x in PAIRS:
-    SCRATCH["upf%d" % _x] = ("sbuf", [128, CR], "float32")
-    SCRATCH["ix%d" % _x] = ("sbuf", [128, 4], "uint16")
-    SCRATCH["bx%d" % _x] = ("sbuf", [128, 2], "uint16")
-    SCRATCH["px%d" % _x] = ("sbuf", [128, 4], "uint16")
-    SCRATCH["ex%d" % _x] = ("sbuf", [128, 4], "uint16")
-    SCRATCH["sp%d" % _x] = ("sbuf", [128, 128], "float32")
-    SCRATCH["pk%d" % _x] = ("sbuf", [128, 96], "float32")
-    SCRATCH["lp%d" % _x] = ("sbuf", [128, 128], "float32")
-    SCRATCH["ce%d" % _x] = ("sbuf", [128, 128], "float32")
-SEMAPHORES = (["x%d" % i for i in range(NXS)] + ["arr%d_%d" % k for k in sorted(FULL | set(PLAIN))]
-              + ["pre%d" % x for x in PAIRS] + ["q_%s%d" % (q, i) for q in KQ for i in range(KQ[q])] + ["sent"])
+for _n in ("ua", "ub", "uc", "ud", "ue", "uf", "ug", "uh", "ui", "uj", "uk", "um", "un", "uo", "uq"):
+    SCRATCH[_n] = f32(48)
+for _k in SENDS:
+    SCRATCH["sb%d_%d" % _k] = f32(3 * MW)
+SEMAPHORES = (["x%d" % i for i in range(NXS)] + ["arr%d_%d" % k for k in SENDS] + ["pre"]
+              + ["q_%s%d" % (q, i) for q in KQ for i in range(KQ[q])] + ["sent"])
 PSUM = ("ps", "pf")
 
 
@@ -103,6 +94,9 @@ def rank_program(g, core, T, topo):
         return
     cores = list(T.cores)
     others = [c for c in cores if c != core]
+    calls = send_calls(topo, core, others)
+    order = [T.rank_of(d) for call in calls for d, e in call]
+    rising = sorted(order)
     queues = {"v": g.vector, "s": g.scalar, "t": g.tensor, "g": g, "y": g.sync}
     ops, group, groups = [], [None], [0]
 
@@ -118,8 +112,14 @@ def rank_program(g, core, T, topo):
         ap = t[0:p, a:b] if step == 1 else t[0:p, a:b:step]
         return (ap, [reg(name, a, b, step)])
 
+    def N(name, a, n, step=1):
+        return R(name, a, a + step * (n - 1) + 1, step if n > 1 else 1)
+
     def X(name, b, off, oa, ob, a=0):
         return (T[name][:, a:b].indirect(T[off][:, oa:ob]), [reg(name, a, b), reg(off, oa, ob)])
+
+    def K(x):
+        return x if isinstance(x, tuple) else (x, [])
 
     def add_op(q, fn, reads, writes, kind="c", n=1, sem=None):
         rd, wr = [], []
@@ -137,10 +137,12 @@ def rank_program(g, core, T, topo):
         add_op("v", lambda: g.vector.tensor_tensor(out=out[0], in0=a[0], in1=b[0], op=op), [a[1], b[1]] + r, w)
 
     def ts(out, a, s1, op0, s2=None, op1=None):
+        k1, k2 = K(s1), K(s2)
         if op1 is None:
-            add_op("v", lambda: g.vector.tensor_scalar(out=out[0], in0=a[0], scalar1=s1, scalar2=None, op0=op0), [a[1]], [out[1]])
+            add_op("v", lambda: g.vector.tensor_scalar(out=out[0], in0=a[0], scalar1=k1[0], scalar2=None, op0=op0), [a[1], k1[1]], [out[1]])
         else:
-            add_op("v", lambda: g.vector.tensor_scalar(out=out[0], in0=a[0], scalar1=s1, scalar2=s2, op0=op0, op1=op1), [a[1]], [out[1]])
+            add_op("v", lambda: g.vector.tensor_scalar(out=out[0], in0=a[0], scalar1=k1[0], scalar2=k2[0], op0=op0, op1=op1),
+                   [a[1], k1[1], k2[1]], [out[1]])
 
     def cp(out, a):
         w, r = split(out)
@@ -149,21 +151,16 @@ def rank_program(g, core, T, topo):
     def fill(out, v):
         add_op("v", lambda: g.vector.memset(out[0], v), [], [out[1]])
 
-    def scan(out, d0, d1, op0, op1):
-        add_op("v", lambda: g.vector.tensor_tensor_scan(out=out[0], data0=d0[0], data1=d1[0], initial=0.0, op0=op0, op1=op1),
+    def scan(out, d0, d1, first=0.0):
+        add_op("v", lambda: g.vector.tensor_tensor_scan(out=out[0], data0=d0[0], data1=d1[0], initial=first, op0=O.add, op1=O.max),
                [d0[1], d1[1]], [out[1]])
 
-    def act(out, a, bias=0.0):
-        add_op("s", lambda: g.scalar.activation(out=out[0], in_=a[0], func=AF.Identity, bias=bias), [a[1]], [out[1]])
+    def act(out, a, bias=0.0, scale=1.0, func=AF.Identity):
+        kb = K(bias)
+        add_op("s", lambda: g.scalar.activation(out=out[0], in_=a[0], func=func, bias=kb[0], scale=scale), [a[1], kb[1]], [out[1]])
 
-    def relu(out, a, bias):
-        add_op("s", lambda: g.scalar.activation(out=out[0], in_=a[0], func=AF.Relu, bias=bias), [a[1]], [out[1]])
-
-    def zeros(name, a, b, step=1):
-        act(R(name, a, b, step), R("zer", 0, len(range(a, b, step))))
-
-    def negs(name, a, b, step=1):
-        act(R(name, a, b, step), R("neg", 0, len(range(a, b, step))))
+    def const(name, a, n, step=1, v=0.0):
+        act(N(name, a, n, step), R("zer", 0, n), v)
 
     def mm(out, lhsT, rhs, start=True, stop=True):
         add_op("t", lambda: g.tensor.matmul(out=out[0], lhsT=lhsT[0], rhs=rhs[0], start=start, stop=stop), [lhsT[1], rhs[1]], [out[1]])
@@ -176,100 +173,115 @@ def rank_program(g, core, T, topo):
         o = R(name, 0, n, 1, p)
         add_op(q, lambda: queues[q].dma_start(o[0], src[:, :]), [], [o[1]], "dma", 16)
 
-    def iota(out, pattern, base, cm, flag):
-        if flag:
+    def iota(out, pattern, base, cm=0):
+        if SCRATCH[out[1][0][0]][2] == "float32":
             add_op("g", lambda: g.iota(out[0], pattern, base, cm, allow_small_or_imprecise_dtypes=True), [], [out[1]])
         else:
             add_op("g", lambda: g.iota(out[0], pattern, base, cm), [], [out[1]])
+
+    def runs():
+        out = []
+        for j, d in enumerate(rising):
+            if out and out[-1][1] + out[-1][2] == d:
+                out[-1][2] += 1
+            else:
+                out.append([j, d, 1])
+        return out
 
     def message(sb, width, src_at, dst, dst_at, sem):
         def one(call):
             tr = []
             for d, e in call:
                 rid, pid = topo.addr(d)[:2]
-                k = T.rank_of(d)
-                sa, da, m = src_at(k), dst_at(k), sum(1 << x for x in e)
+                sa, m = src_at(T.rank_of(d)), sum(1 << x for x in e)
                 if len(call) == 1:
-                    return g.remote_dma(out_ap=T[dst][:, da:da + width], in_ap=T[sb][:, sa:sa + width], remote_sem=T.sem[sem],
+                    return g.remote_dma(out_ap=T[dst][:, dst_at:dst_at + width], in_ap=T[sb][:, sa:sa + width], remote_sem=T.sem[sem],
                                         local_sem=T.sem["sent"], pid=pid, routing_id=rid, dma_engine_mask=m)
                 tr.append(RemoteDMATransfer(dst_ids=[DstId(rid=rid, pnc=pid)], dma_engine_mask=m, remote_sem=T.sem[sem],
-                                            src=T[sb][:, sa:sa + width], dst=T[dst][:, da:da + width]))
+                                            src=T[sb][:, sa:sa + width], dst=T[dst][:, dst_at:dst_at + width]))
             return g.remote_dma_fused(tr, local_sem=T.sem["sent"])
 
-        n = SCRATCH[sb][1][1]
-        for call in send_calls(topo, core, others):
-            add_op("g", lambda call=call: one(call), [[reg(sb, 0, n)]], [], "remote", sum(len(e) for d, e in call))
+        for call in calls:
+            add_op("g", lambda call=call: one(call), [[reg(sb, src_at(T.rank_of(d)), src_at(T.rank_of(d)) + width) for d, e in call]], [],
+                   "remote", sum(len(e) for d, e in call))
 
     def landing(dst, width, at, sem):
         n = sum(engines_to(topo, c, core, [d for d in cores if d != c]) for c in others)
-        add_op("ext", None, [], [[reg(dst, at(T.rank_of(c)), at(T.rank_of(c)) + width) for c in others]], "ext", n, sem)
+        add_op("ext", None, [], [[reg(dst, at(k), at(k) + width) for k in order]], "ext", n, sem)
 
-    def index_of(k):
-        return [T.rank_of(c) for c in others].index(k)
+    def win(s, a, b, step=1):
+        return R("win%d" % s, BASE[s] + a, BASE[s] + b, step)
 
-    def plain_at(w, s, d):
-        if w % 2 == 0:
-            return slot_at(w) + 32 * s + 8 * d
-        return slot_at(w) + 32 + 24 * s
+    def pick(s, a, b, off, oa, ob):
+        return X("win%d" % s, BASE[s] + b, off, oa, ob, BASE[s] + a)
+
+    def keep(s, w):
+        a = slot_at(w) + MW * rank
+        act(win(s, a, a + NS), R("sb%d_%d" % (s, w), 0, NS))
 
     def send(s, w):
-        sb, win, sem = "sb%d_%d" % (s, w), "win%d" % s, "arr%d_%d" % (s, w)
-        if (s, w) in FULL:
-            message(sb, NS, lambda k: NS * index_of(k), win, lambda k: slot_at(w) + NS * rank, sem)
-            act(R(win, slot_at(w) + NS * rank, slot_at(w) + NS * rank + NS), R(sb, 0, NS))
-        else:
-            c = PLAIN[(s, w)]
-            message(sb, c, lambda k: c * k, win, lambda k: plain_at(w, rank, k), sem)
+        sb, i = "sb%d_%d" % (s, w), w // 2
+        act(R(sb, 2 * MW, 3 * MW), pick(s, 0, slot_at(w), "l16", 10 * i + 6, 10 * i + 9))
+        cp(R(sb, 0, 2 * MW), pick(s, 0, slot_at(w), "l16", 10 * i, 10 * i + 6))
+        message(sb, MW, lambda k: MW * order.index(k), "win%d" % s, BASE[s] + slot_at(w) + MW * rank, "arr%d_%d" % (s, w))
+        keep(s, w)
 
-    def arrival(s, w):
-        win, sem = "win%d" % s, "arr%d_%d" % (s, w)
-        if (s, w) in FULL:
-            landing(win, NS, lambda k: slot_at(w) + NS * k, sem)
-        else:
-            landing(win, PLAIN[(s, w)], lambda k: plain_at(w, k, rank), sem)
+    def arrival(s, w, width=MW):
+        landing("win%d" % s, width, lambda k: BASE[s] + slot_at(w) + MW * k, "arr%d_%d" % (s, w))
 
     def own(s, w):
-        return R("win%d" % s, own_at(w) + 2, own_at(w) + 192, 3)
+        return win(s, own_at(w) + 2, own_at(w) + 192, 3)
+
+    def terms(w):
+        return ("dbo", DB * (w // 2)) if w % 2 else ("dbe", 0)
+
+    def coefs(w):
+        return R("cro", 128 * (w // 2), 128 * (w // 2) + 128) if w % 2 else R("cre", 64 * w - 128, 64 * w)
+
+    def term_constants(w):
+        d, a = terms(w)
+        const(d, a + 1, 64, 3, -BIG)
+        const(d, a + 2, 64, 3)
+        const(d, a + 194, 63, 3, -BIG)
 
     def chain_gather(s, w):
-        tt(R("dbl%d" % (w % 4), 1, 385, 3), X("win%d" % s, own_at(w), "up16", 8 * w, 8 * w + 8), R("cr", CR * w, CR * w + 128), O.mult)
+        d, a = terms(w)
+        tt(N(d, a, 128, 3), pick(s, 0, own_at(w), "up16", 8 * w, 8 * w + 8), coefs(w), O.mult)
 
     def chain_scan(s, w):
-        d = "dbl%d" % (w % 4)
-        scan(R("win%d" % s, own_at(w), own_at(w) + 192), R(d, 0, 192), R(d, 193, 385), O.add, O.max)
+        d, a = terms(w)
+        scan(win(s, own_at(w), own_at(w) + 192), N(d, a + 191, 192), N(d, a, 192), -BIG)
 
     def finish_gather(s, x):
-        w = x - 1
-        act(R("ebs", 2, 98, 3), X("win%d" % s, slot_at(w) + 128, "pl", 0, 2, slot_at(w)))
-        tt(R("ebs", 1, 193, 3), X("win%d" % s, slot_at(w) + 128, "ex%d" % x, 0, 4, slot_at(w) - 8), R("ce%d" % x, 64, 128), O.mult)
+        w, i = x - 1, x // 2
+        if (s, x) == (0, 1):
+            act(N("ebs", 4, NS, 6), X("win0", LP, "pla", 0, 2))
+            a = X("win0", BASE[0] + slot_at(0) + 192, "ex", 12, 16)
+        else:
+            act(N("ebs", 4, NS, 6), pick(s, slot_at(w), slot_at(w) + 192, "pl", 0, 2))
+            a = pick(s, slot_at(w), slot_at(w) + 192, "ex", 4 * i, 4 * i + 4)
+        tt(N("ebs", 2, 64, 3), a, R("ce", 64 * i, 64 * i + 64), O.mult)
 
     def finish_scan(s, x):
-        a = slot_at(x) + 32
-        scan(R("win%d" % s, a, a + 96), R("ebs", 0, 96), R("ebs", 97, 193), O.add, O.max)
+        scan(win(s, slot_at(x), slot_at(x) + 96), N("ebs", 0, 96, 2), N("ebs", 5, 96, 2))
 
-    def partial_base(x):
-        cp(R("dbs", 2, 98, 3), X("dbl%d" % (x % 4), 392, "bx%d" % x, 0, 2))
-
-    def partial(s, w):
-        x, win, i = w + 1, "win%d" % s, w // 2
-        tt(R("dbs", 1, 193, 3), X(win, own_at(w) + 200, "px%d" % x, 0, 4), R("sp%d" % x, 64, 128), O.mult)
-        scan(R(win, 8, 104), R("dbs", 0, 96), R("dbs", 97, 193), O.add, O.max)
-        cp(R("sb%d_%d" % (s, w), 0, 96), X(win, own_at(w) + 200, "l96", 6 * i, 6 * i + 6))
-        send(s, w)
+    def sent_base(s, x):
+        cp(win(s, 8, 72, 2), X("dbo", 3 * DB, "bx", x - 1, x + 1))
 
     def base(w, src):
+        d, a = terms(w)
         x = X("qsb", C, "seq16", 4 * w, 4 * w + 4) if src == "qsb" else X("src", 512, "seqp", 4 * w, 4 * w + 4)
-        tt(R("dbl%d" % (w % 4), 2, 194, 3), x, R("rmp", F * w, F * w + F), O.mult)
+        tt(N(d, a + 193, F, 3), x, R("rmp", F * w, F * w + F), O.mult)
 
     def twice_at(w):
-        return 128 * (w - 2) + 512 if 2 <= w < 6 else 128 * (w == 6) * 8
+        return 128 * (w // 2) if w % 2 else 512 + 64 * w
 
     def twice(w):
         for u in range(U):
-            act(R("ps", twice_at(w) + 64 * u, twice_at(w) + 64 * u + F), R("rmp", F * w, F * w + F))
+            act(N("ps", twice_at(w) + 64 * u, F), N("rmp", F * w, F))
 
     def coef(w):
-        tt(R("cr", CR * w, CR * w + 128), R("cob", 128 * w, 128 * w + 128), R("ps", twice_at(w), twice_at(w) + 128), O.mult)
+        tt(coefs(w), N("cob", 128 * w, 128), N("ps", twice_at(w), 128), O.mult)
 
     def to_cells(s, w):
         cp(X("psic%d" % s, 512, "seqp", 4 * w, 4 * w + 4), own(s, w))
@@ -277,271 +289,231 @@ def rank_program(g, core, T, topo):
     def flux(s, j, start, stop):
         mm(R("pf", 512 * j, 512 * j + 32, 1, CELLS[j]), R("psic%d" % s, 128 * j, 128 * j + CELLS[j]), R("mskw", 0, 32), start, stop)
 
-    def spread(x):
-        act(R("upf%d" % x, 0, 128), X("tab", Z + 8, "upr16", 8 * x, 8 * x + 8))
+    def pair(s, x):
+        finish_gather(s, x)
+        chain_gather(s, x)
+        finish_scan(s, x)
+        chain_scan(s, x)
+        chain_gather(s, x + 1)
+        if x == 5:
+            to_cells(s, 5)
+        chain_scan(s, x + 1)
 
-    def picks(x):
-        for u in range(U):
-            ts(R("ix%d" % x, 2 * u, 2 * u + 2), R("s2", 2 * x, 2 * x + 2), float(64 * u - 64 * x), O.add, 128.0, O.min)
-        ts(R("bx%d" % x, 0, 2), R("s3", 2 * x, 2 * x + 2), float(2 - 192 * x), O.add, 195.0, O.min)
-
-    def cells_sent(x):
-        act(R("sp%d" % x, 0, 64), X("upf%d" % x, CR, "ix%d" % x, 0, 4))
-        act(R("sp%d" % x, 64, 128), X("cr", CR * x + CR, "ix%d" % x, 0, 4, CR * x))
-
-    def fold(src, out, limit, op, t):
-        tt(R("fo" + t, 0, 64), R(src, 0, 64), R("mskw", 0, 64), O.mult)
-        scan(R("cum" + t, 16, 80), R("fo" + t, 0, 64), R("fo" + t, 0, 64), O.add, O.max)
-        tt(R("r4" + t, 0, 4), R("cum" + t, 31, 80, 16), R("cum" + t, 15, 64, 16), O.subtract)
-        ts(R(out, 0, 4), R("r4" + t, 0, 4), *([limit, O.min] if op == "min" else [limit, O.max, -limit, O.add]))
-
-    def pack(x):
-        together(True)
-        for c in others:
-            k, i = T.rank_of(c), index_of(T.rank_of(c))
-            for j in range(4):
-                act(R("pk%d" % x, 32 * i + 8 * j, 32 * i + 8 * j + 8), R("sp%d" % x, 32 * j + 8 * k, 32 * j + 8 * k + 8))
-        together(False)
-        message("pk%d" % x, NS, lambda k: NS * index_of(k), "lp%d" % x, lambda k: NS * rank, "pre%d" % x)
-
-    def unpack(x):
-        landing("lp%d" % x, NS, lambda k: NS * k, "pre%d" % x)
-        together(True)
-        for c in others:
-            k = T.rank_of(c)
-            for j in range(4):
-                act(R("ce%d" % x, 32 * j + 8 * k, 32 * j + 8 * k + 8), R("lp%d" % x, 32 * k + 8 * j, 32 * k + 8 * j + 8))
-        together(False)
-
-    def known(x):
-        fold("sp%d" % x, "px%d" % x, float(slot_at(x - 1) - 1), "min", "")
-
-    def unknown(x):
-        fold("ce%d" % x, "ex%d" % x, float(slot_at(x - 1) - 8), "max", "2")
+    col = lambda k: N("col", k, 1)
+    p16, m8 = N("p16", 0, 1), N("m8", 0, 1)
 
     load("y", "seq32", T.seq)
     load("s", "snd32", T.snd)
-    load("s", "rmb", T.rm)
     load("y", "qsb", T.qs)
+    load("s", "rmb", T.rm)
     load("y", "up32", T.up)
-    load("s", "cob", T.co)
+    load("y", "cob", T.co)
     load("y", "scb", T.sc, 16)
-    iota(R("pi", 0, 4), [[0, 4]], 0, 1, False)
-    iota(R("iot", 0, 128), [[1, 128]], 1024, -1, False)
-    iota(R("tab", 0, 64), [[3, 64]], own_at(0) + 2, 0, True)
-    iota(R("tab", C, C + 32), [[32, 4], [1, 8]], slot_at(0) + 8 * rank, 0, True)
-    iota(R("tab", C + 32, C + 64), [[3, 32]], slot_at(1) + 34, 0, True)
-    fill(R("zer", 0, 304), 0.0)
-    fill(R("neg", 0, 200), -BIG)
+    iota(R("pi", 0, 2), [[0, 2]], 0, 1)
+    iota(R("c16", 0, 12), [[16, 12]], 0)
+    iota(R("iot", 0, 192), [[1, 192]], 1024, -1)
+    iota(N("tab", C, 32), [[MW, 4], [1, 8]], slot_at(0) + 8 * rank)
+    iota(N("tab", C + 32, 32), [[3, 32]], slot_at(1) + 2)
+    iota(N("tab", 0, 320), [[BW, 5], [3, 64]], own_at(0) + 2)
+    iota(R("lim", 0, 12), [[2 * BW, 3], [0, 4]], slot_at(0) - 1)
+    iota(R("limw", 0, 48), [[BW, 6], [0, 8]], own_at(1) - 1)
+    fill(R("zer", 0, 192), 0.0)
+    ts(R("p16i", 0, 2), R("pi", 0, 2), 15, O.bitwise_and)
+    fill(win(0, 0, HD), 0.0)
+    cp(R("p16", 0, 2), R("p16i", 0, 2))
+    fill(win(0, own_at(1) - 1, WIN, BW), 0.0)
+    ts(R("m8", 0, 2), R("p16i", 0, 2), 8.0, O.is_ge)
+    ts(R("p4", 0, 4), R("c16", 0, 4), p16, O.add)
+    fill(R("cum", 0, 16), 0.0)
     together(True)
-    zeros("win0", 0, own_at(0) + 200)
-    for s in range(NR):
-        a = slot_at(0) + NS * s
-        if s == rank:
-            zeros("win0", a, a + NS)
-        else:
-            if rank > 0:
-                zeros("win0", a, a + 8 * rank)
-            if rank < NR - 1:
-                zeros("win0", a + 8 * rank + 8, a + NS)
+    term_constants(1)
+    const("dbo", 3 * DB - 1, 1)
+    const("upf", 384, 8)
+    const("cro", 384, 8)
+    const("tab", Z, 8)
+    const("pkf", 0, 16)
     together(False)
     together(True)
-    zeros("sb0_1", 0, 96)
-    zeros("win0", slot_at(1) - 8, slot_at(1) + 32)
-    zeros("win0", slot_at(1) + 32 + 24 * rank, slot_at(1) + 56 + 24 * rank)
-    for i in (1, 2):
-        negs("dbl%d" % i, 0, 192, 3)
-        negs("dbl%d" % i, 194, 386, 3)
-        zeros("dbl%d" % i, 195, 387, 3)
+    act(col(0), p16, float(MW * rank + 33))
+    act(col(1), p16, float(LW * rank + 49))
+    for j, d in enumerate(rising):
+        act(N("pkf", 5 * j, 3), N("c16", 0, 3, 4), N("p4", d, 1))
+    for j, d, n in runs():
+        act(N("pkf", 5 * j + 4, n, 5), N("p4", d, n), 200.0)
     together(False)
-    ts(R("p7", 0, 4), R("pi", 0, 4), 7, O.bitwise_and)
-    ts(R("p8", 0, 4), R("pi", 0, 4), 8, O.bitwise_and)
-    ts(R("iam", 0, 128), R("iot", 0, 128), 15, O.bitwise_and)
-    fill(R("k18", 0, 18), 0.0)
-    ts(R("mskw", 0, 128), R("iam", 0, 128), 0.0, O.is_equal)
+    together(True)
+    act(N("tab", C + 64, 64), N("tab", C, 64), float(2 * BW))
+    act(N("tab", C + 128, 32), N("tab", C, 32), float(4 * BW))
+    together(False)
 
-    cp(R("seq16", 0, 28), R("seq32", 0, 28))
     ts(R("s5", 0, 12), R("snd32", 0, 12), float(Z), O.is_ge, -8192.0, O.mult)
     ts(R("s6", 0, 12), R("snd32", 0, 12), 3.0, O.mult)
-    cp(R("rmp", 0, F), X("rmb", C, "seq16", 0, 4))
+    cp(R("seq16", 0, 28), R("seq32", 0, 28))
     tt(R("s7", 0, 12), R("s6", 0, 12), R("s5", 0, 12), O.add)
-    tt(R("z0", 0, F), X("qsb", C, "seq16", 0, 4), R("rmp", 0, F), O.mult)
+    for c in range(2):
+        ts(N("bx", c, 3, 2), N("s6", 2 + c, 3, 4), 1.0, O.add, float(3 * DB - 1), O.min)
     ts(R("l0", 0, 2), R("s7", 0, 2), float(own_at(0) + 2), O.add, 0.0, O.max)
-    ts(own(0, 0), R("z0", 0, F), 0.0, O.max)
-    cp(R("sb0_0", 0, NS), X("win0", own_at(0) + 200, "l0", 0, 2))
-    send(0, 0)
+    cp(R("rmp", 0, F), X("rmb", C, "seq16", 0, 4))
     act(R("rmp", F, C), X("rmb", C, "seq16", 4, 28))
+    for u in range(U):
+        for c in range(2):
+            ts(N("ix", 6 * u + c, 3, 2), N("snd32", 2 + c, 3, 4), float(64 * u - 64), O.add, 384.0, O.min)
+    tt(R("z0", 0, F), X("qsb", C, "seq16", 0, 4), R("rmp", 0, F), O.mult)
+    ts(R("iam", 0, 192), R("iot", 0, 192), 15, O.bitwise_and)
+    ts(own(0, 0), R("z0", 0, F), 0.0, O.max)
+    cp(R("upr16", 0, 56), R("up32", 0, 56))
+    cp(R("sb0_0", 0, NS), pick(0, 0, slot_at(0), "l0", 0, 2))
+    message("sb0_0", NS, lambda k: 0, "win0", BASE[0] + slot_at(0) + MW * rank, "arr0_0")
+
     together(True)
     twice(1)
     together(False)
     together(True)
-    for w in range(2, W):
-        twice(w)
+    for i in range(3):
+        act(N("upf", 128 * i, 128), X("tab", Z + 8, "upr16", 16 * i + 8, 16 * i + 16))
+    together(False)
+    together(True)
+    for x in (3, 5):
+        twice(x)
     together(False)
     u, fu = R("up32", 8, 56), (lambda n: R(n, 0, 48))
-    shift = OFF - 266.0
+    shift = OFF - (BW + 2 - 96)
+    ts(R("mskw", 0, 192), R("iam", 0, 192), 0.0, O.is_equal)
+    base(1, "qsb")
+    cp(R("pk16", 0, 16), R("pkf", 0, 16))
     ts(fu("uH"), u, 0x3C0, O.bitwise_and)
     ts(fu("uL"), u, 0x3F, O.bitwise_and)
+    sent_base(0, 1)
     ts(fu("ut"), u, 7, O.bitwise_and)
     ts(fu("ud"), u, float(C), O.is_ge, -8192.0, O.mult)
-    ts(fu("un"), u, float(Z), O.is_ge, -8192.0, O.mult)
-    ts(fu("ua"), fu("uH"), 5.125, O.mult, float(own_at(0) + 2), O.add)
+    ts(fu("ua"), fu("uH"), BW / 64, O.mult, float(own_at(0) + 2), O.add)
+    for v in range(U):
+        tt(N("fo", v, 96, 2), X("upf", 392, "ix", 6 * v, 6 * v + 6), N("mskw", v, 96, 2), O.mult)
     ts(fu("ub"), fu("uL"), 3.0, O.mult)
-    ts(fu("ue"), fu("uH"), 10.25, O.mult, float(slot_at(0)) - 10.25 * C - shift, O.add)
-    ts(fu("uf"), fu("uL"), 4.0, O.mult, 8.0 * rank + shift, O.add)
-    ts(fu("ug"), fu("ut"), 3.0, O.mult)
+    scan(R("cum", 16, 208), R("fo", 0, 192), R("fo", 0, 192))
+    for x in (1, 3, 5):
+        coef(x)
+    tt(R("c12", 0, 12), N("cum", 31, 12, 16), N("cum", 15, 12, 16), O.subtract)
+    together(True)
+    for v in range(U):
+        act(N("win0", LP + v, 96, 2), X("cro", 392, "ix", 6 * v, 6 * v + 6))
+    together(False)
+    keep(0, 0)
+    ts(fu("ue"), fu("uH"), BW / 32, O.mult, float(slot_at(0)) - BW / 32 * C - shift, O.add)
+    tt(R("t1", 0, 12), R("c12", 0, 12), R("lim", 0, 12), O.subtract)
+    tt(R("hx", 0, 12), R("c12", 0, 12), R("lim", 0, 12), O.min)
+    ts(R("em", 0, 12), R("t1", 0, 12), 1.0, O.is_lt, col(0), O.mult)
+    ts(R("a1", 0, 4), R("t1", 0, 4), 1.0, O.is_ge, float(BASE[0] + slot_at(0)), O.mult)
+    for j, d, n in runs():
+        ts(N("pk16", 5 * j + 3, n, 5), N("hx", d, n), 192.0, O.add)
+    tt(R("a2", 0, 4), R("a1", 0, 4), R("t1", 0, 4), O.add)
+    for i in range(3):
+        tt(N("win0", BASE[0] + 9 + 2 * i, 4, 16), N("t1", 4 * i, 4), N("em", 4 * i, 4), O.max)
+    ts(N("win0", BASE[0] + 15, 4, 16), R("a2", 0, 4), col(1), O.max)
+    cp(R("pk", 0, 3 * LW), X("win0", BASE[0] + slot_at(0), "pk16", 0, 15, LP))
+    message("pk", LW, lambda k: LW * rising.index(k), "win0", LW * rank, "pre")
+    iota(R("cei", 0, 12), [[16, 3], [LW, 4]], 0)
+    iota(R("kw", 0, 12), [[BW - 192, 6], [0, 2]], own_at(0) + 2)
+    together(True)
+    const("win0", LW * rank, LW)
+    const("ebs", 0, 192, 1, -BIG)
+    const("ebs", 192, 8, 1, -BIG)
+    act(col(2), m8, p16, 48.0)
+    act(col(3), m8, p16, 32.0)
+    act(col(4), m8, p16, -8.0)
+    act(col(5), m8, float(1 - rank % 2), float(2 * (rank % 2) - 1))
+    together(False)
+    together(True)
+    const("ebs", 9, NS, 6)
+    act(col(6), col(4), 8.0, 2.0)
+    term_constants(2)
+    term_constants(3)
+    for w in (2, 4, 6):
+        twice(w)
+    together(False)
+
+    ts(fu("uf"), fu("uL"), 6.0, O.mult, 8.0 * rank + shift, O.add)
+    ts(fu("ug"), fu("ut"), 5.0, O.mult)
     ts(fu("ui"), fu("uL"), 32.0, O.is_ge, OFF, O.mult)
     tt(fu("uc"), fu("ua"), fu("ub"), O.add)
     tt(fu("uh"), fu("uf"), fu("ug"), O.subtract)
     tt(fu("uj"), fu("ub"), fu("ui"), O.add)
-    tt(fu("uo"), fu("ue"), fu("un"), O.add)
     tt(fu("um"), fu("uc"), fu("ud"), O.add)
     tt(fu("uk"), fu("uh"), fu("uj"), O.max)
-    base(1, "qsb")
-    tt(fu("ue"), fu("uo"), fu("uk"), O.add)
-    coef(1)
-    tt(fu("ua"), fu("um"), fu("ue"), O.max)
-    ts(R("l1", 0, 2), R("s7", 2, 4), float(own_at(1) + 2 - 192), O.add, 0.0, O.max)
-    cp(R("up16", 8, 56), fu("ua"))
-    ts(R("s1", 0, 12), R("snd32", 0, 12), float(Z), O.is_ge, 1024.0, O.mult)
-    cp(R("upr16", 0, 56), R("up32", 0, 56))
-    tt(R("s2", 0, 12), R("snd32", 0, 12), R("s1", 0, 12), O.add)
-    ts(R("s3", 0, 12), R("s2", 0, 12), 3.0, O.mult)
-    picks(3)
+    ts(R("cel", 0, 12), R("cei", 0, 12), p16, O.add)
+    tt(fu("uo"), fu("ue"), fu("uk"), O.add)
+    ts(R("pla", 0, 2), N("c16", 2, 2, 5), col(3), O.add, 2.0, O.mult)
+    tt(fu("un"), fu("um"), fu("uo"), O.max)
+    tt(R("s8", 0, 12), R("s7", 0, 12), R("kw", 0, 12), O.add)
+    tt(fu("uq"), fu("un"), R("limw", 0, 48), O.min)
+    ts(R("kc", 0, 4), R("c16", 0, 4), col(6), O.add, col(5), O.mult)
+    cp(R("up16", 8, 56), fu("uq"))
+    act(R("s9", 0, 12), R("s8", 0, 12), 0.0, 1.0, AF.Relu)
     together(True)
-    for i in range(3):
-        for j in range(3):
-            a = 6 * i + 2 * j
-            relu(R("l96f", a, a + 2), R("s7", 4 * i, 4 * i + 2), float(own_at(2 * i) + 2 - 384 * i))
+    const("l16f", 9, 3, 10)
+    for j, d in enumerate(order):
+        for c in range(2):
+            act(N("l16f", 3 * j + c, 3, 10), N("s9", c, 3, 4), N("kc", d, 1) if c == rank // 2 else 0.0)
+        act(N("l16f", 3 * j + 2, 3, 10), N("hx", d, 3, 4))
     together(False)
-    together(True)
-    for i in range(1, W):
-        act(R("tab", 64 * i, 64 * i + 64), R("tab", 0, 64), float(BW * i))
-    for i in range(2, W - 1):
-        a, b = C + 32 * i, C + 32 * (i % 2)
-        act(R("tab", a, a + 32), R("tab", b, b + 32), float(BW * (i - i % 2)))
-    zeros("tab", Z, Z + 8)
-    zeros("upf3", 128, CR)
-    zeros("cr", CR * 3 + 128, CR * 4)
-    together(False)
-    together(True)
-    negs("dbl3", 0, 192, 3)
-    negs("dbl3", 194, 386, 3)
-    zeros("dbl3", 195, 387, 3)
-    negs("dbs", 0, 200)
-    zeros("cum", 0, 16)
-    together(False)
-    arrival(0, 0)
-
+    arrival(0, 0, NS)
     chain_gather(0, 1)
-    chain_scan(0, 1)
-    cp(R("sb0_1", 2, 96, 3), X("win0", own_at(1) + 200, "l1", 0, 2))
-    send(0, 1)
-    coef(3)
-    spread(3)
-    cells_sent(3)
-    pack(3)
     base(2, "qsb")
-    together(True)
-    negs("dbl0", 0, 192, 3)
-    negs("dbl0", 194, 386, 3)
-    zeros("dbl0", 195, 387, 3)
-    for i in range(2, W - 1):
-        zeros("win0", slot_at(i) - 8, slot_at(i) + (32 if i % 2 else 0))
-    for x in PAIRS:
-        zeros("ce%d" % x, 0, 128)
-    negs("ebs", 0, 97)
-    negs("ebs", 98, 194, 3)
-    zeros("ebs", 99, 195, 3)
-    zeros("cum2", 0, 16)
-    for x in (5, 1):
-        zeros("upf%d" % x, 128, CR)
-        zeros("cr", CR * x + 128, CR * (x + 1))
-    zeros("src", 352, 512)
-    together(False)
+    chain_scan(0, 1)
     coef(2)
     base(3, "qsb")
-    ts(R("ph", 0, 3), R("p8", 0, 3), float(8 * (rank % 2)), O.is_equal)
-    ts(R("pv", 0, 3), R("p7", 0, 3), 3.0, O.mult)
-    ts(R("pa", 0, 2), R("p8", 0, 2), 5.0, O.mult)
-    partial_base(3)
-    for c in others:
-        k, i = T.rank_of(c), index_of(T.rank_of(c))
-        a = 2 * i + rank // 2
-        o, v, h = R("k18", a, a + 13, 6), R("pv", 0, 3), R("ph", 0, 1)
-        add_op("v", lambda o=o, v=v, h=h, k=k: g.vector.tensor_scalar(out=o[0], in0=v[0], scalar1=float(24 * k + 10), scalar2=h[0],
-                                                                      op0=O.add, op1=O.mult), [v[1], h[1]], [o[1]])
-    known(3)
-    tt(R("l96g", 0, 18), R("l96f", 0, 18), R("k18", 0, 18), O.add)
-    tt(R("pb", 0, 2), R("pa", 0, 2), R("p7", 0, 2), O.add)
-    cp(R("l96", 0, 18), R("l96g", 0, 18))
-    ts(R("qa", 0, 28), R("seq32", 0, 28), 0x1F, O.bitwise_and)
-    ts(R("qb", 0, 28), R("seq32", 0, 28), 0x60, O.bitwise_and)
-    ts(R("qc", 0, 28), R("seq32", 0, 28), 0x180, O.bitwise_and)
-    arrival(0, 1)
-
+    cp(R("l16", 0, 30), R("l16f", 0, 30))
+    sent_base(0, 3)
+    landing("win0", LW, lambda k: LW * k, "pre")
+    act(R("ce", 0, 64), X("win0", LP, "cel", 0, 4))
+    ts(R("ex", 12, 16), N("win0", 71, 4, LW), -1.0, O.add)
+    finish_gather(0, 1)
+    finish_scan(0, 1)
     chain_gather(0, 2)
     chain_scan(0, 2)
-    partial(0, 2)
-    spread(5)
-    unpack(3)
-    picks(5)
-    coef(5)
-    cells_sent(5)
-    pack(5)
-    ts(R("pl", 0, 1), R("pb", 0, 1), 0.0, O.add)
-    ts(R("pl", 1, 2), R("pb", 1, 2), 80.0, O.add)
+    send(0, 2)
+    act(R("ce", 64, 192), X("win0", LP, "cel", 4, 12))
+    term_constants(5)
+    const("src", 352, 160)
+    for i in (1, 2, 0):
+        ts(N("ex", 4 * i, 4), N("win0", 65 + 2 * i, 4, LW), -1.0, O.add)
+    ts(R("pl", 0, 2), N("c16", 0, 2, 7), col(2), O.add)
     base(4, "qsb")
     coef(4)
     base(5, "qsb")
-    unknown(3)
-    partial_base(5)
-    known(5)
-    arrival(0, 2)
-
-    finish_gather(0, 3)
-    chain_gather(0, 3)
-    finish_scan(0, 3)
-    chain_scan(0, 3)
-    chain_gather(0, 4)
-    chain_scan(0, 4)
-    partial(0, 4)
-    unpack(5)
-    spread(1)
-    picks(1)
-    cells_sent(1)
-    pack(1)
+    ts(R("qa", 0, 28), R("seq32", 0, 28), 0x1F, O.bitwise_and)
+    ts(R("qb", 0, 28), R("seq32", 0, 28), 0x60, O.bitwise_and)
+    ts(R("qc", 0, 28), R("seq32", 0, 28), 0x180, O.bitwise_and)
+    sent_base(0, 5)
     ts(R("qd", 0, 28), R("qb", 0, 28), 4.0, O.mult)
     ts(R("qe", 0, 28), R("qc", 0, 28), 0.25, O.mult)
-    base(6, "qsb")
-    tt(R("qf", 0, 28), R("qd", 0, 28), R("qa", 0, 28), O.add)
     coef(6)
-    tt(R("qg", 0, 28), R("qf", 0, 28), R("qe", 0, 28), O.add)
-    unknown(5)
-    cp(R("seqp", 0, 28), R("qg", 0, 28))
-    for x in range(3):
-        to_cells(0, x)
-    zeros("win1", 0, own_at(0) + 200)
-    arrival(0, 4)
-
-    finish_gather(0, 5)
-    chain_gather(0, 5)
-    finish_scan(0, 5)
-    chain_scan(0, 5)
-    chain_gather(0, 6)
+    tt(R("qf", 0, 28), R("qd", 0, 28), R("qa", 0, 28), O.add)
     cp(R("scf", 0, 16, 1, 16), R("scb", 0, 16, 1, 16))
+    tt(R("qg", 0, 28), R("qf", 0, 28), R("qe", 0, 28), O.add)
+    fill(win(1, 0, HD), 0.0)
+    cp(R("seqp", 0, 28), R("qg", 0, 28))
+    fill(win(1, own_at(1) - 1, WIN, BW), 0.0)
+    to_cells(0, 0)
+    to_cells(0, 1)
+    arrival(0, 2)
+
+    pair(0, 3)
+    send(0, 4)
     mm(R("pf", 0, 16), R("mskw", 0, 128, 1, 16), R("scf", 0, 16, 1, 16))
     together(True)
     for i in range(8):
         act(R("screp", 16 * i, 16 * i + 16), R("pf", 0, 16))
     together(False)
-    chain_scan(0, 6)
-    for x in (3, 4, 5, 6):
+    base(6, "qsb")
+    for x in (2, 3, 4):
         to_cells(0, x)
+    arrival(0, 4)
+    pair(0, 5)
+    to_cells(0, 6)
 
     for i in range(4):
         mm(R("ps", 512 * i, 512 * i + CELLS[i]), R("screp", 0, 128), R("psic0", 128 * i, 128 * i + CELLS[i]))
-    known(1)
     for i in range(4):
         o, a = R("src", 128 * i, 128 * i + CELLS[i]), R("ps", 512 * i, 512 * i + CELLS[i])
         if i % 2 == 0:
@@ -551,41 +523,28 @@ def rank_program(g, core, T, topo):
     tt(R("z0", 0, F), X("src", 512, "seqp", 0, 4), R("rmp", 0, F), O.mult)
     base(1, "src")
     ts(own(1, 0), R("z0", 0, F), 0.0, O.max)
-    partial_base(1)
-    partial(1, 0)
-    unpack(1)
-    together(True)
-    for i in range(1, W - 1):
-        zeros("win1", slot_at(i) - 8, slot_at(i) + (32 if i % 2 else 0))
-    together(False)
+    sent_base(1, 1)
+    send(1, 0)
     for j in range(4):
         flux(0, j, True, False)
-    base(2, "src")
     base(3, "src")
+    base(2, "src")
+    sent_base(1, 3)
+    base(5, "src")
     to_cells(1, 0)
-    partial_base(3)
-    unknown(1)
     arrival(1, 0)
 
-    for x in (1, 3, 5):
-        finish_gather(1, x)
-        chain_gather(1, x)
-        finish_scan(1, x)
-        chain_scan(1, x)
-        chain_gather(1, x + 1)
-        chain_scan(1, x + 1)
-        if x < 5:
-            partial(1, x + 1)
-            base(x + 3, "src")
-            if x == 1:
-                base(5, "src")
-                partial_base(5)
-            to_cells(1, x)
-            to_cells(1, x + 1)
-            arrival(1, x + 1)
-        else:
-            to_cells(1, 5)
-            to_cells(1, 6)
+    for x in (1, 3):
+        pair(1, x)
+        send(1, x + 1)
+        base(x + 3, "src")
+        if x == 1:
+            sent_base(1, 5)
+        to_cells(1, x)
+        to_cells(1, x + 1)
+        arrival(1, x + 1)
+    pair(1, 5)
+    to_cells(1, 6)
 
     for j in range(4):
         flux(1, j, False, True)
@@ -605,7 +564,7 @@ def meets(x, y, same):
         return x[1] // 512 <= (y[2] - 1) // 512 and y[1] // 512 <= (x[2] - 1) // 512
     if x[0] != y[0] or x[1] >= y[2] or y[1] >= x[2]:
         return False
-    return x[3] != y[3] or x[3] == 1 or (x[1] - y[1]) % x[3] == 0
+    return not set(range(x[1], x[2], x[3])).isdisjoint(range(y[1], y[2], y[3]))
 
 
 def clash(a, b):
@@ -620,8 +579,12 @@ def clash(a, b):
     return False
 
 
-def plan_waits(ops, flagged, members):
-    known, issued, start, waits, new = {}, {}, {}, [], set(flagged)
+def plan_waits(ops, clashes, flagged, members):
+    known, issued, start, waits, new, turn, reader = {}, {}, {}, [], set(flagged), {}, {}
+    for i in range(len(ops) - 1, -1, -1):
+        for j in clashes[i]:
+            if ops[j]["q"] == ops[i]["q"]:
+                reader[j] = i
     for i, o in enumerate(ops):
         ws = []
         q = o["q"]
@@ -631,8 +594,8 @@ def plan_waits(ops, flagged, members):
             continue
         k = known.get(q, 0)
         mine = issued.setdefault(q, [[] for r in range(KQ.get(q, 1))])
-        for j in range(i - 1, -1, -1):
-            if k >> j & 1 or not clash(o, ops[j]):
+        for j in clashes[i]:
+            if k >> j & 1:
                 continue
             p = ops[j]
             if p["kind"] == "remote":
@@ -654,9 +617,12 @@ def plan_waits(ops, flagged, members):
         start[i] = k
         known[q] = k
         if o["kind"] == "c" and i not in flagged:
-            mine[sum(len(m) for m in mine) % len(mine)].append(i)
+            by_age = sorted(range(len(mine)), key=lambda n: mine[n][-1] if mine[n] else -1)
+            free = [n for n in by_age if all(k >> m & 1 or reader.get(m, i) <= i for m in mine[n])]
+            turn[i] = (free + by_age)[0]
+            mine[turn[i]].append(i)
         waits.append(ws)
-    return waits, new
+    return waits, new, turn
 
 
 def emit(g, T, queues, ops):
@@ -664,8 +630,9 @@ def emit(g, T, queues, ops):
     for i, o in enumerate(ops):
         if o["grp"] is not None and o["kind"] == "c":
             members.setdefault(o["grp"], []).append(i)
+    clashes = [[j for j in range(i - 1, -1, -1) if clash(o, ops[j])] for i, o in enumerate(ops)]
     while True:
-        waits, new = plan_waits(ops, flagged, members)
+        waits, new, turn = plan_waits(ops, clashes, flagged, members)
         if new == flagged:
             break
         flagged = new
@@ -697,7 +664,7 @@ def emit(g, T, queues, ops):
         elif i in names:
             x.then_inc(T.sem[names[i]], o["n"])
         else:
-            r = sum(count.get((q, n), 0) for n in range(KQ[q])) % KQ[q]
+            r = turn[i]
             x.then_inc(T.sem["q_%s%d" % (q, r)], 1)
             count[(q, r)] = count.get((q, r), 0) + 1
     for q, r in count:

@@ -6,18 +6,18 @@ C = W * F
 Z = C + (W - 1) * NR * CAP
 NS = NR * CAP
 MW = 48
-BW = 392
+LW = MW + NS
+BW = 400 + NR * LW
 HD = 72
 WIN = HD + BW * (W - 1) + 192
-LW = 80
-LP = NR * LW
-BASE = (LP + 192, 0)
+BASE = (256, 0)
 DB = 384
+DO = 193
 BIG = 9.0e29
-OFF = 4096.0
+DROP = BW * C // 32 - 192 + HD + 4 + 40
 CELLS = (128, 128, 96, 96)
-KQ = {"v": 14, "s": 8, "t": 2, "g": 2}
-NXS = 112
+KQ = {"v": 16, "s": 12, "t": 2, "g": 2}
+NXS = 80
 SENDS = [(s, w) for s in range(SW) for w in (0, 2, 4)]
 
 
@@ -27,6 +27,10 @@ def own_at(w):
 
 def slot_at(w):
     return HD + BW * w + 192
+
+
+def known_to(w):
+    return slot_at(w - 1) + 200
 
 
 def f32(n):
@@ -46,24 +50,23 @@ SCRATCH = {
     "qsb": ("sbuf", [128, C], "bfloat16"), "rmb": ("sbuf", [128, C], "bfloat16"), "cob": ("sbuf", [128, 2 * C], "bfloat16"),
     "scb": ("sbuf", [128, 16], "bfloat16"), "scf": f32(16),
     "seq16": u16(28), "up16": u16(56), "upr16": u16(56), "seqp": u16(28),
-    "rmp": f32(C), "cro": f32(392), "cre": f32(384), "z0": f32(F), "win0": f32(BASE[0] + WIN), "win1": f32(WIN),
-    "psic0": f32(512), "psic1": f32(512), "src": f32(512), "dbo": f32(3 * DB), "dbe": f32(DB), "ebs": f32(200),
-    "tab": f32(Z + 8), "zer": f32(192), "iot": i32(192), "iam": i32(192), "mskw": f32(192), "upf": f32(392),
-    "pi": i32(2), "p16i": i32(2), "p16": f32(2), "m8": f32(2), "c16": f32(12), "p4": f32(4), "col": f32(16), "kc": f32(4),
-    "lim": i32(12), "limw": i32(48), "kw": i32(12), "cei": i32(12),
-    "uH": i32(48), "uL": i32(48), "ut": i32(48),
-    "s5": f32(12), "s6": f32(12), "s7": f32(12), "s8": f32(12), "s9": f32(12), "l16f": f32(30), "l0": u16(2), "l16": u16(30), "ix": u16(12), "bx": u16(6),
-    "fo": f32(192), "cum": f32(208), "c12": f32(12), "t1": f32(12), "hx": f32(12), "em": f32(12), "a1": f32(4), "a2": f32(4),
-    "pkf": f32(16), "pk16": u16(16), "pk": f32(3 * LW), "ex": u16(16), "cel": u16(12), "pl": u16(2), "pla": u16(2), "ce": f32(192),
-    "screp": f32(128), "yo": f32(128),
+    "rmp": f32(C), "cro": f32(392), "cre": f32(384), "win0": f32(BASE[0] + WIN), "win1": f32(WIN),
+    "psic0": f32(512), "psic1": f32(512), "src": f32(512), "dbo": f32(DO + 3 * DB), "dbe": f32(DB + 1), "ebs": f32(200),
+    "tab": f32(Z + 8), "zer": f32(LW), "iot": i32(64), "iam": i32(64), "mskw": f32(128), "upf": f32(392),
+    "pi": i32(2), "p16i": i32(2), "p16": f32(2), "m8": f32(2), "c16": f32(16), "col": f32(16), "kc": f32(4),
+    "lim": i32(12), "limw": i32(48), "uH": i32(48), "uL": i32(48),
+    "s5": f32(12), "sz": f32(12), "s9": f32(6), "l16f": f32(36), "l0": u16(2), "l16": u16(36), "ix": u16(12), "bx": u16(6),
+    "fo": f32(192), "cum": f32(224), "c12": f32(12), "t1": f32(12), "hx": f32(12), "em": f32(12), "a1": f32(4),
+    "pk": f32(NR * LW), "pq": f32(NR * MW), "lq": f32(NR * MW), "ex": u16(16), "ce": f32(192), "hp": f32(12), "a12": f32(12),
+    "e12": f32(12), "ki": i32(40), "k16": u16(44), "screp": f32(128), "yo": f32(128),
     "qa": i32(28), "qb": i32(28), "qc": i32(28), "qd": f32(28), "qe": f32(28), "qf": f32(28), "qg": f32(28),
     "ps": ("psum", [128, 2048], "float32"), "pf": ("psum", [128, 2048], "float32"),
 }
-for _n in ("ua", "ub", "uc", "ud", "ue", "uf", "ug", "uh", "ui", "uj", "uk", "um", "un", "uo", "uq"):
+for _n in ("ua", "ub", "uc", "ud", "uf", "ug", "uh", "uj", "uk", "un", "uq"):
     SCRATCH[_n] = f32(48)
 for _k in SENDS:
     SCRATCH["sb%d_%d" % _k] = f32(3 * MW)
-SEMAPHORES = (["x%d" % i for i in range(NXS)] + ["arr%d_%d" % k for k in SENDS] + ["pre"]
+SEMAPHORES = (["x%d" % i for i in range(NXS)] + ["arr%d_%d" % k for k in SENDS] + ["pre0", "pre1", "pre2"]
               + ["q_%s%d" % (q, i) for q in KQ for i in range(KQ[q])] + ["sent"])
 PSUM = ("ps", "pf")
 
@@ -72,20 +75,9 @@ def send_calls(topo, src, dests):
     far = [d for d in dests if not topo.mates(topo.chip(src), topo.chip(d))]
     near = [d for d in dests if topo.mates(topo.chip(src), topo.chip(d))]
     far.sort(key=lambda d: topo.same_plane(topo.chip(src), topo.chip(d)))
-    calls = []
-    if len(far) == 2 and len(near) == 1:
-        e = [topo.engines(src, d) for d in far]
-        h = len(e[0]) // 2
-        calls.append([(far[0], e[0][:h]), (far[1], e[1][h:])])
-        calls.append([(near[0], topo.engines(src, near[0]))])
-    else:
-        for d in far + near:
-            calls.append([(d, topo.engines(src, d))])
-    return calls
-
-
-def engines_to(topo, src, dst, dests):
-    return sum(len(e) for call in send_calls(topo, src, dests) for d, e in call if d == dst)
+    e = [topo.engines(src, d) for d in far]
+    h = len(e[0]) // 2
+    return [[(far[0], e[0][:h]), (far[1], e[1][h:])], [(near[0], topo.engines(src, near[0]))]]
 
 
 def rank_program(g, core, T, topo):
@@ -93,16 +85,11 @@ def rank_program(g, core, T, topo):
     if rank is None:
         return
     cores = list(T.cores)
-    others = [c for c in cores if c != core]
-    calls = send_calls(topo, core, others)
+    calls = send_calls(topo, core, [c for c in cores if c != core])
     order = [T.rank_of(d) for call in calls for d, e in call]
-    rising = sorted(order)
+    mate = order[2]
     queues = {"v": g.vector, "s": g.scalar, "t": g.tensor, "g": g, "y": g.sync}
-    ops, group, groups = [], [None], [0]
-
-    def together(on):
-        groups[0] += 1
-        group[0] = groups[0] if on else None
+    ops = []
 
     def reg(name, a, b, step=1):
         return (name, a, b, step)
@@ -127,7 +114,7 @@ def rank_program(g, core, T, topo):
             rd += x
         for x in writes:
             wr += x
-        ops.append({"q": q, "fn": fn, "r": rd, "w": wr, "kind": kind, "n": n, "sem": sem, "grp": group[0]})
+        ops.append({"q": q, "fn": fn, "r": rd, "w": wr, "kind": kind, "n": n, "sem": sem})
 
     def split(out):
         return [out[1][0:1]], [out[1][1:]]
@@ -156,8 +143,8 @@ def rank_program(g, core, T, topo):
                [d0[1], d1[1]], [out[1]])
 
     def act(out, a, bias=0.0, scale=1.0, func=AF.Identity):
-        kb = K(bias)
-        add_op("s", lambda: g.scalar.activation(out=out[0], in_=a[0], func=func, bias=kb[0], scale=scale), [a[1], kb[1]], [out[1]])
+        kb, ks = K(bias), K(scale)
+        add_op("s", lambda: g.scalar.activation(out=out[0], in_=a[0], func=func, bias=kb[0], scale=ks[0]), [a[1], kb[1], ks[1]], [out[1]])
 
     def const(name, a, n, step=1, v=0.0):
         act(N(name, a, n, step), R("zer", 0, n), v)
@@ -168,10 +155,10 @@ def rank_program(g, core, T, topo):
     def turn(out, a):
         add_op("v", lambda: g.vector.transpose(out=out[0], in_=a[0]), [a[1]], [out[1]])
 
-    def load(q, name, src, p=128):
-        n = SCRATCH[name][1][1]
-        o = R(name, 0, n, 1, p)
-        add_op(q, lambda: queues[q].dma_start(o[0], src[:, :]), [], [o[1]], "dma", 16)
+    def load(q, name, src, p=128, a=0, b=None):
+        b = b or SCRATCH[name][1][1]
+        o = R(name, a, b, 1, p)
+        add_op(q, lambda: queues[q].dma_start(o[0], src[:, a:b]), [], [o[1]], "dma", 16)
 
     def iota(out, pattern, base, cm=0):
         if SCRATCH[out[1][0][0]][2] == "float32":
@@ -179,16 +166,14 @@ def rank_program(g, core, T, topo):
         else:
             add_op("g", lambda: g.iota(out[0], pattern, base, cm), [], [out[1]])
 
-    def runs():
-        out = []
-        for j, d in enumerate(rising):
-            if out and out[-1][1] + out[-1][2] == d:
-                out[-1][2] += 1
-            else:
-                out.append([j, d, 1])
-        return out
+    def gconst(name, a, n, step=1, v=0.0):
+        o, z = N(name, a, n, step), R("zer", 0, n)
+        if v == 0.0:
+            iota(o, [[0, n]], 0)
+        else:
+            add_op("g", lambda: g.affine_select(o[0], z[0], [[0, n]], O.is_gt, v, 0, 0), [z[1]], [o[1]])
 
-    def message(sb, width, src_at, dst, dst_at, sem):
+    def message(sb, width, src_at, dst, dst_at, sem, which=(0, 1)):
         def one(call):
             tr = []
             for d, e in call:
@@ -201,13 +186,14 @@ def rank_program(g, core, T, topo):
                                             src=T[sb][:, sa:sa + width], dst=T[dst][:, dst_at:dst_at + width]))
             return g.remote_dma_fused(tr, local_sem=T.sem["sent"])
 
-        for call in calls:
+        for call in [calls[i] for i in which]:
             add_op("g", lambda call=call: one(call), [[reg(sb, src_at(T.rank_of(d)), src_at(T.rank_of(d)) + width) for d, e in call]], [],
                    "remote", sum(len(e) for d, e in call))
 
-    def landing(dst, width, at, sem):
-        n = sum(engines_to(topo, c, core, [d for d in cores if d != c]) for c in others)
-        add_op("ext", None, [], [[reg(dst, at(k), at(k) + width) for k in order]], "ext", n, sem)
+    def landing(dst, width, at, sem, which=(0, 1)):
+        got = [(T.rank_of(c), len(e)) for c in cores if c != core for i in which
+               for d, e in send_calls(topo, c, [x for x in cores if x != c])[i] if d == core]
+        add_op("ext", None, [], [[reg(dst, at(k), at(k) + width) for k, n in got]], "ext", sum(n for k, n in got), sem)
 
     def win(s, a, b, step=1):
         return R("win%d" % s, BASE[s] + a, BASE[s] + b, step)
@@ -221,60 +207,67 @@ def rank_program(g, core, T, topo):
 
     def send(s, w):
         sb, i = "sb%d_%d" % (s, w), w // 2
-        act(R(sb, 2 * MW, 3 * MW), pick(s, 0, slot_at(w), "l16", 10 * i + 6, 10 * i + 9))
-        cp(R(sb, 0, 2 * MW), pick(s, 0, slot_at(w), "l16", 10 * i, 10 * i + 6))
+        for j in range(3):
+            (act if j == 1 else cp)(N(sb, MW * j, MW), pick(s, 0, slot_at(w), "l16", 12 * i + 4 * j, 12 * i + 4 * j + 3))
         message(sb, MW, lambda k: MW * order.index(k), "win%d" % s, BASE[s] + slot_at(w) + MW * rank, "arr%d_%d" % (s, w))
         keep(s, w)
 
-    def arrival(s, w, width=MW):
-        landing("win%d" % s, width, lambda k: BASE[s] + slot_at(w) + MW * k, "arr%d_%d" % (s, w))
+    def arrival(s, w, width=MW, which=(0, 1)):
+        landing("win%d" % s, width, lambda k: BASE[s] + slot_at(w) + MW * k, "arr%d_%d" % (s, w), which)
+
+    LP = known_to(1)
 
     def own(s, w):
         return win(s, own_at(w) + 2, own_at(w) + 192, 3)
 
     def terms(w):
-        return ("dbo", DB * (w // 2)) if w % 2 else ("dbe", 0)
+        return ("dbo", DO + DB * (w // 2)) if w % 2 else ("dbe", 1)
 
     def coefs(w):
-        return R("cro", 128 * (w // 2), 128 * (w // 2) + 128) if w % 2 else R("cre", 64 * w - 128, 64 * w)
+        return N("cro", 8 + 128 * (w // 2), 128) if w % 2 else N("cre", 64 * w - 128, 128)
 
-    def term_constants(w):
+    def term_constants(w, make=const):
         d, a = terms(w)
-        const(d, a + 1, 64, 3, -BIG)
-        const(d, a + 2, 64, 3)
-        const(d, a + 194, 63, 3, -BIG)
+        if w < 3:
+            make(d, a - 1, 1)
+        make(d, a + 2, 63, 3, -BIG)
+        make(d, a + 193, 64, 3, -BIG)
+        make(d, a + 194, 64, 3)
 
     def chain_gather(s, w):
         d, a = terms(w)
-        tt(N(d, a, 128, 3), pick(s, 0, own_at(w), "up16", 8 * w, 8 * w + 8), coefs(w), O.mult)
+        tt(N(d, a, 128, 3), pick(s, 0, known_to(w), "up16", 8 * w, 8 * w + 8), coefs(w), O.mult)
 
     def chain_scan(s, w):
         d, a = terms(w)
-        scan(win(s, own_at(w), own_at(w) + 192), N(d, a + 191, 192), N(d, a, 192), -BIG)
+        scan(win(s, own_at(w), own_at(w) + 192), N(d, a - 1, 192), N(d, a + 192, 192), -BIG)
 
     def finish_gather(s, x):
         w, i = x - 1, x // 2
         if (s, x) == (0, 1):
-            act(N("ebs", 4, NS, 6), X("win0", LP, "pla", 0, 2))
-            a = X("win0", BASE[0] + slot_at(0) + 192, "ex", 12, 16)
+            act(N("ebs", 4, NS, 6), pick(0, LP, own_at(1), "k16", 40, 42))
+            a = pick(0, slot_at(0), own_at(1), "ex", 12, 16)
         else:
-            act(N("ebs", 4, NS, 6), pick(s, slot_at(w), slot_at(w) + 192, "pl", 0, 2))
+            act(N("ebs", 4, NS, 6), pick(s, slot_at(w), slot_at(w) + 192, "k16", 42, 44))
             a = pick(s, slot_at(w), slot_at(w) + 192, "ex", 4 * i, 4 * i + 4)
         tt(N("ebs", 2, 64, 3), a, R("ce", 64 * i, 64 * i + 64), O.mult)
 
     def finish_scan(s, x):
-        scan(win(s, slot_at(x), slot_at(x) + 96), N("ebs", 0, 96, 2), N("ebs", 5, 96, 2))
+        scan(win(s, slot_at(x), slot_at(x) + 191, 2), N("ebs", 0, 96, 2), N("ebs", 5, 96, 2))
 
     def sent_base(s, x):
-        cp(win(s, 8, 72, 2), X("dbo", 3 * DB, "bx", x - 1, x + 1))
+        cp(win(s, 8, 72, 2), X("dbo", terms(x)[1] + 192, "bx", x - 1, x + 1))
 
     def base(w, src):
-        d, a = terms(w)
+        d, a = terms(w) if w else ("dbo", 1)
         x = X("qsb", C, "seq16", 4 * w, 4 * w + 4) if src == "qsb" else X("src", 512, "seqp", 4 * w, 4 * w + 4)
-        tt(N(d, a + 193, F, 3), x, R("rmp", F * w, F * w + F), O.mult)
+        tt(N(d, a + 1, F, 3), x, N("rmp", F * w, F), O.mult)
+
+    def first(s):
+        ts(own(s, 0), N("dbo", 2, F, 3), 0.0, O.max)
 
     def twice_at(w):
-        return 128 * (w // 2) if w % 2 else 512 + 64 * w
+        return (0, 1024, 0, 512, 1152, 640, 1280)[w] if w != 2 else 1536
 
     def twice(w):
         for u in range(U):
@@ -282,6 +275,23 @@ def rank_program(g, core, T, topo):
 
     def coef(w):
         tt(coefs(w), N("cob", 128 * w, 128), N("ps", twice_at(w), 128), O.mult)
+
+    def spread(i):
+        act(N("upf", 8 + 128 * i, 128), X("tab", Z + 8, "upr16", 16 * i + 8, 16 * i + 16))
+
+    def sent_columns(i, n):
+        for u in range(U):
+            tt(N("fo", 64 * i + u, NS * n, 2), X("upf", 8 + 128 * (i + n), "ix", 6 * u + 2 * i, 6 * u + 2 * (i + n)), N("mskw", u, NS * n, 2), O.mult)
+
+    def running(i, n):
+        scan(N("cum", 16 + 80 * i, 64 * n), N("fo", 64 * i, 64 * n), N("fo", 64 * i, 64 * n))
+
+    def folded(i, n):
+        tt(N("c12", 4 * i, 4 * n), N("cum", 31 + 80 * i, 4 * n, 16), N("cum", 15 + 80 * i, 4 * n, 16), O.subtract)
+
+    def sent_coefs(i, n):
+        for u in range(U):
+            act(N("win0", 64 * i + u, NS * n, 2), X("cro", 8 + 128 * (i + n), "ix", 6 * u + 2 * i, 6 * u + 2 * (i + n)))
 
     def to_cells(s, w):
         cp(X("psic%d" % s, 512, "seqp", 4 * w, 4 * w + 4), own(s, w))
@@ -301,228 +311,215 @@ def rank_program(g, core, T, topo):
 
     col = lambda k: N("col", k, 1)
     p16, m8 = N("p16", 0, 1), N("m8", 0, 1)
+    u, fu = R("up32", 8, 56), (lambda n: R(n, 0, 48))
 
     load("y", "seq32", T.seq)
     load("s", "snd32", T.snd)
     load("y", "qsb", T.qs)
     load("s", "rmb", T.rm)
     load("y", "up32", T.up)
-    load("y", "cob", T.co)
+    load("y", "cob", T.co, 128, 128, 256)
+    load("y", "cob", T.co, 128, 256)
     load("y", "scb", T.sc, 16)
     iota(R("pi", 0, 2), [[0, 2]], 0, 1)
-    iota(R("c16", 0, 12), [[16, 12]], 0)
-    iota(R("iot", 0, 192), [[1, 192]], 1024, -1)
+    iota(R("iot", 0, 64), [[1, 64]], 1024, -1)
+    iota(R("c16", 0, 16), [[16, 16]], 0)
     iota(N("tab", C, 32), [[MW, 4], [1, 8]], slot_at(0) + 8 * rank)
-    iota(N("tab", C + 32, 32), [[3, 32]], slot_at(1) + 2)
+    iota(N("tab", C + 32, 32), [[6, 32]], slot_at(1) + 4)
     iota(N("tab", 0, 320), [[BW, 5], [3, 64]], own_at(0) + 2)
+    iota(N("ki", 0, 16), [[16, 4], [BASE[0] // 2 + 4, 4]], 0)
+    iota(N("ki", 16, 12), [[16, 4], [64, 3]], 64)
+    iota(N("ki", 28, 4), [[LW, 4]], 0)
+    iota(N("ki", 32, 8), [[16, 2], [MW, 4]], 0)
     iota(R("lim", 0, 12), [[2 * BW, 3], [0, 4]], slot_at(0) - 1)
-    iota(R("limw", 0, 48), [[BW, 6], [0, 8]], own_at(1) - 1)
-    fill(R("zer", 0, 192), 0.0)
+    gconst("win0", BASE[0] + LP + LW * rank, MW)
+    fill(R("zer", 0, LW), 0.0)
     ts(R("p16i", 0, 2), R("pi", 0, 2), 15, O.bitwise_and)
-    fill(win(0, 0, HD), 0.0)
+    fill(win(0, -64, HD), 0.0)
     cp(R("p16", 0, 2), R("p16i", 0, 2))
-    fill(win(0, own_at(1) - 1, WIN, BW), 0.0)
+    fill(win(0, known_to(1) - 1, WIN, BW), 0.0)
+    ts(R("iam", 0, 64), R("iot", 0, 64), 15, O.bitwise_and)
     ts(R("m8", 0, 2), R("p16i", 0, 2), 8.0, O.is_ge)
-    ts(R("p4", 0, 4), R("c16", 0, 4), p16, O.add)
-    fill(R("cum", 0, 16), 0.0)
-    together(True)
+    ts(R("mskw", 0, 64), R("iam", 0, 64), 0.0, O.is_equal)
+    fill(N("cum", 15, 2, 80), 0.0)
+    const("dbo", 0, 1)
+    const("upf", 0, 1)
+    const("cro", 0, 1)
+    const("tab", Z, 1)
+    const("l16f", 3, 9, 4)
     term_constants(1)
-    const("dbo", 3 * DB - 1, 1)
-    const("upf", 384, 8)
-    const("cro", 384, 8)
-    const("tab", Z, 8)
-    const("pkf", 0, 16)
-    together(False)
-    together(True)
-    act(col(0), p16, float(MW * rank + 33))
-    act(col(1), p16, float(LW * rank + 49))
-    for j, d in enumerate(rising):
-        act(N("pkf", 5 * j, 3), N("c16", 0, 3, 4), N("p4", d, 1))
-    for j, d, n in runs():
-        act(N("pkf", 5 * j + 4, n, 5), N("p4", d, n), 200.0)
-    together(False)
-    together(True)
-    act(N("tab", C + 64, 64), N("tab", C, 64), float(2 * BW))
-    act(N("tab", C + 128, 32), N("tab", C, 32), float(4 * BW))
-    together(False)
-
-    ts(R("s5", 0, 12), R("snd32", 0, 12), float(Z), O.is_ge, -8192.0, O.mult)
-    ts(R("s6", 0, 12), R("snd32", 0, 12), 3.0, O.mult)
-    cp(R("seq16", 0, 28), R("seq32", 0, 28))
-    tt(R("s7", 0, 12), R("s6", 0, 12), R("s5", 0, 12), O.add)
-    for c in range(2):
-        ts(N("bx", c, 3, 2), N("s6", 2 + c, 3, 4), 1.0, O.add, float(3 * DB - 1), O.min)
-    ts(R("l0", 0, 2), R("s7", 0, 2), float(own_at(0) + 2), O.add, 0.0, O.max)
-    cp(R("rmp", 0, F), X("rmb", C, "seq16", 0, 4))
-    act(R("rmp", F, C), X("rmb", C, "seq16", 4, 28))
-    for u in range(U):
-        for c in range(2):
-            ts(N("ix", 6 * u + c, 3, 2), N("snd32", 2 + c, 3, 4), float(64 * u - 64), O.add, 384.0, O.min)
-    tt(R("z0", 0, F), X("qsb", C, "seq16", 0, 4), R("rmp", 0, F), O.mult)
-    ts(R("iam", 0, 192), R("iot", 0, 192), 15, O.bitwise_and)
-    ts(own(0, 0), R("z0", 0, F), 0.0, O.max)
-    cp(R("upr16", 0, 56), R("up32", 0, 56))
-    cp(R("sb0_0", 0, NS), pick(0, 0, slot_at(0), "l0", 0, 2))
-    message("sb0_0", NS, lambda k: 0, "win0", BASE[0] + slot_at(0) + MW * rank, "arr0_0")
-
-    together(True)
-    twice(1)
-    together(False)
-    together(True)
-    for i in range(3):
-        act(N("upf", 128 * i, 128), X("tab", Z + 8, "upr16", 16 * i + 8, 16 * i + 16))
-    together(False)
-    together(True)
-    for x in (3, 5):
-        twice(x)
-    together(False)
-    u, fu = R("up32", 8, 56), (lambda n: R(n, 0, 48))
-    shift = OFF - (BW + 2 - 96)
-    ts(R("mskw", 0, 192), R("iam", 0, 192), 0.0, O.is_equal)
-    base(1, "qsb")
-    cp(R("pk16", 0, 16), R("pkf", 0, 16))
-    ts(fu("uH"), u, 0x3C0, O.bitwise_and)
-    ts(fu("uL"), u, 0x3F, O.bitwise_and)
-    sent_base(0, 1)
-    ts(fu("ut"), u, 7, O.bitwise_and)
-    ts(fu("ud"), u, float(C), O.is_ge, -8192.0, O.mult)
-    ts(fu("ua"), fu("uH"), BW / 64, O.mult, float(own_at(0) + 2), O.add)
-    for v in range(U):
-        tt(N("fo", v, 96, 2), X("upf", 392, "ix", 6 * v, 6 * v + 6), N("mskw", v, 96, 2), O.mult)
-    ts(fu("ub"), fu("uL"), 3.0, O.mult)
-    scan(R("cum", 16, 208), R("fo", 0, 192), R("fo", 0, 192))
-    for x in (1, 3, 5):
-        coef(x)
-    tt(R("c12", 0, 12), N("cum", 31, 12, 16), N("cum", 15, 12, 16), O.subtract)
-    together(True)
-    for v in range(U):
-        act(N("win0", LP + v, 96, 2), X("cro", 392, "ix", 6 * v, 6 * v + 6))
-    together(False)
-    keep(0, 0)
-    ts(fu("ue"), fu("uH"), BW / 32, O.mult, float(slot_at(0)) - BW / 32 * C - shift, O.add)
-    tt(R("t1", 0, 12), R("c12", 0, 12), R("lim", 0, 12), O.subtract)
-    tt(R("hx", 0, 12), R("c12", 0, 12), R("lim", 0, 12), O.min)
-    ts(R("em", 0, 12), R("t1", 0, 12), 1.0, O.is_lt, col(0), O.mult)
-    ts(R("a1", 0, 4), R("t1", 0, 4), 1.0, O.is_ge, float(BASE[0] + slot_at(0)), O.mult)
-    for j, d, n in runs():
-        ts(N("pk16", 5 * j + 3, n, 5), N("hx", d, n), 192.0, O.add)
-    tt(R("a2", 0, 4), R("a1", 0, 4), R("t1", 0, 4), O.add)
-    for i in range(3):
-        tt(N("win0", BASE[0] + 9 + 2 * i, 4, 16), N("t1", 4 * i, 4), N("em", 4 * i, 4), O.max)
-    ts(N("win0", BASE[0] + 15, 4, 16), R("a2", 0, 4), col(1), O.max)
-    cp(R("pk", 0, 3 * LW), X("win0", BASE[0] + slot_at(0), "pk16", 0, 15, LP))
-    message("pk", LW, lambda k: LW * rising.index(k), "win0", LW * rank, "pre")
-    iota(R("cei", 0, 12), [[16, 3], [LW, 4]], 0)
-    iota(R("kw", 0, 12), [[BW - 192, 6], [0, 2]], own_at(0) + 2)
-    together(True)
-    const("win0", LW * rank, LW)
-    const("ebs", 0, 192, 1, -BIG)
-    const("ebs", 192, 8, 1, -BIG)
+    act(col(1), p16, float(LP + LW * rank + 16))
     act(col(2), m8, p16, 48.0)
     act(col(3), m8, p16, 32.0)
     act(col(4), m8, p16, -8.0)
     act(col(5), m8, float(1 - rank % 2), float(2 * (rank % 2) - 1))
-    together(False)
-    together(True)
-    const("ebs", 9, NS, 6)
+    act(N("tab", C + 64, 64), N("tab", C, 64), float(2 * BW))
+    act(N("tab", C + 128, 32), N("tab", C, 32), float(4 * BW))
     act(col(6), col(4), 8.0, 2.0)
-    term_constants(2)
-    term_constants(3)
-    for w in (2, 4, 6):
-        twice(w)
-    together(False)
+    act(R("mskw", 64, 128), R("mskw", 0, 64))
 
-    ts(fu("uf"), fu("uL"), 6.0, O.mult, 8.0 * rank + shift, O.add)
-    ts(fu("ug"), fu("ut"), 5.0, O.mult)
-    ts(fu("ui"), fu("uL"), 32.0, O.is_ge, OFF, O.mult)
+    ts(R("s5", 0, 12), R("snd32", 0, 12), float(Z), O.is_ge, -4096.0, O.mult)
+    cp(R("seq16", 0, 28), R("seq32", 0, 28))
+    tt(R("sz", 0, 12), R("snd32", 0, 12), R("s5", 0, 12), O.add)
+    ts(N("k16", 42, 2), N("c16", 0, 2, 7), col(2), O.add)
+    for c in range(2):
+        ts(N("bx", c, 3, 2), N("sz", 2 + c, 3, 4), 3.0, O.mult, 2.0, O.add)
+    ts(R("l0", 0, 2), R("sz", 0, 2), 3.0, O.mult, 2.0, O.add)
+    cp(R("rmp", 0, F), X("rmb", C, "seq16", 0, 4))
+    act(R("rmp", F, C), X("rmb", C, "seq16", 4, 28))
+    for v in range(U):
+        for c in range(2):
+            ts(N("ix", 6 * v + c, 3, 2), N("sz", 2 + c, 3, 4), float(64 * v - 56), O.add)
+    base(0, "qsb")
+    ts(R("k16", 0, 40), R("ki", 0, 40), p16, O.add)
+    twice(1)
+    ts(R("sb0_0", 0, NS), X("dbo", 192, "l0", 0, 2), 0.0, O.max)
+    cp(R("upr16", 0, 56), R("up32", 0, 56))
+    message("sb0_0", NS, lambda k: 0, "win0", BASE[0] + slot_at(0) + MW * rank, "arr0_0", (0,))
+
+    spread(0)
+    first(0)
+    base(1, "qsb")
+    coef(1)
+    sent_coefs(0, 1)
+    sent_columns(0, 1)
+    sent_base(0, 1)
+    running(0, 1)
+    act(N("pk", LW * mate + MW, NS), R("sb0_0", 0, NS))
+    spread(1)
+    spread(2)
+    ts(fu("uH"), u, 0x3C0, O.bitwise_and)
+    folded(0, 1)
+    ts(fu("uL"), u, 0x27, O.bitwise_and)
+    ts(R("a1", 0, 4), R("c12", 0, 4), float(slot_at(0)), O.is_lt, col(1), O.mult)
+    ts(N("k16", 1, 4, 4), R("c12", 0, 4), float(slot_at(0) - 1), O.min, float(BASE[0]), O.add)
+    tt(win(0, 15, 64, 16), R("a1", 0, 4), R("c12", 0, 4), O.max)
+    ts(fu("ub"), u, 3.0, O.mult)
+    for j in (2, 0, 1):
+        d = order[j]
+        (act if j == 0 else cp)(N("pk", LW * d, MW), X("win0", BASE[0] + slot_at(0), "k16", 4 * d, 4 * d + 3))
+    message("pk", LW, lambda k: LW * k, "win0", BASE[0] + LP + LW * rank, "pre0", (1,))
+    message("pk", MW, lambda k: LW * k, "win0", BASE[0] + LP + LW * rank, "pre1", (0,))
+    iota(R("limw", 0, 48), [[BW, 6], [0, 8]], known_to(1) - 1 + DROP)
+    gconst("lq", MW * rank, MW)
+    gconst("ebs", 9, NS, 6)
+    gconst("ebs", 0, NS, 6, -BIG)
+    gconst("ebs", 7, NS, 6, -BIG)
+    twice(3)
+    twice(5)
+    keep(0, 0)
+    act(col(8), col(6), 0.0, col(5))
+    twice(2)
+    act(R("kc", 0, 4), R("c16", 0, 4), col(8), col(5))
+    for i in range(3):
+        act(N("s9", 2 * i, 2), N("sz", 4 * i, 2), float(own_at(2 * i) + 2 - 384 * i), 3.0, AF.Relu)
+
+    sent_columns(1, 2)
+    ts(fu("ua"), fu("uH"), BW / 64 - 3, O.mult, float(own_at(0) + 2), O.add)
+    running(1, 2)
+    coef(3)
+    coef(5)
+    folded(1, 2)
+    sent_coefs(1, 2)
+    for i in range(3):
+        act(N("win0", 192 + i, 4, 16), N("c12", 4 * i, 4))
+    ts(fu("uf"), fu("uL"), -5.0, O.mult, 8.0 * rank + 40, O.add)
+    ts(fu("ug"), fu("uL"), 32.0, O.is_ge, float(BW + 4 - 192 + 40), O.mult)
     tt(fu("uc"), fu("ua"), fu("ub"), O.add)
-    tt(fu("uh"), fu("uf"), fu("ug"), O.subtract)
-    tt(fu("uj"), fu("ub"), fu("ui"), O.add)
-    tt(fu("um"), fu("uc"), fu("ud"), O.add)
-    tt(fu("uk"), fu("uh"), fu("uj"), O.max)
-    ts(R("cel", 0, 12), R("cei", 0, 12), p16, O.add)
-    tt(fu("uo"), fu("ue"), fu("uk"), O.add)
-    ts(R("pla", 0, 2), N("c16", 2, 2, 5), col(3), O.add, 2.0, O.mult)
-    tt(fu("un"), fu("um"), fu("uo"), O.max)
-    tt(R("s8", 0, 12), R("s7", 0, 12), R("kw", 0, 12), O.add)
+    tt(fu("uk"), fu("uf"), fu("ug"), O.max)
+    ts(fu("ud"), u, float(C), O.is_lt, float(DROP), O.mult)
+    tt(fu("uh"), fu("uc"), fu("uk"), O.add)
+    tt(R("hx", 0, 12), R("c12", 0, 12), R("lim", 0, 12), O.min)
+    tt(fu("uj"), fu("uh"), fu("ud"), O.max)
+    act(R("pq", 0, NR * MW), X("win0", BASE[0], "k16", 16, 28))
+    message("pq", MW, lambda k: MW * k, "lq", MW * rank, "pre2")
+    term_constants(2, gconst)
+    base(3, "qsb")
+    tt(fu("un"), fu("uc"), fu("uj"), O.add)
+    base(2, "qsb")
     tt(fu("uq"), fu("un"), R("limw", 0, 48), O.min)
-    ts(R("kc", 0, 4), R("c16", 0, 4), col(6), O.add, col(5), O.mult)
-    cp(R("up16", 8, 56), fu("uq"))
-    act(R("s9", 0, 12), R("s8", 0, 12), 0.0, 1.0, AF.Relu)
-    together(True)
-    const("l16f", 9, 3, 10)
+    sent_base(0, 3)
+    ts(R("up16", 8, 56), fu("uq"), float(-DROP), O.add)
+    coef(2)
+    landing("win0", LW, lambda k: BASE[0] + LP + LW * k, "pre0", (1,))
+    act(win(0, slot_at(0) + MW * mate, slot_at(0) + MW * mate + NS), win(0, LP + LW * mate + MW, LP + LW * mate + LW))
     for j, d in enumerate(order):
         for c in range(2):
-            act(N("l16f", 3 * j + c, 3, 10), N("s9", c, 3, 4), N("kc", d, 1) if c == rank // 2 else 0.0)
-        act(N("l16f", 3 * j + 2, 3, 10), N("hx", d, 3, 4))
-    together(False)
-    arrival(0, 0, NS)
+            act(N("l16f", 4 * j + c, 3, 12), N("s9", c, 3, 2), N("kc", d, 1) if c == rank // 2 else 0.0)
+    arrival(0, 0, NS, (0,))
+    ts(N("k16", 40, 2), N("c16", 1, 2, 5), col(3), O.add, 2.0, O.mult)
     chain_gather(0, 1)
-    base(2, "qsb")
+    ts(R("qa", 0, 28), R("seq32", 0, 28), 0x1F, O.bitwise_and)
     chain_scan(0, 1)
-    coef(2)
-    base(3, "qsb")
-    cp(R("l16", 0, 30), R("l16f", 0, 30))
-    sent_base(0, 3)
-    landing("win0", LW, lambda k: LW * k, "pre")
-    act(R("ce", 0, 64), X("win0", LP, "cel", 0, 4))
-    ts(R("ex", 12, 16), N("win0", 71, 4, LW), -1.0, O.add)
+    landing("win0", MW, lambda k: BASE[0] + LP + LW * k, "pre1", (0,))
+    act(R("ce", 0, 64), pick(0, LP, own_at(1), "k16", 28, 32))
+    ts(R("ex", 12, 16), win(0, LP + 39, own_at(1), LW), float(-slot_at(0)), O.add)
     finish_gather(0, 1)
+    for j, d in enumerate(order):
+        act(N("l16f", 4 * j + 2, 3, 12), N("hx", d, 3, 4))
+    ts(R("qb", 0, 28), R("seq32", 0, 28), 0x60, O.bitwise_and)
     finish_scan(0, 1)
     chain_gather(0, 2)
+    cp(R("l16", 0, 36), R("l16f", 0, 36))
     chain_scan(0, 2)
     send(0, 2)
-    act(R("ce", 64, 192), X("win0", LP, "cel", 4, 12))
-    term_constants(5)
-    const("src", 352, 160)
-    for i in (1, 2, 0):
-        ts(N("ex", 4 * i, 4), N("win0", 65 + 2 * i, 4, LW), -1.0, O.add)
-    ts(R("pl", 0, 2), N("c16", 0, 2, 7), col(2), O.add)
+    twice(4)
+    act(col(0), p16, 33.0)
+    term_constants(3)
+    for i in range(3):
+        act(N("hp", 4 * i, 4), N("c16", 0, 4, 3), col(0))
+    const("hp", rank, 3, 4)
+    landing("lq", MW, lambda k: MW * k, "pre2")
+    for i in range(3):
+        act(N("a12", 4 * i, 4), N("lq", 32 + i, 4, MW), float(1 - slot_at(2 * i)))
+    act(R("ce", 64, 192), X("lq", NR * MW, "k16", 32, 40))
     base(4, "qsb")
-    coef(4)
-    base(5, "qsb")
-    ts(R("qa", 0, 28), R("seq32", 0, 28), 0x1F, O.bitwise_and)
-    ts(R("qb", 0, 28), R("seq32", 0, 28), 0x60, O.bitwise_and)
     ts(R("qc", 0, 28), R("seq32", 0, 28), 0x180, O.bitwise_and)
-    sent_base(0, 5)
+    base(5, "qsb")
     ts(R("qd", 0, 28), R("qb", 0, 28), 4.0, O.mult)
     ts(R("qe", 0, 28), R("qc", 0, 28), 0.25, O.mult)
-    coef(6)
+    coef(4)
     tt(R("qf", 0, 28), R("qd", 0, 28), R("qa", 0, 28), O.add)
-    cp(R("scf", 0, 16, 1, 16), R("scb", 0, 16, 1, 16))
+    sent_base(0, 5)
     tt(R("qg", 0, 28), R("qf", 0, 28), R("qe", 0, 28), O.add)
-    fill(win(1, 0, HD), 0.0)
+    ts(R("t1", 0, 12), R("a12", 0, 12), 1.0, O.is_lt)
     cp(R("seqp", 0, 28), R("qg", 0, 28))
-    fill(win(1, own_at(1) - 1, WIN, BW), 0.0)
+    tt(R("em", 0, 12), R("t1", 0, 12), R("hp", 0, 12), O.mult)
+    cp(R("scf", 0, 16, 1, 16), R("scb", 0, 16, 1, 16))
+    tt(R("e12", 0, 12), R("em", 0, 12), R("a12", 0, 12), O.max)
     to_cells(0, 0)
-    to_cells(0, 1)
+    ts(R("ex", 0, 12), R("e12", 0, 12), -1.0, O.add)
     arrival(0, 2)
 
     pair(0, 3)
     send(0, 4)
+    twice(6)
+    term_constants(5)
+    const("src", 352, 32)
+    const("src", 480, 32)
     mm(R("pf", 0, 16), R("mskw", 0, 128, 1, 16), R("scf", 0, 16, 1, 16))
-    together(True)
     for i in range(8):
         act(R("screp", 16 * i, 16 * i + 16), R("pf", 0, 16))
-    together(False)
+    to_cells(0, 1)
     base(6, "qsb")
-    for x in (2, 3, 4):
-        to_cells(0, x)
+    to_cells(0, 2)
+    coef(6)
+    fill(win(1, 0, HD), 0.0)
+    to_cells(0, 3)
+    fill(win(1, known_to(1) - 1, WIN, BW), 0.0)
+    to_cells(0, 4)
     arrival(0, 4)
     pair(0, 5)
     to_cells(0, 6)
 
-    for i in range(4):
-        mm(R("ps", 512 * i, 512 * i + CELLS[i]), R("screp", 0, 128), R("psic0", 128 * i, 128 * i + CELLS[i]))
-    for i in range(4):
-        o, a = R("src", 128 * i, 128 * i + CELLS[i]), R("ps", 512 * i, 512 * i + CELLS[i])
-        if i % 2 == 0:
-            act(o, a)
-        else:
-            cp(o, a)
-    tt(R("z0", 0, F), X("src", 512, "seqp", 0, 4), R("rmp", 0, F), O.mult)
+    blocks = ((0, 288), (384, 96), (288, 64))
+    for i, (a, n) in enumerate(blocks):
+        mm(N("ps", 512 * i, n), R("screp", 0, 128), N("psic0", a, n))
+    for i, (a, n) in enumerate(blocks):
+        (cp if i == 2 else act)(N("src", a, n), N("ps", 512 * i, n))
+    base(0, "src")
     base(1, "src")
-    ts(own(1, 0), R("z0", 0, F), 0.0, O.max)
+    first(1)
     sent_base(1, 1)
     send(1, 0)
     for j in range(4):
@@ -579,7 +576,7 @@ def clash(a, b):
     return False
 
 
-def plan_waits(ops, clashes, flagged, members):
+def plan_waits(ops, clashes, flagged):
     known, issued, start, waits, new, turn, reader = {}, {}, {}, [], set(flagged), {}, {}
     for i in range(len(ops) - 1, -1, -1):
         for j in clashes[i]:
@@ -601,19 +598,14 @@ def plan_waits(ops, clashes, flagged, members):
             if p["kind"] == "remote":
                 raise ValueError("a call waits for a message's source")
             if p["q"] == q and p["kind"] == "c" and j not in flagged:
-                r = [n for n in range(len(mine)) if j in mine[n]][0]
-                ws.append(("q", (r, len(mine[r]))))
-                for m in mine[r]:
+                ws.append(("q", (turn[j], len(mine[turn[j]]))))
+                for m in mine[turn[j]]:
                     k |= 1 << m | start[m]
             else:
-                all_of = members.get(p["grp"], [j])
-                if all_of[-1] >= i:
-                    raise ValueError("a call waits for a group that isn't whole yet")
-                ws.append(("u", all_of[0]))
-                for m in all_of:
-                    k |= 1 << m | start[m]
+                ws.append(("u", j))
+                k |= 1 << j | start[j]
                 if p["kind"] == "c":
-                    new.update(all_of)
+                    new.add(j)
         start[i] = k
         known[q] = k
         if o["kind"] == "c" and i not in flagged:
@@ -622,30 +614,28 @@ def plan_waits(ops, clashes, flagged, members):
             turn[i] = (free + by_age)[0]
             mine[turn[i]].append(i)
         waits.append(ws)
-    return waits, new, turn
+    return waits, new, turn, start
 
 
 def emit(g, T, queues, ops):
-    flagged, members, names = set(), {}, {}
-    for i, o in enumerate(ops):
-        if o["grp"] is not None and o["kind"] == "c":
-            members.setdefault(o["grp"], []).append(i)
+    flagged, names = set(), {}
     clashes = [[j for j in range(i - 1, -1, -1) if clash(o, ops[j])] for i, o in enumerate(ops)]
     while True:
-        waits, new, turn = plan_waits(ops, clashes, flagged, members)
+        waits, new, turn, start = plan_waits(ops, clashes, flagged)
         if new == flagged:
             break
         flagged = new
-    own, total = 0, {}
+    own, total, last = 0, {}, {}
     for i, o in enumerate(ops):
-        first = members.get(o["grp"], [i])[0]
         if o["kind"] == "ext":
             names[i], total[i] = o["sem"], o["n"]
-        elif first in names:
-            names[i] = names[first]
         elif o["kind"] == "dma" or i in flagged:
-            names[i], total[i] = "x%d" % own, o["n"] * len(members.get(o["grp"], [i]))
-            own += 1
+            free = [x for x in last if o["kind"] == "c" and start[i] >> last[x] & 1]
+            names[i] = free[0] if free else "x%d" % own
+            total[i] = o["n"] + (total[last[free[0]]] if free else 0)
+            own += 0 if free else 1
+            if o["kind"] == "c":
+                last[names[i]] = i
     count, done, sent, waited = {}, {}, 0, set()
     for i, o in enumerate(ops):
         if o["kind"] == "ext":
@@ -664,9 +654,8 @@ def emit(g, T, queues, ops):
         elif i in names:
             x.then_inc(T.sem[names[i]], o["n"])
         else:
-            r = turn[i]
-            x.then_inc(T.sem["q_%s%d" % (q, r)], 1)
-            count[(q, r)] = count.get((q, r), 0) + 1
+            x.then_inc(T.sem["q_%s%d" % (q, turn[i])], 1)
+            count[(q, turn[i])] = count.get((q, turn[i]), 0) + 1
     for q, r in count:
         if done.get((q, r), 0) < count[(q, r)]:
             queues[q].wait_ge(T.sem["q_%s%d" % (q, r)], count[(q, r)])

@@ -1,4 +1,3 @@
-from concourse.bass import DstId, RemoteDMATransfer
 from concourse.mybir import AluOpType as O, ActivationFunctionType as AF
 
 W, F, U, CAP, SW, NR = 7, 64, 2, 8, 2, 4
@@ -12,12 +11,13 @@ HD = 72
 WIN = HD + BW * (W - 1) + 192
 BASE = (256, 0)
 DB = 384
-DO = 193
+DO = HD + 193
 BIG = 9.0e29
 DROP = BW * C // 32 - 192 + HD + 4 + 40
 CELLS = (128, 128, 96, 96)
 KQ = {"v": 16, "s": 12, "t": 2, "g": 2}
 NXS = 80
+ALL, FAR, MATE = (0, 1, 2), (0, 1), (2,)
 SENDS = [(s, w) for s in range(SW) for w in (0, 2, 4)]
 
 
@@ -49,17 +49,17 @@ SCRATCH = {
     "seq32": i32(28), "up32": i32(56), "snd32": i32(12),
     "qsb": ("sbuf", [128, C], "bfloat16"), "rmb": ("sbuf", [128, C], "bfloat16"), "cob": ("sbuf", [128, 2 * C], "bfloat16"),
     "scb": ("sbuf", [128, 16], "bfloat16"), "scf": f32(16),
-    "seq16": u16(28), "up16": u16(56), "upr16": u16(56), "seqp": u16(28),
+    "seq16": u16(28), "up16": u16(56), "upr16": u16(56),
     "rmp": f32(C), "cro": f32(392), "cre": f32(384), "win0": f32(BASE[0] + WIN), "win1": f32(WIN),
-    "psic0": f32(512), "psic1": f32(512), "src": f32(512), "dbo": f32(DO + 3 * DB), "dbe": f32(DB + 1), "ebs": f32(200),
-    "tab": f32(Z + 8), "zer": f32(LW), "iot": i32(64), "iam": i32(64), "mskw": f32(128), "upf": f32(392),
+    "psic0": f32(512), "psic1": f32(512), "src": f32(512), "dbo": f32(DO + 3 * DB), "dbe": f32(2 * DB + 1), "ebs": f32(200),
+    "tab": f32(Z + 8), "zer": f32(64), "one": f32(128), "iot": i32(128), "iam": i32(64), "mskw": f32(128), "upf": f32(392),
     "pi": i32(2), "p16i": i32(2), "p16": f32(2), "m8": f32(2), "c16": f32(16), "col": f32(16), "kc": f32(4),
     "lim": i32(12), "limw": i32(48), "uH": i32(48), "uL": i32(48),
-    "s5": f32(12), "sz": f32(12), "s9": f32(6), "l16f": f32(36), "l0": u16(2), "l16": u16(36), "ix": u16(12), "bx": u16(6),
+    "s5": f32(12), "sz": f32(12), "s9": f32(6), "l16f": f32(36), "l16": u16(36), "ix": u16(12), "bx": u16(12),
     "fo": f32(192), "cum": f32(224), "c12": f32(12), "t1": f32(12), "hx": f32(12), "em": f32(12), "a1": f32(4),
     "pk": f32(NR * LW), "pq": f32(NR * MW), "lq": f32(NR * MW), "ex": u16(16), "ce": f32(192), "hp": f32(12), "a12": f32(12),
     "e12": f32(12), "ki": i32(40), "k16": u16(44), "screp": f32(128), "yo": f32(128),
-    "qa": i32(28), "qb": i32(28), "qc": i32(28), "qd": f32(28), "qe": f32(28), "qf": f32(28), "qg": f32(28),
+    "idt": f32(C), "sq1": f32(8 + F), "rs1": f32(NS), "sl1": u16(2), "floor": f32(MW),
     "ps": ("psum", [128, 2048], "float32"), "pf": ("psum", [128, 2048], "float32"),
 }
 for _n in ("ua", "ub", "uc", "ud", "uf", "ug", "uh", "uj", "uk", "un", "uq"):
@@ -71,13 +71,9 @@ SEMAPHORES = (["x%d" % i for i in range(NXS)] + ["arr%d_%d" % k for k in SENDS] 
 PSUM = ("ps", "pf")
 
 
-def send_calls(topo, src, dests):
-    far = [d for d in dests if not topo.mates(topo.chip(src), topo.chip(d))]
-    near = [d for d in dests if topo.mates(topo.chip(src), topo.chip(d))]
-    far.sort(key=lambda d: topo.same_plane(topo.chip(src), topo.chip(d)))
-    e = [topo.engines(src, d) for d in far]
-    h = len(e[0]) // 2
-    return [[(far[0], e[0][:h]), (far[1], e[1][h:])], [(near[0], topo.engines(src, near[0]))]]
+def send_order(topo, src, dests):
+    a = topo.chip(src)
+    return sorted(dests, key=lambda d: (topo.mates(a, topo.chip(d)), topo.same_plane(a, topo.chip(d))))
 
 
 def rank_program(g, core, T, topo):
@@ -85,8 +81,7 @@ def rank_program(g, core, T, topo):
     if rank is None:
         return
     cores = list(T.cores)
-    calls = send_calls(topo, core, [c for c in cores if c != core])
-    order = [T.rank_of(d) for call in calls for d, e in call]
+    order = [T.rank_of(d) for d in send_order(topo, core, [c for c in cores if c != core])]
     mate = order[2]
     queues = {"v": g.vector, "s": g.scalar, "t": g.tensor, "g": g, "y": g.sync}
     ops = []
@@ -173,27 +168,18 @@ def rank_program(g, core, T, topo):
         else:
             add_op("g", lambda: g.affine_select(o[0], z[0], [[0, n]], O.is_gt, v, 0, 0), [z[1]], [o[1]])
 
-    def message(sb, width, src_at, dst, dst_at, sem, which=(0, 1)):
-        def one(call):
-            tr = []
-            for d, e in call:
-                rid, pid = topo.addr(d)[:2]
-                sa, m = src_at(T.rank_of(d)), sum(1 << x for x in e)
-                if len(call) == 1:
-                    return g.remote_dma(out_ap=T[dst][:, dst_at:dst_at + width], in_ap=T[sb][:, sa:sa + width], remote_sem=T.sem[sem],
-                                        local_sem=T.sem["sent"], pid=pid, routing_id=rid, dma_engine_mask=m)
-                tr.append(RemoteDMATransfer(dst_ids=[DstId(rid=rid, pnc=pid)], dma_engine_mask=m, remote_sem=T.sem[sem],
-                                            src=T[sb][:, sa:sa + width], dst=T[dst][:, dst_at:dst_at + width]))
-            return g.remote_dma_fused(tr, local_sem=T.sem["sent"])
+    def message(sb, width, src_at, dst, dst_at, sem, which=ALL):
+        for k in [order[j] for j in which]:
+            rid, pid = topo.addr(cores[k])[:2]
+            add_op("g", lambda k=k, rid=rid, pid=pid: g.remote_dma(
+                out_ap=T[dst][:, dst_at:dst_at + width], in_ap=T[sb][:, src_at(k):src_at(k) + width], remote_sem=T.sem[sem],
+                local_sem=T.sem["sent"], pid=pid, routing_id=rid, dma_engine_mask=topo.mask(core, cores[k])),
+                [[reg(sb, src_at(k), src_at(k) + width)]], [], "remote", len(topo.engines(core, cores[k])))
 
-        for call in [calls[i] for i in which]:
-            add_op("g", lambda call=call: one(call), [[reg(sb, src_at(T.rank_of(d)), src_at(T.rank_of(d)) + width) for d, e in call]], [],
-                   "remote", sum(len(e) for d, e in call))
-
-    def landing(dst, width, at, sem, which=(0, 1)):
-        got = [(T.rank_of(c), len(e)) for c in cores if c != core for i in which
-               for d, e in send_calls(topo, c, [x for x in cores if x != c])[i] if d == core]
-        add_op("ext", None, [], [[reg(dst, at(k), at(k) + width) for k, n in got]], "ext", sum(n for k, n in got), sem)
+    def landing(dst, width, at, sem, which=ALL):
+        got = [c for c in cores if c != core for j in which if send_order(topo, c, [x for x in cores if x != c])[j] == core]
+        add_op("ext", None, [], [[reg(dst, at(T.rank_of(c)), at(T.rank_of(c)) + width) for c in got]], "ext",
+               sum(len(topo.engines(c, core)) for c in got), sem)
 
     def win(s, a, b, step=1):
         return R("win%d" % s, BASE[s] + a, BASE[s] + b, step)
@@ -202,17 +188,20 @@ def rank_program(g, core, T, topo):
         return X("win%d" % s, BASE[s] + b, off, oa, ob, BASE[s] + a)
 
     def keep(s, w):
-        a = slot_at(w) + MW * rank
-        act(win(s, a, a + NS), R("sb%d_%d" % (s, w), 0, NS))
+        a, n = slot_at(w) + MW * rank, NS if (s, w) == (0, 0) else MW
+        act(win(s, a, a + n), R("sb%d_%d" % (s, w), 0, n))
 
     def send(s, w):
         sb, i = "sb%d_%d" % (s, w), w // 2
         for j in range(3):
-            (act if j == 1 else cp)(N(sb, MW * j, MW), pick(s, 0, slot_at(w), "l16", 12 * i + 4 * j, 12 * i + 4 * j + 3))
+            if w:
+                (act if j == 1 else cp)(N(sb, MW * j, MW), pick(s, 0, slot_at(w), "l16", 12 * i + 4 * j, 12 * i + 4 * j + 3))
+            else:
+                tt(N(sb, MW * j, MW), X("dbo", slot_at(0), "l16", 4 * j, 4 * j + 3), R("floor", 0, MW), O.max)
         message(sb, MW, lambda k: MW * order.index(k), "win%d" % s, BASE[s] + slot_at(w) + MW * rank, "arr%d_%d" % (s, w))
         keep(s, w)
 
-    def arrival(s, w, width=MW, which=(0, 1)):
+    def arrival(s, w, width=MW, which=ALL):
         landing("win%d" % s, width, lambda k: BASE[s] + slot_at(w) + MW * k, "arr%d_%d" % (s, w), which)
 
     LP = known_to(1)
@@ -221,7 +210,7 @@ def rank_program(g, core, T, topo):
         return win(s, own_at(w) + 2, own_at(w) + 192, 3)
 
     def terms(w):
-        return ("dbo", DO + DB * (w // 2)) if w % 2 else ("dbe", 1)
+        return ("dbo", DO + DB * (w // 2)) if w % 2 else ("dbe", 1 + DB * (w == 4))
 
     def coefs(w):
         return N("cro", 8 + 128 * (w // 2), 128) if w % 2 else N("cre", 64 * w - 128, 128)
@@ -255,26 +244,35 @@ def rank_program(g, core, T, topo):
     def finish_scan(s, x):
         scan(win(s, slot_at(x), slot_at(x) + 191, 2), N("ebs", 0, 96, 2), N("ebs", 5, 96, 2))
 
-    def sent_base(s, x):
-        cp(win(s, 8, 72, 2), X("dbo", terms(x)[1] + 192, "bx", x - 1, x + 1))
+    def sent_base(s, x, by=cp):
+        by(win(s, 8, 72, 2), X("dbo", terms(x)[1] + 192, "bx", 2 * x, 2 * x + 2, HD))
 
-    def base(w, src):
-        d, a = terms(w) if w else ("dbo", 1)
-        x = X("qsb", C, "seq16", 4 * w, 4 * w + 4) if src == "qsb" else X("src", 512, "seqp", 4 * w, 4 * w + 4)
-        tt(N(d, a + 1, F, 3), x, N("rmp", F * w, F), O.mult)
+    def base(w, src, k=0, n=F):
+        d, a = terms(w) if w else ("dbo", HD + 1)
+        tt(N(d, a + 1 + 3 * k, n, 3), X(src, C, "seq16", 4 * w + k // 16, 4 * w + (k + n) // 16), N("rmp", F * w + k, n), O.mult)
 
-    def first(s):
-        ts(own(s, 0), N("dbo", 2, F, 3), 0.0, O.max)
+    def halves(w, src):
+        return [lambda: base(w, src, 0, F // 2), lambda: base(w, src, F // 2, F // 2)]
+
+    def first(s, by=cp):
+        if by is act:
+            act(own(s, 0), N("dbo", HD + 2, F, 3), 0.0, 1.0, AF.Relu)
+        else:
+            ts(own(s, 0), N("dbo", HD + 2, F, 3), 0.0, O.max)
 
     def twice_at(w):
-        return (0, 1024, 0, 512, 1152, 640, 1280)[w] if w != 2 else 1536
+        return ("ps", 512 * (w - 1)) if w < 5 else ("pf", 512 * (w - 4))
 
     def twice(w):
+        p, a = twice_at(w)
         for u in range(U):
-            act(N("ps", twice_at(w) + 64 * u, F), N("rmp", F * w, F))
+            if w == 1:
+                act(N(p, a + 64 * u, F), N("rmp", F * w, F))
+            else:
+                mm(N(p, a + 64 * u, F), R("one", 0, 128), N("rmp", F * w, F))
 
     def coef(w):
-        tt(coefs(w), N("cob", 128 * w, 128), N("ps", twice_at(w), 128), O.mult)
+        tt(coefs(w), N("cob", 128 * w, 128), N(*twice_at(w), 128), O.mult)
 
     def spread(i):
         act(N("upf", 8 + 128 * i, 128), X("tab", Z + 8, "upr16", 16 * i + 8, 16 * i + 16))
@@ -294,20 +292,21 @@ def rank_program(g, core, T, topo):
             act(N("win0", 64 * i + u, NS * n, 2), X("cro", 8 + 128 * (i + n), "ix", 6 * u + 2 * i, 6 * u + 2 * (i + n)))
 
     def to_cells(s, w):
-        cp(X("psic%d" % s, 512, "seqp", 4 * w, 4 * w + 4), own(s, w))
+        cp(X("psic%d" % s, C, "seq16", 4 * w, 4 * w + 4), own(s, w))
 
     def flux(s, j, start, stop):
-        mm(R("pf", 512 * j, 512 * j + 32, 1, CELLS[j]), R("psic%d" % s, 128 * j, 128 * j + CELLS[j]), R("mskw", 0, 32), start, stop)
+        mm(N("pf", 512 * j, 32), N("psic%d" % s, j, 128, 4), R("mskw", 0, 32), start, stop)
 
-    def pair(s, x):
-        finish_gather(s, x)
+    def pair(s, x, meanwhile):
         chain_gather(s, x)
-        finish_scan(s, x)
+        finish_gather(s, x)
         chain_scan(s, x)
+        finish_scan(s, x)
+        meanwhile[0]()
         chain_gather(s, x + 1)
-        if x == 5:
-            to_cells(s, 5)
+        meanwhile[1]()
         chain_scan(s, x + 1)
+        meanwhile[2]()
 
     col = lambda k: N("col", k, 1)
     p16, m8 = N("p16", 0, 1), N("m8", 0, 1)
@@ -322,18 +321,16 @@ def rank_program(g, core, T, topo):
     load("y", "cob", T.co, 128, 256)
     load("y", "scb", T.sc, 16)
     iota(R("pi", 0, 2), [[0, 2]], 0, 1)
-    iota(R("iot", 0, 64), [[1, 64]], 1024, -1)
+    iota(R("iot", 0, 128), [[1, 128]], 1024, -1)
     iota(R("c16", 0, 16), [[16, 16]], 0)
     iota(N("tab", C, 32), [[MW, 4], [1, 8]], slot_at(0) + 8 * rank)
     iota(N("tab", C + 32, 32), [[6, 32]], slot_at(1) + 4)
-    iota(N("tab", 0, 320), [[BW, 5], [3, 64]], own_at(0) + 2)
+    iota(N("tab", 0, 128), [[BW, 2], [3, 64]], own_at(0) + 2)
     iota(N("ki", 0, 16), [[16, 4], [BASE[0] // 2 + 4, 4]], 0)
     iota(N("ki", 16, 12), [[16, 4], [64, 3]], 64)
-    iota(N("ki", 28, 4), [[LW, 4]], 0)
-    iota(N("ki", 32, 8), [[16, 2], [MW, 4]], 0)
+    iota(R("limw", 0, 48), [[BW, 6], [0, 8]], known_to(1) - 1 + DROP)
     iota(R("lim", 0, 12), [[2 * BW, 3], [0, 4]], slot_at(0) - 1)
-    gconst("win0", BASE[0] + LP + LW * rank, MW)
-    fill(R("zer", 0, LW), 0.0)
+    fill(R("zer", 0, 64), 0.0)
     ts(R("p16i", 0, 2), R("pi", 0, 2), 15, O.bitwise_and)
     fill(win(0, -64, HD), 0.0)
     cp(R("p16", 0, 2), R("p16i", 0, 2))
@@ -342,80 +339,77 @@ def rank_program(g, core, T, topo):
     ts(R("m8", 0, 2), R("p16i", 0, 2), 8.0, O.is_ge)
     ts(R("mskw", 0, 64), R("iam", 0, 64), 0.0, O.is_equal)
     fill(N("cum", 15, 2, 80), 0.0)
-    const("dbo", 0, 1)
+    const("dbo", HD, 1)
     const("upf", 0, 1)
     const("cro", 0, 1)
     const("tab", Z, 1)
     const("l16f", 3, 9, 4)
-    term_constants(1)
+    const("ebs", 9, NS, 6)
+    const("ebs", 0, NS, 6, -BIG)
+    const("ebs", 7, NS, 6, -BIG)
     act(col(1), p16, float(LP + LW * rank + 16))
-    act(col(2), m8, p16, 48.0)
     act(col(3), m8, p16, 32.0)
-    act(col(4), m8, p16, -8.0)
+    act(col(6), p16, float(8 - 16 * (rank % 2)), 2.0)
     act(col(5), m8, float(1 - rank % 2), float(2 * (rank % 2) - 1))
     act(N("tab", C + 64, 64), N("tab", C, 64), float(2 * BW))
     act(N("tab", C + 128, 32), N("tab", C, 32), float(4 * BW))
-    act(col(6), col(4), 8.0, 2.0)
-    act(R("mskw", 64, 128), R("mskw", 0, 64))
 
     ts(R("s5", 0, 12), R("snd32", 0, 12), float(Z), O.is_ge, -4096.0, O.mult)
     cp(R("seq16", 0, 28), R("seq32", 0, 28))
     tt(R("sz", 0, 12), R("snd32", 0, 12), R("s5", 0, 12), O.add)
-    ts(N("k16", 42, 2), N("c16", 0, 2, 7), col(2), O.add)
-    for c in range(2):
-        ts(N("bx", c, 3, 2), N("sz", 2 + c, 3, 4), 3.0, O.mult, 2.0, O.add)
-    ts(R("l0", 0, 2), R("sz", 0, 2), 3.0, O.mult, 2.0, O.add)
     cp(R("rmp", 0, F), X("rmb", C, "seq16", 0, 4))
     act(R("rmp", F, C), X("rmb", C, "seq16", 4, 28))
-    for v in range(U):
-        for c in range(2):
-            ts(N("ix", 6 * v + c, 3, 2), N("sz", 2 + c, 3, 4), float(64 * v - 56), O.add)
+    act(N("tab", 128, 128), N("tab", 0, 128), float(2 * BW))
+    act(N("tab", 256, 64), N("tab", 0, 64), float(4 * BW))
+    ts(R("bx", 0, 12), R("sz", 0, 12), 3.0, O.mult, 2.0, O.add)
     base(0, "qsb")
-    ts(R("k16", 0, 40), R("ki", 0, 40), p16, O.add)
+    ix = [lambda v=v, c=c: ts(N("ix", 6 * v + c, 3, 2), N("sz", 2 + c, 3, 4), float(64 * v - 56), O.add) for v in range(U) for c in range(2)]
+    ix[0]()
     twice(1)
-    ts(R("sb0_0", 0, NS), X("dbo", 192, "l0", 0, 2), 0.0, O.max)
-    cp(R("upr16", 0, 56), R("up32", 0, 56))
-    message("sb0_0", NS, lambda k: 0, "win0", BASE[0] + slot_at(0) + MW * rank, "arr0_0", (0,))
+    ts(R("sb0_0", 0, NS), X("dbo", HD + 192, "bx", 0, 2, HD), 0.0, O.max)
+    message("sb0_0", NS, lambda k: 0, "win0", BASE[0] + slot_at(0) + MW * rank, "arr0_0", FAR)
 
+    cp(R("upr16", 0, 56), R("up32", 0, 56))
     spread(0)
-    first(0)
+    for f in ix[1:]:
+        f()
+    ts(R("one", 0, 128), R("iot", 0, 128), 1024.0, O.is_equal)
+    for w in (3, 5, 2, 4, 6):
+        twice(w)
     base(1, "qsb")
+    ts(R("k16", 0, 28), R("ki", 0, 28), p16, O.add)
     coef(1)
+    first(0, act)
+    sent_base(0, 1, act)
     sent_coefs(0, 1)
     sent_columns(0, 1)
-    sent_base(0, 1)
+    ts(fu("uH"), u, 0x3C0, O.bitwise_and)
     running(0, 1)
     act(N("pk", LW * mate + MW, NS), R("sb0_0", 0, NS))
+    act(R("mskw", 64, 128), R("mskw", 0, 64))
     spread(1)
     spread(2)
-    ts(fu("uH"), u, 0x3C0, O.bitwise_and)
-    folded(0, 1)
     ts(fu("uL"), u, 0x27, O.bitwise_and)
+    folded(0, 1)
+    ts(fu("ub"), u, 3.0, O.mult)
     ts(R("a1", 0, 4), R("c12", 0, 4), float(slot_at(0)), O.is_lt, col(1), O.mult)
     ts(N("k16", 1, 4, 4), R("c12", 0, 4), float(slot_at(0) - 1), O.min, float(BASE[0]), O.add)
     tt(win(0, 15, 64, 16), R("a1", 0, 4), R("c12", 0, 4), O.max)
-    ts(fu("ub"), u, 3.0, O.mult)
+    ts(fu("ua"), fu("uH"), BW / 64 - 3, O.mult, float(own_at(0) + 2), O.add)
     for j in (2, 0, 1):
         d = order[j]
         (act if j == 0 else cp)(N("pk", LW * d, MW), X("win0", BASE[0] + slot_at(0), "k16", 4 * d, 4 * d + 3))
-    message("pk", LW, lambda k: LW * k, "win0", BASE[0] + LP + LW * rank, "pre0", (1,))
-    message("pk", MW, lambda k: LW * k, "win0", BASE[0] + LP + LW * rank, "pre1", (0,))
-    iota(R("limw", 0, 48), [[BW, 6], [0, 8]], known_to(1) - 1 + DROP)
-    gconst("lq", MW * rank, MW)
-    gconst("ebs", 9, NS, 6)
-    gconst("ebs", 0, NS, 6, -BIG)
-    gconst("ebs", 7, NS, 6, -BIG)
-    twice(3)
-    twice(5)
+    message("pk", LW, lambda k: LW * k, "win0", BASE[0] + LP + LW * rank, "pre0", MATE)
+    message("pk", MW, lambda k: LW * k, "win0", BASE[0] + LP + LW * rank, "pre1", FAR)
     keep(0, 0)
     act(col(8), col(6), 0.0, col(5))
-    twice(2)
-    act(R("kc", 0, 4), R("c16", 0, 4), col(8), col(5))
     for i in range(3):
         act(N("s9", 2 * i, 2), N("sz", 4 * i, 2), float(own_at(2 * i) + 2 - 384 * i), 3.0, AF.Relu)
+    act(R("kc", 0, 4), R("c16", 0, 4), col(8), col(5))
+    term_constants(1)
 
     sent_columns(1, 2)
-    ts(fu("ua"), fu("uH"), BW / 64 - 3, O.mult, float(own_at(0) + 2), O.add)
+    ts(fu("uf"), fu("uL"), -5.0, O.mult, 8.0 * rank + 40, O.add)
     running(1, 2)
     coef(3)
     coef(5)
@@ -423,135 +417,139 @@ def rank_program(g, core, T, topo):
     sent_coefs(1, 2)
     for i in range(3):
         act(N("win0", 192 + i, 4, 16), N("c12", 4 * i, 4))
-    ts(fu("uf"), fu("uL"), -5.0, O.mult, 8.0 * rank + 40, O.add)
     ts(fu("ug"), fu("uL"), 32.0, O.is_ge, float(BW + 4 - 192 + 40), O.mult)
     tt(fu("uc"), fu("ua"), fu("ub"), O.add)
     tt(fu("uk"), fu("uf"), fu("ug"), O.max)
     ts(fu("ud"), u, float(C), O.is_lt, float(DROP), O.mult)
     tt(fu("uh"), fu("uc"), fu("uk"), O.add)
-    tt(R("hx", 0, 12), R("c12", 0, 12), R("lim", 0, 12), O.min)
+    base(3, "qsb")
     tt(fu("uj"), fu("uh"), fu("ud"), O.max)
+    landing("win0", LW, lambda k: BASE[0] + LP + LW * k, "pre0", MATE)
+    const("win0", BASE[0] + LP + LW * rank, MW)
     act(R("pq", 0, NR * MW), X("win0", BASE[0], "k16", 16, 28))
     message("pq", MW, lambda k: MW * k, "lq", MW * rank, "pre2")
-    term_constants(2, gconst)
-    base(3, "qsb")
-    tt(fu("un"), fu("uc"), fu("uj"), O.add)
-    base(2, "qsb")
-    tt(fu("uq"), fu("un"), R("limw", 0, 48), O.min)
-    sent_base(0, 3)
-    ts(R("up16", 8, 56), fu("uq"), float(-DROP), O.add)
-    coef(2)
-    landing("win0", LW, lambda k: BASE[0] + LP + LW * k, "pre0", (1,))
     act(win(0, slot_at(0) + MW * mate, slot_at(0) + MW * mate + NS), win(0, LP + LW * mate + MW, LP + LW * mate + LW))
+    sent_base(0, 3, act)
+    base(2, "qsb")
+    tt(fu("un"), fu("uc"), fu("uj"), O.add)
+    tt(R("hx", 0, 12), R("c12", 0, 12), R("lim", 0, 12), O.min)
+    tt(fu("uq"), fu("un"), R("limw", 0, 48), O.min)
+    ts(N("k16", 28, 4), N("c16", 0, 4, 5), p16, O.add)
+    ts(R("up16", 8, 56), fu("uq"), float(-DROP), O.add)
+    ts(N("k16", 40, 2), N("c16", 1, 2, 5), col(3), O.add, 2.0, O.mult)
     for j, d in enumerate(order):
         for c in range(2):
             act(N("l16f", 4 * j + c, 3, 12), N("s9", c, 3, 2), N("kc", d, 1) if c == rank // 2 else 0.0)
-    arrival(0, 0, NS, (0,))
-    ts(N("k16", 40, 2), N("c16", 1, 2, 5), col(3), O.add, 2.0, O.mult)
+    arrival(0, 0, NS, FAR)
     chain_gather(0, 1)
-    ts(R("qa", 0, 28), R("seq32", 0, 28), 0x1F, O.bitwise_and)
-    chain_scan(0, 1)
-    landing("win0", MW, lambda k: BASE[0] + LP + LW * k, "pre1", (0,))
+    coef(2)
+    landing("win0", MW, lambda k: BASE[0] + LP + LW * k, "pre1", FAR)
     act(R("ce", 0, 64), pick(0, LP, own_at(1), "k16", 28, 32))
     ts(R("ex", 12, 16), win(0, LP + 39, own_at(1), LW), float(-slot_at(0)), O.add)
+    chain_scan(0, 1)
     finish_gather(0, 1)
     for j, d in enumerate(order):
         act(N("l16f", 4 * j + 2, 3, 12), N("hx", d, 3, 4))
-    ts(R("qb", 0, 28), R("seq32", 0, 28), 0x60, O.bitwise_and)
+    term_constants(2)
+    ts(N("k16", 32, 4), N("c16", 0, 4, 3), p16, O.add)
     finish_scan(0, 1)
+    ts(N("k16", 36, 4), N("c16", 1, 4, 3), p16, O.add)
     chain_gather(0, 2)
     cp(R("l16", 0, 36), R("l16f", 0, 36))
     chain_scan(0, 2)
+    cp(R("scf", 0, 16, 1, 16), R("scb", 0, 16, 1, 16))
     send(0, 2)
-    twice(4)
-    act(col(0), p16, 33.0)
-    term_constants(3)
-    for i in range(3):
-        act(N("hp", 4 * i, 4), N("c16", 0, 4, 3), col(0))
-    const("hp", rank, 3, 4)
+    const("lq", MW * rank, MW)
+    iota(N("ki", 28, 12), [[0, 3], [MW, 4]], NS + 1)
+    iota(R("idt", 0, C), [[1, C]], 0)
+    act(col(2), m8, p16, 48.0)
     landing("lq", MW, lambda k: MW * k, "pre2")
     for i in range(3):
         act(N("a12", 4 * i, 4), N("lq", 32 + i, 4, MW), float(1 - slot_at(2 * i)))
     act(R("ce", 64, 192), X("lq", NR * MW, "k16", 32, 40))
+    term_constants(3)
+    term_constants(4)
     base(4, "qsb")
-    ts(R("qc", 0, 28), R("seq32", 0, 28), 0x180, O.bitwise_and)
+    ts(N("k16", 42, 2), N("c16", 0, 2, 7), col(2), O.add)
     base(5, "qsb")
-    ts(R("qd", 0, 28), R("qb", 0, 28), 4.0, O.mult)
-    ts(R("qe", 0, 28), R("qc", 0, 28), 0.25, O.mult)
     coef(4)
-    tt(R("qf", 0, 28), R("qd", 0, 28), R("qa", 0, 28), O.add)
-    sent_base(0, 5)
-    tt(R("qg", 0, 28), R("qf", 0, 28), R("qe", 0, 28), O.add)
+    ts(R("hp", 0, 12), R("ki", 28, 40), p16, O.add)
     ts(R("t1", 0, 12), R("a12", 0, 12), 1.0, O.is_lt)
-    cp(R("seqp", 0, 28), R("qg", 0, 28))
+    fill(win(1, 0, HD), 0.0)
     tt(R("em", 0, 12), R("t1", 0, 12), R("hp", 0, 12), O.mult)
-    cp(R("scf", 0, 16, 1, 16), R("scb", 0, 16, 1, 16))
+    coef(6)
     tt(R("e12", 0, 12), R("em", 0, 12), R("a12", 0, 12), O.max)
-    to_cells(0, 0)
+    sent_base(0, 5)
     ts(R("ex", 0, 12), R("e12", 0, 12), -1.0, O.add)
+    to_cells(0, 0)
     arrival(0, 2)
 
-    pair(0, 3)
+    pair(0, 3, halves(6, "qsb") + [lambda: fill(win(1, known_to(1) - 1, WIN, BW), 0.0)])
     send(0, 4)
-    twice(6)
     term_constants(5)
-    const("src", 352, 32)
-    const("src", 480, 32)
+    const("sq1", 0, 1, 1, float(C))
+    act(N("sq1", 8, F), X("idt", C, "seq16", 4, 8))
+    act(R("rs1", 0, NS), X("rmp", 2 * F, "ix", 0, 2, F - 8))
+    const("src", C, 8)
+    const("floor", 0, MW)
+    const("psic0", C, 64)
+    const("psic1", C, 64)
+    const("floor", 8 * rank, 8, 1, -BIG)
     mm(R("pf", 0, 16), R("mskw", 0, 128, 1, 16), R("scf", 0, 16, 1, 16))
     for i in range(8):
         act(R("screp", 16 * i, 16 * i + 16), R("pf", 0, 16))
     to_cells(0, 1)
-    base(6, "qsb")
+    fill(R("dbo", 0, 8), 0.0)
     to_cells(0, 2)
-    coef(6)
-    fill(win(1, 0, HD), 0.0)
+    tt(R("fo", 0, NS), X("sq1", 8 + F, "ix", 0, 2), R("mskw", 0, NS), O.mult)
     to_cells(0, 3)
-    fill(win(1, known_to(1) - 1, WIN, BW), 0.0)
+    scan(N("cum", 16, NS), R("fo", 0, NS), R("fo", 0, NS))
     to_cells(0, 4)
     arrival(0, 4)
-    pair(0, 5)
+    pair(0, 5, [lambda: tt(R("c12", 0, 2), N("cum", 31, 2, 16), N("cum", 15, 2, 16), O.subtract), lambda: to_cells(0, 5),
+                lambda: cp(R("sl1", 0, 2), R("c12", 0, 2))])
     to_cells(0, 6)
 
-    blocks = ((0, 288), (384, 96), (288, 64))
+    blocks = ((0, 256), (256, 128), (384, 64))
     for i, (a, n) in enumerate(blocks):
         mm(N("ps", 512 * i, n), R("screp", 0, 128), N("psic0", a, n))
     for i, (a, n) in enumerate(blocks):
         (cp if i == 2 else act)(N("src", a, n), N("ps", 512 * i, n))
     base(0, "src")
-    base(1, "src")
-    first(1)
-    sent_base(1, 1)
+    tt(N("dbo", 8, NS, 2), X("src", C + 8, "sl1", 0, 2), R("rs1", 0, NS), O.mult)
     send(1, 0)
     for j in range(4):
         flux(0, j, True, False)
+    first(1)
+    base(1, "src")
     base(3, "src")
     base(2, "src")
     sent_base(1, 3)
-    base(5, "src")
+    b5 = halves(5, "src")
+    b5[0]()
     to_cells(1, 0)
     arrival(1, 0)
 
     for x in (1, 3):
-        pair(1, x)
+        pair(1, x, halves(x + 3, "src") + [b5[1] if x == 1 else lambda: None])
         send(1, x + 1)
-        base(x + 3, "src")
         if x == 1:
             sent_base(1, 5)
         to_cells(1, x)
         to_cells(1, x + 1)
         arrival(1, x + 1)
-    pair(1, 5)
+    pair(1, 5, [lambda: None, lambda: to_cells(1, 5), lambda: None])
     to_cells(1, 6)
 
     for j in range(4):
         flux(1, j, False, True)
     for j in range(4):
-        turn(R("yo", 32 * j, 32 * j + 32, 1, CELLS[j]), R("pf", 512 * j, 512 * j + 32, 1, CELLS[j]))
+        turn(N("yo", j, 32, 4), N("pf", 512 * j, 32))
     for k in range(4):
         a, b = 128 * k, min(C, 128 * k + 128)
         q = "y" if k % 2 == 1 else "s"
         add_op(q, lambda q=q, a=a, b=b, k=k: queues[q].dma_start(T.y[:, a:b], T.yo[32 * k:32 * k + 16, 0:b - a]),
-               [[("yo", 0, b - a, 1)]], [[("y", a, b, 1)]], "dma", 16)
+               [[("yo", 0, 128, 1)]], [[("y", a, b, 1)]], "dma", 16)
 
     emit(g, T, queues, ops)
 

@@ -4,33 +4,52 @@ W, F, U, CAP, SW, NR = 7, 64, 2, 8, 2, 4
 C = W * F
 Z = C + (W - 1) * NR * CAP
 NS = NR * CAP
+NF = NS - CAP
 MW = 48
-LW = MW + NS
-BW = 400 + NR * LW
-HD = 72
-WIN = HD + BW * (W - 1) + 192
-BASE = (256, 0)
+MS = MW - CAP
+LW = MW + 2 * NS
+HD = 70
+ZB = 2 * HD + 6 * C + 44
+WIN = ZB + 192 * (W - 1)
+LP = ZB - 3 * LW - 80
 DB = 384
 DO = HD + 193
 BIG = 9.0e29
-DROP = BW * C // 32 - 192 + HD + 4 + 40
-CELLS = (128, 128, 96, 96)
+CB = C // 4
 KQ = {"v": 16, "s": 12, "t": 2, "g": 2}
-NXS = 80
-ALL, FAR, MATE = (0, 1, 2), (0, 1), (2,)
+NXS = 90
+FAR, PLANE, MATE = 0, 1, 2
 SENDS = [(s, w) for s in range(SW) for w in (0, 2, 4)]
+LATER = (("pre3", 0, NS, 0), ("pre4", 128, NS, 96), ("pre5", 256, CAP, 192), ("pre6", 288, CAP, 216))
+SENT_AT = (32, 0, 16)
+
+
+def block(q, d):
+    return 16 * (q % 2) + CAP * ((d + 2 * (0 < q < NR - 1)) % NR)
+
+
+def values_at(q):
+    return NS * (1 - q % 2)
+
+
+def sent_from(q):
+    return CAP * (1 - q % 2)
+
+
+def filled_from(q):
+    return CAP + CAP * (q % 2)
+
+
+def slots_before(q, d):
+    return d == 0 or d == q + 1 < NR - 1
 
 
 def own_at(w):
-    return HD + BW * w
+    return HD + 192 * w
 
 
 def slot_at(w):
-    return HD + BW * w + 192
-
-
-def known_to(w):
-    return slot_at(w - 1) + 200
+    return ZB + 192 * w
 
 
 def f32(n):
@@ -46,29 +65,30 @@ def u16(n):
 
 
 SCRATCH = {
-    "seq32": i32(28), "up32": i32(56), "snd32": i32(12),
+    "ls": i32(96), "ls16": u16(96), "up16": u16(66),
     "qsb": ("sbuf", [128, C], "bfloat16"), "rmb": ("sbuf", [128, C], "bfloat16"), "cob": ("sbuf", [128, 2 * C], "bfloat16"),
     "scb": ("sbuf", [128, 16], "bfloat16"), "scf": f32(16),
-    "seq16": u16(28), "up16": u16(56), "upr16": u16(56),
-    "rmp": f32(C), "cro": f32(392), "cre": f32(384), "win0": f32(BASE[0] + WIN), "win1": f32(WIN),
-    "psic0": f32(512), "psic1": f32(512), "src": f32(512), "dbo": f32(DO + 3 * DB), "dbe": f32(2 * DB + 1), "ebs": f32(200),
-    "tab": f32(Z + 8), "zer": f32(64), "one": f32(128), "iot": i32(128), "iam": i32(64), "mskw": f32(128), "upf": f32(392),
-    "pi": i32(2), "p16i": i32(2), "p16": f32(2), "m8": f32(2), "c16": f32(16), "col": f32(16), "kc": f32(4),
-    "lim": i32(12), "limw": i32(48), "uH": i32(48), "uL": i32(48),
-    "s5": f32(12), "sz": f32(12), "s9": f32(6), "l16f": f32(36), "l16": u16(36), "ix": u16(12), "bx": u16(12),
-    "fo": f32(192), "cum": f32(224), "c12": f32(12), "t1": f32(12), "hx": f32(12), "em": f32(12), "a1": f32(4),
-    "pk": f32(NR * LW), "pq": f32(NR * MW), "lq": f32(NR * MW), "ex": u16(16), "ce": f32(192), "hp": f32(12), "a12": f32(12),
-    "e12": f32(12), "ki": i32(40), "k16": u16(44), "screp": f32(128), "yo": f32(128),
-    "idt": f32(C), "sq1": f32(8 + F), "rs1": f32(NS), "sl1": u16(2), "floor": f32(MW),
+    "rmp": f32(C), "cre": f32(384), "win0": f32(WIN), "win1": f32(WIN),
+    "psic0": f32(64 + C), "psic1": f32(16 + C), "src": f32(C + 8), "dbo": f32(DO + 3 * DB), "dbe": f32(DB + 1), "ebs": f32(200),
+    "tab": f32(Z + 3 * 400), "zer": f32(128), "one": f32(128), "iot": i32(128), "iam": i32(64), "mskw": f32(128),
+    "pi": i32(2), "pb": i32(2), "p16": f32(2), "c16": f32(16), "col": f32(12), "kz": f32(4), "kf": f32(10),
+    "zf": f32(60), "vz": f32(60), "x3": f32(60), "mt": i32(48), "mq": i32(48), "anew": f32(128),
+    "l16f": f32(48), "l16": u16(48), "ix": u16(24), "bx": u16(12), "k0": u16(6),
+    "fo": f32(512), "cum": f32(512), "a1": f32(12),
+    "pk": f32(NR * MW + 2 * NS), "pq": f32(10 * NS), "lq": f32(240), "rs": f32(NS), "ex": u16(16), "ce": f32(3 * MW),
+    "screp": f32(128), "yo": f32(128), "idt": f32(C), "oc": f32(C), "invs": f32(512), "iv": u16(32),
+    "sq1": f32(16 + F), "idw": f32(HD + 192), "lc": u16(14), "floor": f32(MW),
     "ps": ("psum", [128, 2048], "float32"), "pf": ("psum", [128, 2048], "float32"),
 }
-for _n in ("ua", "ub", "uc", "ud", "uf", "ug", "uh", "uj", "uk", "un", "uq"):
+for _n in ("e1", "e2", "e3", "e4", "e5", "gate", "y2"):
     SCRATCH[_n] = f32(48)
-for _k in SENDS:
+for _k in SENDS[1:]:
     SCRATCH["sb%d_%d" % _k] = f32(3 * MW)
-SEMAPHORES = (["x%d" % i for i in range(NXS)] + ["arr%d_%d" % k for k in SENDS] + ["pre0", "pre1", "pre2"]
+SEMAPHORES = (["x%d" % i for i in range(NXS)] + ["arr%d_%d" % k for k in SENDS] + ["pre%d" % i for i in range(7)]
               + ["q_%s%d" % (q, i) for q in KQ for i in range(KQ[q])] + ["sent"])
 PSUM = ("ps", "pf")
+PART = {"upf": ("tab", Z + 400), "cro": ("tab", Z + 800),
+        "upr16": ("ls16", 0), "seq16": ("ls16", 68), "k16": ("up16", 56)}
 
 
 def send_order(topo, src, dests):
@@ -76,20 +96,47 @@ def send_order(topo, src, dests):
     return sorted(dests, key=lambda d: (topo.mates(a, topo.chip(d)), topo.same_plane(a, topo.chip(d))))
 
 
+def helper_of(topo, cores, src):
+    far = [c for c in cores if c != src]
+    h = [c for c in topo.cores_of(src) if c not in cores and topo.die(c) == topo.die(src) and all(topo.may_write(c, d) for d in far)][0]
+    return h, [e for e in topo.engines(src, h) if e not in topo.engines(src, far[0])]
+
+
+def helper_program(g, core, src, T, topo):
+    cores, rank = list(T.cores), T.rank_of(src)
+    order = send_order(topo, src, [c for c in cores if c != src])
+    for sem, a0, n, b0 in LATER:
+        g.wait_ge(T.sem[sem], len(helper_of(topo, cores, src)[1]))
+        for d in order:
+            k, (rid, pid) = T.rank_of(d), topo.addr(d)[:2]
+            a, b = a0 + n * k, b0 + n * (rank - (rank > k))
+            g.remote_dma(out_ap=T.lq[:, b:b + n], in_ap=T.pq[:, a:a + n], remote_sem=T.sem[sem], local_sem=T.sem["sent"], pid=pid,
+                         routing_id=rid, dma_engine_mask=topo.mask(core, d))
+    g.wait_ge(T.sem["sent"], len(LATER) * sum(len(topo.engines(core, d)) for d in order))
+
+
 def rank_program(g, core, T, topo):
     rank = T.rank_of(core)
-    if rank is None:
-        return
     cores = list(T.cores)
+    if rank is None:
+        for c in cores:
+            if helper_of(topo, cores, c)[0] == core:
+                helper_program(g, core, c, T, topo)
+        return
     order = [T.rank_of(d) for d in send_order(topo, core, [c for c in cores if c != core])]
-    mate = order[2]
+    others = sorted(order)
     queues = {"v": g.vector, "s": g.scalar, "t": g.tensor, "g": g, "y": g.sync}
     ops = []
 
     def reg(name, a, b, step=1):
         return (name, a, b, step)
 
+    def part(name, a, b):
+        name, at = PART.get(name, (name, 0))
+        return name, a + at, b + at
+
     def R(name, a, b, step=1, p=128):
+        name, a, b = part(name, a, b)
         t = T[name]
         ap = t[0:p, a:b] if step == 1 else t[0:p, a:b:step]
         return (ap, [reg(name, a, b, step)])
@@ -98,6 +145,8 @@ def rank_program(g, core, T, topo):
         return R(name, a, a + step * (n - 1) + 1, step if n > 1 else 1)
 
     def X(name, b, off, oa, ob, a=0):
+        name, a, b = part(name, a, b)
+        off, oa, ob = part(off, oa, ob)
         return (T[name][:, a:b].indirect(T[off][:, oa:ob]), [reg(name, a, b), reg(off, oa, ob)])
 
     def K(x):
@@ -130,11 +179,12 @@ def rank_program(g, core, T, topo):
         w, r = split(out)
         add_op("v", lambda: g.vector.tensor_copy(out=out[0], in_=a[0]), [a[1]] + r, w)
 
-    def fill(out, v):
+    def fill(name, a, n, step=1, v=0.0):
+        out = N(name, a, n, step)
         add_op("v", lambda: g.vector.memset(out[0], v), [], [out[1]])
 
-    def scan(out, d0, d1, first=0.0):
-        add_op("v", lambda: g.vector.tensor_tensor_scan(out=out[0], data0=d0[0], data1=d1[0], initial=first, op0=O.add, op1=O.max),
+    def scan(out, d0, d1, first=0.0, op0=O.add, op1=O.max):
+        add_op("v", lambda: g.vector.tensor_tensor_scan(out=out[0], data0=d0[0], data1=d1[0], initial=first, op0=op0, op1=op1),
                [d0[1], d1[1]], [out[1]])
 
     def act(out, a, bias=0.0, scale=1.0, func=AF.Identity):
@@ -146,13 +196,14 @@ def rank_program(g, core, T, topo):
 
     def mm(out, lhsT, rhs, start=True, stop=True):
         add_op("t", lambda: g.tensor.matmul(out=out[0], lhsT=lhsT[0], rhs=rhs[0], start=start, stop=stop), [lhsT[1], rhs[1]], [out[1]])
+        ops[-1]["opens"] = not stop
 
     def turn(out, a):
         add_op("v", lambda: g.vector.transpose(out=out[0], in_=a[0]), [a[1]], [out[1]])
 
-    def load(q, name, src, p=128, a=0, b=None):
+    def load(q, name, src, p=128, a=0, b=None, at=0):
         b = b or SCRATCH[name][1][1]
-        o = R(name, a, b, 1, p)
+        o = R(name, at + a, at + b, 1, p)
         add_op(q, lambda: queues[q].dma_start(o[0], src[:, a:b]), [], [o[1]], "dma", 16)
 
     def iota(out, pattern, base, cm=0):
@@ -168,64 +219,65 @@ def rank_program(g, core, T, topo):
         else:
             add_op("g", lambda: g.affine_select(o[0], z[0], [[0, n]], O.is_gt, v, 0, 0), [z[1]], [o[1]])
 
-    def message(sb, width, src_at, dst, dst_at, sem, which=ALL):
+    def message(sb, width, src_at, dst, dst_at, sem, which=(FAR, PLANE, MATE)):
         for k in [order[j] for j in which]:
             rid, pid = topo.addr(cores[k])[:2]
             add_op("g", lambda k=k, rid=rid, pid=pid: g.remote_dma(
-                out_ap=T[dst][:, dst_at:dst_at + width], in_ap=T[sb][:, src_at(k):src_at(k) + width], remote_sem=T.sem[sem],
+                out_ap=T[dst][:, dst_at(k):dst_at(k) + width], in_ap=T[sb][:, src_at(k):src_at(k) + width], remote_sem=T.sem[sem],
                 local_sem=T.sem["sent"], pid=pid, routing_id=rid, dma_engine_mask=topo.mask(core, cores[k])),
                 [[reg(sb, src_at(k), src_at(k) + width)]], [], "remote", len(topo.engines(core, cores[k])))
 
-    def landing(dst, width, at, sem, which=ALL):
-        got = [c for c in cores if c != core for j in which if send_order(topo, c, [x for x in cores if x != c])[j] == core]
-        add_op("ext", None, [], [[reg(dst, at(T.rank_of(c)), at(T.rank_of(c)) + width) for c in got]], "ext",
-               sum(len(topo.engines(c, core)) for c in got), sem)
+    def landing(dst, width, at, sem, senders=others):
+        add_op("ext", None, [], [[reg(dst, at(k), at(k) + width) for k in senders]], "ext", sum(len(topo.engines(cores[k], core)) for k in senders), sem)
+
+    def hand_on(i):
+        h, engines = helper_of(topo, cores, core)
+        rid, pid = topo.addr(h)[:2]
+        a = N("pq", LATER[i][1], NR * LATER[i][2])
+        add_op("g", lambda: g.remote_dma(out_ap=a[0], in_ap=a[0], remote_sem=T.sem[LATER[i][0]], local_sem=T.sem["sent"], pid=pid,
+                                         routing_id=rid, dma_engine_mask=sum(1 << e for e in engines)), [a[1]], [], "remote", len(engines))
+
+    def handed(i):
+        landing("lq", LATER[i][2], lambda k: LATER[i][3] + LATER[i][2] * others.index(k), LATER[i][0])
 
     def win(s, a, b, step=1):
-        return R("win%d" % s, BASE[s] + a, BASE[s] + b, step)
+        return R("win%d" % s, a, b, step)
 
     def pick(s, a, b, off, oa, ob):
-        return X("win%d" % s, BASE[s] + b, off, oa, ob, BASE[s] + a)
-
-    def keep(s, w):
-        a, n = slot_at(w) + MW * rank, NS if (s, w) == (0, 0) else MW
-        act(win(s, a, a + n), R("sb%d_%d" % (s, w), 0, n))
+        return X("win%d" % s, b, off, oa, ob, a)
 
     def send(s, w):
-        sb, i = "sb%d_%d" % (s, w), w // 2
-        for j in range(3):
+        sb, i, a = "sb%d_%d" % (s, w), SENT_AT[w // 2], sent_from(rank) if w else 0
+        for j, d in enumerate(order):
             if w:
-                (act if j == 1 else cp)(N(sb, MW * j, MW), pick(s, 0, slot_at(w), "l16", 12 * i + 4 * j, 12 * i + 4 * j + 3))
+                (act if j == 1 else cp)(N(sb, MW * j, MW), pick(s, 0, slot_at(w), "l16", i + 4 * d, i + 4 * d + 3))
             else:
-                tt(N(sb, MW * j, MW), X("dbo", slot_at(0), "l16", 4 * j, 4 * j + 3), R("floor", 0, MW), O.max)
-        message(sb, MW, lambda k: MW * order.index(k), "win%d" % s, BASE[s] + slot_at(w) + MW * rank, "arr%d_%d" % (s, w))
-        keep(s, w)
+                tt(N(sb, MW * j, MW), X("src", C + 8, "lc", 4 * j, 4 * j + 3), R("floor", 0, MW), O.max)
+        message(sb, MS if w else MW, lambda k: MW * order.index(k) + a, "win%d" % s, lambda k: slot_at(w) + MW * rank + a, "arr%d_%d" % (s, w))
+        b = slot_at(w) + MW * rank + filled_from(rank)
+        act(win(s, b, b + NF), N(sb, filled_from(rank), NF))
 
-    def arrival(s, w, width=MW, which=ALL):
-        landing("win%d" % s, width, lambda k: BASE[s] + slot_at(w) + MW * k, "arr%d_%d" % (s, w), which)
+    def arrival(s, w):
+        landing("win%d" % s, MS if w else MW, lambda k: slot_at(w) + MW * k + (sent_from(k) if w else 0), "arr%d_%d" % (s, w))
 
-    LP = known_to(1)
-
-    def own(s, w):
-        return win(s, own_at(w) + 2, own_at(w) + 192, 3)
+    def own(s, w, n=1):
+        return win(s, own_at(w) + 2, own_at(w + n), 3)
 
     def terms(w):
-        return ("dbo", DO + DB * (w // 2)) if w % 2 else ("dbe", 1 + DB * (w == 4))
+        return ("dbo", DO + DB * (w // 2)) if w % 2 else ("dbe", 1)
 
     def coefs(w):
-        return N("cro", 8 + 128 * (w // 2), 128) if w % 2 else N("cre", 64 * w - 128, 128)
+        return N("cro", 16 + 128 * (w // 2), 128) if w % 2 else N("cre", 64 * w - 128, 128)
 
-    def term_constants(w, make=const):
+    def term_constants(w, make):
         d, a = terms(w)
-        if w < 3:
-            make(d, a - 1, 1)
-        make(d, a + 2, 63, 3, -BIG)
+        make(d, a - 1, 64, 3, -BIG) if w < 3 else make(d, a + 2, 63, 3, -BIG)
         make(d, a + 193, 64, 3, -BIG)
         make(d, a + 194, 64, 3)
 
     def chain_gather(s, w):
         d, a = terms(w)
-        tt(N(d, a, 128, 3), pick(s, 0, known_to(w), "up16", 8 * w, 8 * w + 8), coefs(w), O.mult)
+        tt(N(d, a, 128, 3), pick(s, 0, slot_at(w), "up16", 8 * w, 8 * w + 8), coefs(w), O.mult)
 
     def chain_scan(s, w):
         d, a = terms(w)
@@ -234,31 +286,36 @@ def rank_program(g, core, T, topo):
     def finish_gather(s, x):
         w, i = x - 1, x // 2
         if (s, x) == (0, 1):
-            act(N("ebs", 4, NS, 6), pick(0, LP, own_at(1), "k16", 40, 42))
-            a = pick(0, slot_at(0), own_at(1), "ex", 12, 16)
+            act(N("ebs", 4, NS, 6), pick(0, LP, ZB, "k16", 8, 10))
+            a = pick(0, LP, slot_at(1), "ex", 12, 15)
         else:
-            act(N("ebs", 4, NS, 6), pick(s, slot_at(w), slot_at(w) + 192, "k16", 42, 44))
-            a = pick(s, slot_at(w), slot_at(w) + 192, "ex", 4 * i, 4 * i + 4)
-        tt(N("ebs", 2, 64, 3), a, R("ce", 64 * i, 64 * i + 64), O.mult)
+            if x == 1:
+                act(N("ebs", 4, NS, 6), pick(s, slot_at(w), slot_at(x), "lc", 12, 14))
+            a = pick(s, slot_at(w), slot_at(x), "ex", 4 * i, 4 * i + 3)
+        tt(N("ebs", 2, MW, 3), a, N("ce", MW * i, MW), O.mult)
+
+    def others_base(at, step):
+        act(N("ebs", 4, NF, 6), N("lq", at, NF, step))
 
     def finish_scan(s, x):
-        scan(win(s, slot_at(x), slot_at(x) + 191, 2), N("ebs", 0, 96, 2), N("ebs", 5, 96, 2))
+        scan(win(s, slot_at(x), slot_at(x) + 143, 2), N("ebs", 0, 72, 2), N("ebs", 5, 72, 2))
 
-    def sent_base(s, x, by=cp):
-        by(win(s, 8, 72, 2), X("dbo", terms(x)[1] + 192, "bx", 2 * x, 2 * x + 2, HD))
+    def sent_base(out, x, by=act):
+        by(out, X("dbo", terms(x)[1] + 192, "bx", 2 * x, 2 * x + 2))
 
-    def base(w, src, k=0, n=F):
+    def base(w, src, k=0, n=F, by=cp):
         d, a = terms(w) if w else ("dbo", HD + 1)
-        tt(N(d, a + 1 + 3 * k, n, 3), X(src, C, "seq16", 4 * w + k // 16, 4 * w + (k + n) // 16), N("rmp", F * w + k, n), O.mult)
+        o, x = N(d, a + 1 + 3 * k, n, 3), X(src, C, "seq16", 4 * w + k // 16, 4 * w + (k + n) // 16)
+        if src == "src":
+            by(o, x)
+        else:
+            tt(o, x, N("rmp", F * w + k, n), O.mult)
 
     def halves(w, src):
         return [lambda: base(w, src, 0, F // 2), lambda: base(w, src, F // 2, F // 2)]
 
-    def first(s, by=cp):
-        if by is act:
-            act(own(s, 0), N("dbo", HD + 2, F, 3), 0.0, 1.0, AF.Relu)
-        else:
-            ts(own(s, 0), N("dbo", HD + 2, F, 3), 0.0, O.max)
+    def removal(a, b, by=act):
+        by(R("rmp", F * a, F * b), X("rmb", C, "seq16", 4 * a, 4 * b))
 
     def twice_at(w):
         return ("ps", 512 * (w - 1)) if w < 5 else ("pf", 512 * (w - 4))
@@ -266,36 +323,49 @@ def rank_program(g, core, T, topo):
     def twice(w):
         p, a = twice_at(w)
         for u in range(U):
-            if w == 1:
-                act(N(p, a + 64 * u, F), N("rmp", F * w, F))
-            else:
-                mm(N(p, a + 64 * u, F), R("one", 0, 128), N("rmp", F * w, F))
+            mm(N(p, a + 64 * u, F), R("one", 0, 128), N("rmp", F * w, F))
+
+    def added(at, *names):
+        for a in names:
+            mm(N("pf", at, 48), R("one", 0, 128), R(a, 0, 48), a == names[0], a == names[-1])
 
     def coef(w):
         tt(coefs(w), N("cob", 128 * w, 128), N(*twice_at(w), 128), O.mult)
 
     def spread(i):
-        act(N("upf", 8 + 128 * i, 128), X("tab", Z + 8, "upr16", 16 * i + 8, 16 * i + 16))
+        act(N("upf", 16 + 128 * i, 128), X("tab", Z + 8, "upr16", 16 * i + 8, 16 * i + 16))
 
-    def sent_columns(i, n):
-        for u in range(U):
-            tt(N("fo", 64 * i + u, NS * n, 2), X("upf", 8 + 128 * (i + n), "ix", 6 * u + 2 * i, 6 * u + 2 * (i + n)), N("mskw", u, NS * n, 2), O.mult)
+    def sent(name, i, u):
+        return X(name, 16 + 128 * (i + 1), "ix", 12 * u + 4 * i + 2, 12 * u + 4 * i + 4)
 
-    def running(i, n):
-        scan(N("cum", 16 + 80 * i, 64 * n), N("fo", 64 * i, 64 * n), N("fo", 64 * i, 64 * n))
+    def sent_columns(i, u):
+        tt(N("fo", 64 * i + u, NS, 2), sent("upf", i, u), N("mskw", u, NS, 2), O.mult)
 
-    def folded(i, n):
-        tt(N("c12", 4 * i, 4 * n), N("cum", 31 + 80 * i, 4 * n, 16), N("cum", 15 + 80 * i, 4 * n, 16), O.subtract)
+    def fold(a, n):
+        scan(N("cum", a, n), N("anew", 0, n), N("fo", a, n), 0.0, O.mult, O.add)
 
-    def sent_coefs(i, n):
-        for u in range(U):
-            act(N("win0", 64 * i + u, NS * n, 2), X("cro", 8 + 128 * (i + n), "ix", 6 * u + 2 * i, 6 * u + 2 * (i + n)))
+    def folded(a, n):
+        return N("cum", 16 * a + 15, n, 16)
 
-    def to_cells(s, w):
-        cp(X("psic%d" % s, C, "seq16", 4 * w, 4 * w + 4), own(s, w))
+    def sent_lists(i):
+        for c in range(2):
+            act(N("l16f", SENT_AT[i] + rank % 2 + (c ^ turned), NR, 4), R("zer", 0, NR), N("x3", 48 + 4 * i + c, 1))
+        act(N("l16f", SENT_AT[i] + values_at(rank) // 16, NR, 4), folded(4 * i, NR), 0.0, -1.0)
 
-    def flux(s, j, start, stop):
-        mm(N("pf", 512 * j, 32), N("psic%d" % s, j, 128, 4), R("mskw", 0, 32), start, stop)
+    def scattered(w, n=1):
+        cp(X("psic0", 64 + C, "seq16", 4 * w, 4 * (w + n), 64), own(0, w, n))
+
+    def gathered(j, by):
+        by(N("psic1", 16 + CB * j, CB), pick(1, 0, own_at(W), "iv", 8 * j, 8 * j + CB // 16))
+
+    def flux(s, j):
+        mm(N("pf", 512 * j, 32), N("psic1", CB * j, 128) if s else N("psic0", j, 128, 4), R("mskw", 0, 32), s == 0, s == 1)
+
+    def inverse(a, b):
+        cp(X("invs", C, "seq16", 4 * a, 4 * b), R("oc", F * a, F * b))
+
+    def inverse_masked(j):
+        tt(N("fo", 128 * j, 128), N("invs", j, 128, 4), N("ps", 0, 128), O.mult)
 
     def pair(s, x, meanwhile):
         chain_gather(s, x)
@@ -309,246 +379,299 @@ def rank_program(g, core, T, topo):
         meanwhile[2]()
 
     col = lambda k: N("col", k, 1)
-    p16, m8 = N("p16", 0, 1), N("m8", 0, 1)
-    u, fu = R("up32", 8, 56), (lambda n: R(n, 0, 48))
+    p16, m8 = N("p16", 0, 1), N("p16", 1, 1)
+    fu = lambda n: R(n, 0, 48)
+    PK = lambda d: NS + MW * d
+    up = R("ls", 8, 56)
+    twin = rank ^ 1
+    turned = int(0 < rank < NR - 1)
 
-    load("y", "seq32", T.seq)
-    load("s", "snd32", T.snd)
+    load("y", "ls", T.seq, 128, 0, 28, 68)
+    load("s", "ls", T.snd, 128, 0, 12, 56)
+    load("y", "scb", T.sc, 16)
+    load("s", "ls", T.up, 128, 0, 56)
+    load("y", "rmb", T.rm)
     load("y", "qsb", T.qs)
-    load("s", "rmb", T.rm)
-    load("y", "up32", T.up)
     load("y", "cob", T.co, 128, 128, 256)
     load("y", "cob", T.co, 128, 256)
-    load("y", "scb", T.sc, 16)
     iota(R("pi", 0, 2), [[0, 2]], 0, 1)
     iota(R("iot", 0, 128), [[1, 128]], 1024, -1)
+    iota(N("tab", C, NS), [[MW, NR], [1, CAP]], ZB - LP + block(rank ^ 2, rank))
+    iota(N("tab", C + CAP * twin, CAP), [[1, CAP]], ZB - LP + MW * twin + block(twin, rank))
+    iota(N("tab", 0, F), [[-3, F]], -HD - 2)
+    for a, b, k in ((0, rank + 1, 0), (rank + 1, NR, rank)) if turned else ((0, NR, -(rank == 0)),):
+        iota(N("tab", C + NS + CAP * a, CAP * (b - a)), [[-6, CAP * (b - a)]], -slot_at(1) - 4 - MW * k)
     iota(R("c16", 0, 16), [[16, 16]], 0)
-    iota(N("tab", C, 32), [[MW, 4], [1, 8]], slot_at(0) + 8 * rank)
-    iota(N("tab", C + 32, 32), [[6, 32]], slot_at(1) + 4)
-    iota(N("tab", 0, 128), [[BW, 2], [3, 64]], own_at(0) + 2)
-    iota(N("ki", 0, 16), [[16, 4], [BASE[0] // 2 + 4, 4]], 0)
-    iota(N("ki", 16, 12), [[16, 4], [64, 3]], 64)
-    iota(R("limw", 0, 48), [[BW, 6], [0, 8]], known_to(1) - 1 + DROP)
-    iota(R("lim", 0, 12), [[2 * BW, 3], [0, 4]], slot_at(0) - 1)
-    fill(R("zer", 0, 64), 0.0)
-    ts(R("p16i", 0, 2), R("pi", 0, 2), 15, O.bitwise_and)
-    fill(win(0, -64, HD), 0.0)
-    cp(R("p16", 0, 2), R("p16i", 0, 2))
-    fill(win(0, known_to(1) - 1, WIN, BW), 0.0)
+    gconst("win0", LP + 3 * LW + NS + 1, CAP, 6)
+    gconst("l16f", 3, 12, 4)
+    fill("zer", 0, 128)
+    ts(N("pb", 0, 1), N("pi", 0, 1), 15, O.bitwise_and)
+    fill("tab", Z, 3, 400)
+    cp(p16, N("pb", 0, 1))
     ts(R("iam", 0, 64), R("iot", 0, 64), 15, O.bitwise_and)
-    ts(R("m8", 0, 2), R("p16i", 0, 2), 8.0, O.is_ge)
+    ts(m8, p16, 8.0, O.is_ge)
     ts(R("mskw", 0, 64), R("iam", 0, 64), 0.0, O.is_equal)
-    fill(N("cum", 15, 2, 80), 0.0)
-    const("dbo", HD, 1)
-    const("upf", 0, 1)
-    const("cro", 0, 1)
-    const("tab", Z, 1)
-    const("l16f", 3, 9, 4)
-    const("ebs", 9, NS, 6)
-    const("ebs", 0, NS, 6, -BIG)
-    const("ebs", 7, NS, 6, -BIG)
-    act(col(1), p16, float(LP + LW * rank + 16))
-    act(col(3), m8, p16, 32.0)
-    act(col(6), p16, float(8 - 16 * (rank % 2)), 2.0)
-    act(col(5), m8, float(1 - rank % 2), float(2 * (rank % 2) - 1))
-    act(N("tab", C + 64, 64), N("tab", C, 64), float(2 * BW))
-    act(N("tab", C + 128, 32), N("tab", C, 32), float(4 * BW))
-
-    ts(R("s5", 0, 12), R("snd32", 0, 12), float(Z), O.is_ge, -4096.0, O.mult)
-    cp(R("seq16", 0, 28), R("seq32", 0, 28))
-    tt(R("sz", 0, 12), R("snd32", 0, 12), R("s5", 0, 12), O.add)
-    cp(R("rmp", 0, F), X("rmb", C, "seq16", 0, 4))
-    act(R("rmp", F, C), X("rmb", C, "seq16", 4, 28))
-    act(N("tab", 128, 128), N("tab", 0, 128), float(2 * BW))
-    act(N("tab", 256, 64), N("tab", 0, 64), float(4 * BW))
-    ts(R("bx", 0, 12), R("sz", 0, 12), 3.0, O.mult, 2.0, O.add)
-    base(0, "qsb")
-    ix = [lambda v=v, c=c: ts(N("ix", 6 * v + c, 3, 2), N("sz", 2 + c, 3, 4), float(64 * v - 56), O.add) for v in range(U) for c in range(2)]
-    ix[0]()
-    twice(1)
-    ts(R("sb0_0", 0, NS), X("dbo", HD + 192, "bx", 0, 2, HD), 0.0, O.max)
-    message("sb0_0", NS, lambda k: 0, "win0", BASE[0] + slot_at(0) + MW * rank, "arr0_0", FAR)
-
-    cp(R("upr16", 0, 56), R("up32", 0, 56))
-    spread(0)
-    for f in ix[1:]:
-        f()
     ts(R("one", 0, 128), R("iot", 0, 128), 1024.0, O.is_equal)
-    for w in (3, 5, 2, 4, 6):
-        twice(w)
-    base(1, "qsb")
-    ts(R("k16", 0, 28), R("ki", 0, 28), p16, O.add)
-    coef(1)
-    first(0, act)
-    sent_base(0, 1, act)
-    sent_coefs(0, 1)
-    sent_columns(0, 1)
-    ts(fu("uH"), u, 0x3C0, O.bitwise_and)
-    running(0, 1)
-    act(N("pk", LW * mate + MW, NS), R("sb0_0", 0, NS))
-    act(R("mskw", 64, 128), R("mskw", 0, 64))
-    spread(1)
-    spread(2)
-    ts(fu("uL"), u, 0x27, O.bitwise_and)
-    folded(0, 1)
-    ts(fu("ub"), u, 3.0, O.mult)
-    ts(R("a1", 0, 4), R("c12", 0, 4), float(slot_at(0)), O.is_lt, col(1), O.mult)
-    ts(N("k16", 1, 4, 4), R("c12", 0, 4), float(slot_at(0) - 1), O.min, float(BASE[0]), O.add)
-    tt(win(0, 15, 64, 16), R("a1", 0, 4), R("c12", 0, 4), O.max)
-    ts(fu("ua"), fu("uH"), BW / 64 - 3, O.mult, float(own_at(0) + 2), O.add)
-    for j in (2, 0, 1):
-        d = order[j]
-        (act if j == 0 else cp)(N("pk", LW * d, MW), X("win0", BASE[0] + slot_at(0), "k16", 4 * d, 4 * d + 3))
-    message("pk", LW, lambda k: LW * k, "win0", BASE[0] + LP + LW * rank, "pre0", MATE)
-    message("pk", MW, lambda k: LW * k, "win0", BASE[0] + LP + LW * rank, "pre1", FAR)
-    keep(0, 0)
-    act(col(8), col(6), 0.0, col(5))
-    for i in range(3):
-        act(N("s9", 2 * i, 2), N("sz", 4 * i, 2), float(own_at(2 * i) + 2 - 384 * i), 3.0, AF.Relu)
-    act(R("kc", 0, 4), R("c16", 0, 4), col(8), col(5))
-    term_constants(1)
+    const("anew", 0, 128, 1, 1.0)
+    const("dbo", 0, 2, DO)
+    const("pk", PK(0) + 4, NS, 6)
+    const("anew", 0, 8, 16)
+    const("cob", 112, 1)
+    const("sq1", 0, 1)
+    term_constants(1, const)
+    act(col(0), p16, float(LW * rank + NS + 2), 3.0)
+    act(col(1), p16, float(MW * rank + values_at(rank)))
+    act(R("kz", 0, NR), R("zer", 0, NR), col(0))
+    act(col(3), p16, 0.0, 3.0)
+    if rank:
+        act(R("kz", 0, rank), R("kz", 0, rank), -float(LW))
+    act(col(2), p16, NS + 1.0, 6.0)
+    act(col(4), p16, 0.0, 2.0)
+    act(col(5), m8, col(2), LW - 6.0 * CAP)
+    const("win0", 0, 2, 3 * Z + HD + 2)
 
-    sent_columns(1, 2)
-    ts(fu("uf"), fu("uL"), -5.0, O.mult, 8.0 * rank + 40, O.add)
-    running(1, 2)
+    ts(N("zf", 48, 12), N("ls", 56, 12), float(Z), O.is_ge, -4096.0, O.mult)
+    for c in range(1 + turned):
+        ts(N("k0", 4 + c, 2 - turned), N("ls", 56 + (c ^ turned), 2 - turned), 3.0, O.mult, 191.0, O.min)
+    tt(N("vz", 48, 12), N("ls", 56, 12), N("zf", 48, 12), O.add)
+    cp(R("ls16", 0, 96), R("ls", 0, 96))
+    spread(0)
+    removal(1, 2)
+    twice(1)
+    iota(N("tab", F, 4 * F), [[-3, 4 * F]], -HD - 2 - 3 * F)
+    for u in range(U):
+        ts(N("ix", 12 * u, 12), N("vz", 48, 12), float(64 * u - 48), O.add)
+    removal(0, 1, cp)
+    act(N("rs", 0, NS), X("rmp", 2 * F, "ix", 2, 4, F - 16))
+    act(N("sq1", 16, F), X("qsb", C, "seq16", 4, 8))
+
+    beside = lambda d: PK(d) - NF if slots_before(rank, d) else PK(d) + MW
+    outer, inner = sorted((FAR, MATE), key=lambda j: 0 < order[j] < NR - 1)
+    filled = lambda k: slot_at(0) + MW * k + filled_from(k)
+    place = lambda q, d: LP + LW * (q - (q > d)) + NS
+    sent_columns(0, 0)
+    sent_columns(0, 1)
+    base(0, "qsb")
+    fold(0, 64)
+    ts(N("pk", beside(order[outer]) - sent_from(rank), NS), X("dbo", DO + 1, "k0", 4, 6, HD + 2), 0.0, O.max)
+    message("pk", NF, lambda k: beside(order[outer]), "win0", lambda k: filled(rank), "arr0_0", (PLANE,))
+    ts(R("k0", 0, 4), folded(0, 4), -1.0, O.mult)
+    removal(2, 4)
+    act(N("pk", PK(0) + 2, 64, 3), X("dbo", HD + 192, "k0", 0, 4), 0.0, 1.0, AF.Relu)
+    for u in range(U):
+        tt(N("pk", PK(0) + 3 * u, NS, 6), X("cob", 256, "ix", 12 * u + 2, 12 * u + 4, 112), N("rs", 0, NS), O.mult)
+    tt(N("pk", PK(0) + 4, NR, MW), folded(0, 4), R("kz", 0, NR), O.max)
+    tt(N("pk", PK(0) + 1, NS, 6), X("sq1", 16 + F, "ix", 2, 4), N("rs", 0, NS), O.mult)
+    cp(fu("vz"), up)
+    for w in (2, 4):
+        act(N("tab", C + NS * w, NS), N("tab", C, NS), float(LP - ZB))
+    for j in (outer, inner):
+        if j == inner:
+            act(N("pk", beside(order[inner]), NF), N("pk", beside(order[outer]), NF))
+        message("pk", MW + NF, lambda k: PK(k) - NF * slots_before(rank, k), "win0", lambda k: place(rank, k) - NF * slots_before(rank, k),
+                "pre%d" % j, (j,))
+    message("pk", MW, PK, "win0", lambda k: place(rank, k), "pre1", (PLANE,))
+    gconst("ebs", 0, 24, 6, -BIG)
+    gconst("ebs", 7, 24, 6, -BIG)
+
+    act(N("tab", C, NS), N("tab", C, NS), float(-LP), -1.0)
+    act(R("x3", 0, 60), R("vz", 0, 60), float(HD + 2), 3.0)
+    spread(1)
+    act(fu("zf"), fu("vz"), (1 - C - Z) / 2, 1.0, AF.Abs)
+    act(own(0, 0), N("dbo", HD + 2, F, 3), 0.0, 1.0, AF.Relu)
+    act(win(0, filled(rank), filled(rank) + NF), N("pk", beside(order[outer]), NF))
+    twice(3)
+    ts(fu("mq"), up, 0x38, O.bitwise_and)
+    ts(fu("mt"), up, 0x27, O.bitwise_and)
+    ts(fu("e2"), fu("mq"), 32.0, O.is_ge, 44.0, O.mult)
+    ts(fu("e3"), fu("mq"), 32.0 + CAP * rank, O.is_gt, -float(MW), O.mult)
+    added(0, "e2", "e3")
+    twice(2)
+    ts(fu("e1"), fu("mt"), -5.0, O.mult, block(rank ^ 2, rank) + 40.0, O.add)
+    ts(fu("e4"), fu("mq"), float(CAP * twin), O.is_equal, float(block(twin, rank) - block(rank ^ 2, rank)), O.mult)
+    ts(R("bx", 0, 12), N("vz", 48, 12), 3.0, O.mult, float(HD + 2), O.add)
     coef(3)
-    coef(5)
-    folded(1, 2)
-    sent_coefs(1, 2)
-    for i in range(3):
-        act(N("win0", 192 + i, 4, 16), N("c12", 4 * i, 4))
-    ts(fu("ug"), fu("uL"), 32.0, O.is_ge, float(BW + 4 - 192 + 40), O.mult)
-    tt(fu("uc"), fu("ua"), fu("ub"), O.add)
-    tt(fu("uk"), fu("uf"), fu("ug"), O.max)
-    ts(fu("ud"), u, float(C), O.is_lt, float(DROP), O.mult)
-    tt(fu("uh"), fu("uc"), fu("uk"), O.add)
+    for u in range(U):
+        act(N("pq", 2 * u, NS, 4), X("cro", 16 + 256, "ix", 12 * u + 6, 12 * u + 8))
+    const("pq", 1, 64, 4)
+    const("ebs", 9, 24, 6)
+    sent_columns(1, 0)
+    sent_columns(1, 1)
     base(3, "qsb")
-    tt(fu("uj"), fu("uh"), fu("ud"), O.max)
-    landing("win0", LW, lambda k: BASE[0] + LP + LW * k, "pre0", MATE)
-    const("win0", BASE[0] + LP + LW * rank, MW)
-    act(R("pq", 0, NR * MW), X("win0", BASE[0], "k16", 16, 28))
-    message("pq", MW, lambda k: MW * k, "lq", MW * rank, "pre2")
-    act(win(0, slot_at(0) + MW * mate, slot_at(0) + MW * mate + NS), win(0, LP + LW * mate + MW, LP + LW * mate + LW))
-    sent_base(0, 3, act)
-    base(2, "qsb")
-    tt(fu("un"), fu("uc"), fu("uj"), O.add)
-    tt(R("hx", 0, 12), R("c12", 0, 12), R("lim", 0, 12), O.min)
-    tt(fu("uq"), fu("un"), R("limw", 0, 48), O.min)
-    ts(N("k16", 28, 4), N("c16", 0, 4, 5), p16, O.add)
-    ts(R("up16", 8, 56), fu("uq"), float(-DROP), O.add)
-    ts(N("k16", 40, 2), N("c16", 1, 2, 5), col(3), O.add, 2.0, O.mult)
-    for j, d in enumerate(order):
-        for c in range(2):
-            act(N("l16f", 4 * j + c, 3, 12), N("s9", c, 3, 2), N("kc", d, 1) if c == rank // 2 else 0.0)
-    arrival(0, 0, NS, FAR)
-    chain_gather(0, 1)
+    sent_base(N("pq", 3, NS, 4), 3)
+    act(N("kf", 0, 4), N("c16", 0, 4), col(3), LW / 16)
+    act(N("kf", 4, 4), N("c16", 0, 4), col(4), NS / 16)
+    act(N("kf", 8, 2), N("c16", 0, 2), col(5), LW / 8)
+    fold(64, 64)
+    tt(fu("e5"), N("pf", 0, 48), fu("e1"), O.max)
+    added(1536, "e4", "x3", "e5")
+    ts(N("a1", 4, 4), folded(4, 4), 0.5, O.is_lt, col(1), O.mult)
+    ts(fu("gate"), fu("zf"), (Z - C) / 2, O.is_lt)
+    tt(N("pq", 1, NR, NS), N("a1", 4, 4), folded(4, 4), O.max)
+    hand_on(0)
+    term_constants(2, gconst)
+    iota(R("idt", 0, 128), [[1, 128]], 0)
+    coef(1)
+    tt(fu("y2"), N("pf", 1536, 48), fu("gate"), O.mult)
+    mm(N("pf", 48, 10), R("one", 0, 128), R("kf", 0, 10))
+    added(0, "x3", "y2")
+    base(1, "qsb")
     coef(2)
-    landing("win0", MW, lambda k: BASE[0] + LP + LW * k, "pre1", FAR)
-    act(R("ce", 0, 64), pick(0, LP, own_at(1), "k16", 28, 32))
-    ts(R("ex", 12, 16), win(0, LP + 39, own_at(1), LW), float(-slot_at(0)), O.add)
-    chain_scan(0, 1)
+    b2 = halves(2, "qsb")
+    b2[0]()
+    cp(R("up16", 8, 66), N("pf", 0, 58))
+    b2[1]()
+    act(N("tab", C + 2 * NS, NS), N("tab", C + 2 * NS, NS), float(-slot_at(2)), -1.0)
+    act(N("tab", C + 3 * NS, NS), N("tab", C + NS, NS), -384.0)
+    spread(2)
+    landing("win0", NF, filled, "arr0_0", [order[PLANE]])
+    for j in (MATE, FAR):
+        d = order[j]
+        landing("win0", MW + NF, lambda k: place(k, rank) - NF * slots_before(k, rank), "pre%d" % j, [d])
+        act(win(0, filled(d), filled(d) + NF), N("win0", place(d, rank) + (-NF if slots_before(d, rank) else MW), NF))
+    landing("win0", MW, lambda k: place(k, rank), "pre1", [order[PLANE]])
+    act(N("ce", 0, MW), pick(0, LP + NS, ZB, "k16", 0, 3))
+    cp(N("ex", 12, 3), N("win0", LP + NS + 4, 3, LW))
+    chain_gather(0, 1)
     finish_gather(0, 1)
-    for j, d in enumerate(order):
-        act(N("l16f", 4 * j + 2, 3, 12), N("hx", d, 3, 4))
-    term_constants(2)
-    ts(N("k16", 32, 4), N("c16", 0, 4, 3), p16, O.add)
+    sent_lists(1)
+    chain_scan(0, 1)
     finish_scan(0, 1)
-    ts(N("k16", 36, 4), N("c16", 1, 4, 3), p16, O.add)
+    removal(4, 6)
+    twice(5)
+    twice(4)
+    cp(N("l16", 0, 16), N("l16f", 0, 16))
     chain_gather(0, 2)
-    cp(R("l16", 0, 36), R("l16f", 0, 36))
+    b5 = halves(5, "qsb")
+    b5[0]()
     chain_scan(0, 2)
-    cp(R("scf", 0, 16, 1, 16), R("scb", 0, 16, 1, 16))
+    b5[1]()
     send(0, 2)
-    const("lq", MW * rank, MW)
-    iota(N("ki", 28, 12), [[0, 3], [MW, 4]], NS + 1)
-    iota(R("idt", 0, C), [[1, C]], 0)
-    act(col(2), m8, p16, 48.0)
-    landing("lq", MW, lambda k: MW * k, "pre2")
-    for i in range(3):
-        act(N("a12", 4 * i, 4), N("lq", 32 + i, 4, MW), float(1 - slot_at(2 * i)))
-    act(R("ce", 64, 192), X("lq", NR * MW, "k16", 32, 40))
-    term_constants(3)
-    term_constants(4)
-    base(4, "qsb")
-    ts(N("k16", 42, 2), N("c16", 0, 2, 7), col(2), O.add)
-    base(5, "qsb")
+
+    sent_lists(0)
+    sent_base(N("pq", 128 + 3, NS, 4), 5)
+    act(folded(0, 4), folded(0, 4), float(LP - ZB))
+    sent_columns(2, 0)
+    sent_columns(2, 1)
+    coef(5)
+    for u in range(U):
+        act(N("pq", 128 + 2 * u, NS, 4), sent("cro", 2, u))
+    fold(128, 64)
     coef(4)
-    ts(R("hp", 0, 12), R("ki", 28, 40), p16, O.add)
-    ts(R("t1", 0, 12), R("a12", 0, 12), 1.0, O.is_lt)
-    fill(win(1, 0, HD), 0.0)
-    tt(R("em", 0, 12), R("t1", 0, 12), R("hp", 0, 12), O.mult)
-    coef(6)
-    tt(R("e12", 0, 12), R("em", 0, 12), R("a12", 0, 12), O.max)
-    sent_base(0, 5)
-    ts(R("ex", 0, 12), R("e12", 0, 12), -1.0, O.add)
-    to_cells(0, 0)
+    ts(N("a1", 0, 12), folded(0, 12), 0.5, O.is_lt, col(1), O.mult)
+    base(4, "qsb")
+    tt(N("pq", 128 + 5, NR, NS), N("a1", 0, 4), folded(0, 4), O.max)
+    tt(N("pq", 128 + 1, NR, NS), N("a1", 8, 4), folded(8, 4), O.max)
+    hand_on(1)
+    scattered(0, 2)
+    term_constants(3, const)
+    sent_lists(2)
+    removal(6, 7)
+    twice(6)
+    const("psic0", 0, 64)
+    handed(0)
+    act(N("ce", MW, MW), X("lq", 3 * NS, "k16", 4, 7))
+    others_base(3, 4)
+    cp(N("ex", 4, 3), N("lq", 1, 3, NS))
+    act(col(2), m8, p16, -8.0)
+    act(col(6), m8, float(1 - rank % 2), float(2 * (rank % 2) - 1))
+    act(col(7), col(2), 8.0, 2.0)
+    act(col(8), m8, float(rank % 2), float(1 - 2 * (rank % 2)))
+    act(col(9), col(7), 0.0, col(6))
+    const("sq1", 0, 1, 1, float(C))
+    act(col(10), N("x3", 48 + rank // 2, 1), col(9), col(8))
+    const("idw", 0, 1, 1, float(C))
+    act(N("l16f", SENT_AT[0] + block(rank, rank) // 16, NR, 4), R("c16", 0, NR), col(10), col(6))
+    for a, n in ((128, 128), (256, 192)):
+        act(N("idt", a, n), N("idt", 0, n), float(a))
     arrival(0, 2)
 
-    pair(0, 3, halves(6, "qsb") + [lambda: fill(win(1, known_to(1) - 1, WIN, BW), 0.0)])
+    pair(0, 3, [lambda: cp(N("l16", 16, 16), N("l16f", 16, 16)), lambda: coef(6), lambda: cp(N("l16", 32, 16), N("l16f", 32, 16))])
     send(0, 4)
-    term_constants(5)
-    const("sq1", 0, 1, 1, float(C))
-    act(N("sq1", 8, F), X("idt", C, "seq16", 4, 8))
-    act(R("rs1", 0, NS), X("rmp", 2 * F, "ix", 0, 2, F - 8))
-    const("src", C, 8)
-    const("floor", 0, MW)
-    const("psic0", C, 64)
-    const("psic1", C, 64)
-    const("floor", 8 * rank, 8, 1, -BIG)
-    mm(R("pf", 0, 16), R("mskw", 0, 128, 1, 16), R("scf", 0, 16, 1, 16))
+    iota(R("oc", 0, C), [[3, C]], HD + 2)
+    act(R("mskw", 64, 128), R("mskw", 0, 64))
+    act(R("scf", 0, 16, 1, 16), R("scb", 0, 16, 1, 16))
     for i in range(8):
-        act(R("screp", 16 * i, 16 * i + 16), R("pf", 0, 16))
-    to_cells(0, 1)
-    fill(R("dbo", 0, 8), 0.0)
-    to_cells(0, 2)
-    tt(R("fo", 0, NS), X("sq1", 8 + F, "ix", 0, 2), R("mskw", 0, NS), O.mult)
-    to_cells(0, 3)
-    scan(N("cum", 16, NS), R("fo", 0, NS), R("fo", 0, NS))
-    to_cells(0, 4)
+        mm(N("pf", 16 * i, 16), R("mskw", 0, 128, 1, 16), R("scf", 0, 16, 1, 16))
+    act(N("sq1", 16, F), X("idt", C, "seq16", 4, 8))
+    act(N("idw", HD + 2, F, 3), X("idt", C, "seq16", 0, 4))
+    act(N("idw", 8, NS, 2), X("sq1", 16 + F, "ix", 2, 4))
+    term_constants(5, const)
+    const("floor", 0, MW)
+    const("win1", 0, 2, 3 * Z + HD + 2)
+    const("src", C, 8)
+    const("floor", block(rank, rank), CAP, 1, -BIG)
+    at = [float(MW * k + block(k, k)) for k in others]
+    act(col(11), m8, col(2), at[1] - at[0])
+    act(folded(13, 1), col(2), at[2])
+    act(folded(12, 1), col(11), at[0])
+    scattered(2, 3)
+    base(6, "qsb")
+    for j, d in enumerate(order):
+        tt(N("fo", 64 * j, MW), X("idw", HD + 192, "l16", SENT_AT[0] + 4 * d, SENT_AT[0] + 4 * d + 3), R("mskw", 0, MW), O.mult)
+    handed(1)
+    act(N("ce", 2 * MW, MW), X("lq", 6 * NS, "k16", 4, 7, 3 * NS))
+    others_base(3 * NS + 3, 4)
+    cp(N("ex", 8, 3), N("lq", 3 * NS + 1, 3, NS))
+    act(R("screp", 0, 128), R("pf", 0, 128))
     arrival(0, 4)
-    pair(0, 5, [lambda: tt(R("c12", 0, 2), N("cum", 31, 2, 16), N("cum", 15, 2, 16), O.subtract), lambda: to_cells(0, 5),
-                lambda: cp(R("sl1", 0, 2), R("c12", 0, 2))])
-    to_cells(0, 6)
+    pair(0, 5, [lambda: fold(0, 96), lambda: scattered(5), lambda: fold(96, 96)])
+    scattered(6)
+    cp(R("lc", 0, 14), folded(0, 14))
 
-    blocks = ((0, 256), (256, 128), (384, 64))
+    blocks = ((0, 192), (192, 128), (320, 64), (384, 64))
     for i, (a, n) in enumerate(blocks):
-        mm(N("ps", 512 * i, n), R("screp", 0, 128), N("psic0", a, n))
+        mm(N("ps", 512 * i, n), R("screp", 0, 128), N("psic0", 64 + a, n))
     for i, (a, n) in enumerate(blocks):
-        (cp if i == 2 else act)(N("src", a, n), N("ps", 512 * i, n))
-    base(0, "src")
-    tt(N("dbo", 8, NS, 2), X("src", C + 8, "sl1", 0, 2), R("rs1", 0, NS), O.mult)
+        tt(N("src", a, n), N("ps", 512 * i, n), N("rmb", a, n), O.mult)
+    cp(N("ex", 0, 3), N("lq", 3 * NS + 5, 3, NS))
     send(1, 0)
     for j in range(4):
-        flux(0, j, True, False)
-    first(1)
+        flux(0, j)
+    ts(own(1, 0), X("src", C, "seq16", 0, 4), 0.0, O.max)
+    base(3, "src", 0, F, act)
     base(1, "src")
-    base(3, "src")
+    sent_base(N("pq", LATER[2][1], NS), 3)
+    hand_on(2)
     base(2, "src")
-    sent_base(1, 3)
-    b5 = halves(5, "src")
-    b5[0]()
-    to_cells(1, 0)
+    act(N("ps", 0, 128), R("mskw", 0, 128))
+    const("invs", C, 64)
+    inverse(0, 3)
     arrival(1, 0)
 
-    for x in (1, 3):
-        pair(1, x, halves(x + 3, "src") + [b5[1] if x == 1 else lambda: None])
-        send(1, x + 1)
-        if x == 1:
-            sent_base(1, 5)
-        to_cells(1, x)
-        to_cells(1, x + 1)
-        arrival(1, x + 1)
-    pair(1, 5, [lambda: None, lambda: to_cells(1, 5), lambda: None])
-    to_cells(1, 6)
+    pair(1, 1, halves(5, "src") + [lambda: sent_base(N("pq", LATER[3][1], NS), 5, cp)])
+    send(1, 2)
+    hand_on(3)
+    base(4, "src", 0, F, act)
+    inverse(3, W)
+    for j in range(2):
+        inverse_masked(j)
+    handed(2)
+    others_base(LATER[2][3], 1)
+    arrival(1, 2)
+    pair(1, 3, [lambda a=a: fold(a, 64) for a in (0, 64, 128)])
+    send(1, 4)
+    base(6, "src", 0, F, act)
+    for j in range(2, 4):
+        inverse_masked(j)
+    fold(192, 128)
+    fold(320, 128)
+    cp(R("iv", 0, 16), folded(0, 16))
+    handed(3)
+    others_base(LATER[3][3], 1)
+    arrival(1, 4)
+    pair(1, 5, [lambda: fold(448, 64), lambda: cp(N("iv", 16, 16), folded(16, 16)), lambda: fill("psic1", 0, 16)])
 
     for j in range(4):
-        flux(1, j, False, True)
+        gathered(j, act if j % 2 else cp)
+    for j in range(4):
+        flux(1, j)
     for j in range(4):
         turn(N("yo", j, 32, 4), N("pf", 512 * j, 32))
     for k in range(4):
-        a, b = 128 * k, min(C, 128 * k + 128)
+        a, b = max(0, 128 * k - 64), 128 * k + 64
         q = "y" if k % 2 == 1 else "s"
-        add_op(q, lambda q=q, a=a, b=b, k=k: queues[q].dma_start(T.y[:, a:b], T.yo[32 * k:32 * k + 16, 0:b - a]),
+        add_op(q, lambda q=q, a=a, b=b, k=k: queues[q].dma_start(T.y[:, a:b], T.yo[32 * k:32 * k + 16, 128 - (b - a):128]),
                [[("yo", 0, 128, 1)]], [[("y", a, b, 1)]], "dma", 16)
 
     emit(g, T, queues, ops)
@@ -559,10 +682,14 @@ def meets(x, y, same):
         return x[1] // 512 <= (y[2] - 1) // 512 and y[1] // 512 <= (x[2] - 1) // 512
     if x[0] != y[0] or x[1] >= y[2] or y[1] >= x[2]:
         return False
+    if x[3] == 1 and y[3] == 1:
+        return True
     return not set(range(x[1], x[2], x[3])).isdisjoint(range(y[1], y[2], y[3]))
 
 
 def clash(a, b):
+    if a["q"] == "t" and b.get("opens"):
+        return False
     for x in a["w"]:
         for y in b["r"] + b["w"]:
             if meets(x, y, a["q"] == b["q"]):

from concourse.mybir import AluOpType as O, ActivationFunctionType as AF

W, F, U, CAP, SW, NR = 7, 64, 2, 8, 2, 4
C = W * F
Z = C + (W - 1) * NR * CAP
NS = NR * CAP
NF = NS - CAP
MW = 48
MS = MW - CAP
LW = MW + 2 * NS
HD = 70
ZB = 2 * HD + 6 * C + 44
WIN = ZB + 192 * (W - 1)
LP = ZB - 3 * LW - 80
DB = 384
DO = HD + 193
BIG = 9.0e29
CB = C // 4
KQ = {"v": 16, "s": 12, "t": 2, "g": 2}
NXS = 90
FAR, PLANE, MATE = 0, 1, 2
SENDS = [(s, w) for s in range(SW) for w in (0, 2, 4)]
LATER = (("pre3", 0, NS, 0), ("pre4", 128, NS, 96), ("pre5", 256, CAP, 192), ("pre6", 288, CAP, 216))
SENT_AT = (32, 0, 16)


def block(q, d):
    return 16 * (q % 2) + CAP * ((d + 2 * (0 < q < NR - 1)) % NR)


def values_at(q):
    return NS * (1 - q % 2)


def sent_from(q):
    return CAP * (1 - q % 2)


def filled_from(q):
    return CAP + CAP * (q % 2)


def slots_before(q, d):
    return d == 0 or d == q + 1 < NR - 1


def own_at(w):
    return HD + 192 * w


def slot_at(w):
    return ZB + 192 * w


def f32(n):
    return ("sbuf", [128, n], "float32")


def i32(n):
    return ("sbuf", [128, n], "int32")


def u16(n):
    return ("sbuf", [128, n], "uint16")


SCRATCH = {
    "ls": i32(96), "ls16": u16(96), "up16": u16(66),
    "qsb": ("sbuf", [128, C], "bfloat16"), "rmb": ("sbuf", [128, C], "bfloat16"), "cob": ("sbuf", [128, 2 * C], "bfloat16"),
    "scb": ("sbuf", [128, 16], "bfloat16"), "scf": f32(16),
    "rmp": f32(C), "cre": f32(384), "win0": f32(WIN), "win1": f32(WIN),
    "psic0": f32(64 + C), "psic1": f32(16 + C), "src": f32(C + 8), "dbo": f32(DO + 3 * DB), "dbe": f32(DB + 1), "ebs": f32(200),
    "tab": f32(Z + 3 * 400), "zer": f32(128), "one": f32(128), "iot": i32(128), "iam": i32(64), "mskw": f32(128),
    "pi": i32(2), "pb": i32(2), "p16": f32(2), "c16": f32(16), "col": f32(12), "kz": f32(4), "kf": f32(10),
    "zf": f32(60), "vz": f32(60), "x3": f32(60), "mt": i32(48), "mq": i32(48), "anew": f32(128),
    "l16f": f32(48), "l16": u16(48), "ix": u16(24), "bx": u16(12), "k0": u16(6),
    "fo": f32(512), "cum": f32(512), "a1": f32(12),
    "pk": f32(NR * MW + 2 * NS), "pq": f32(10 * NS), "lq": f32(240), "rs": f32(NS), "ex": u16(16), "ce": f32(3 * MW),
    "screp": f32(128), "yo": f32(128), "idt": f32(C), "oc": f32(C), "invs": f32(512), "iv": u16(32),
    "sq1": f32(16 + F), "idw": f32(HD + 192), "lc": u16(14), "floor": f32(MW),
    "ps": ("psum", [128, 2048], "float32"), "pf": ("psum", [128, 2048], "float32"),
}
for _n in ("e1", "e2", "e3", "e4", "e5", "gate", "y2"):
    SCRATCH[_n] = f32(48)
for _k in SENDS[1:]:
    SCRATCH["sb%d_%d" % _k] = f32(3 * MW)
SEMAPHORES = (["x%d" % i for i in range(NXS)] + ["arr%d_%d" % k for k in SENDS] + ["pre%d" % i for i in range(7)]
              + ["q_%s%d" % (q, i) for q in KQ for i in range(KQ[q])] + ["sent"])
PSUM = ("ps", "pf")
PART = {"upf": ("tab", Z + 400), "cro": ("tab", Z + 800),
        "upr16": ("ls16", 0), "seq16": ("ls16", 68), "k16": ("up16", 56)}


def send_order(topo, src, dests):
    a = topo.chip(src)
    return sorted(dests, key=lambda d: (topo.mates(a, topo.chip(d)), topo.same_plane(a, topo.chip(d))))


def helper_of(topo, cores, src):
    far = [c for c in cores if c != src]
    h = [c for c in topo.cores_of(src) if c not in cores and topo.die(c) == topo.die(src) and all(topo.may_write(c, d) for d in far)][0]
    return h, [e for e in topo.engines(src, h) if e not in topo.engines(src, far[0])]


def helper_program(g, core, src, T, topo):
    cores, rank = list(T.cores), T.rank_of(src)
    order = send_order(topo, src, [c for c in cores if c != src])
    for sem, a0, n, b0 in LATER:
        g.wait_ge(T.sem[sem], len(helper_of(topo, cores, src)[1]))
        for d in order:
            k, (rid, pid) = T.rank_of(d), topo.addr(d)[:2]
            a, b = a0 + n * k, b0 + n * (rank - (rank > k))
            g.remote_dma(out_ap=T.lq[:, b:b + n], in_ap=T.pq[:, a:a + n], remote_sem=T.sem[sem], local_sem=T.sem["sent"], pid=pid,
                         routing_id=rid, dma_engine_mask=topo.mask(core, d))
    g.wait_ge(T.sem["sent"], len(LATER) * sum(len(topo.engines(core, d)) for d in order))


def rank_program(g, core, T, topo):
    rank = T.rank_of(core)
    cores = list(T.cores)
    if rank is None:
        for c in cores:
            if helper_of(topo, cores, c)[0] == core:
                helper_program(g, core, c, T, topo)
        return
    order = [T.rank_of(d) for d in send_order(topo, core, [c for c in cores if c != core])]
    others = sorted(order)
    queues = {"v": g.vector, "s": g.scalar, "t": g.tensor, "g": g, "y": g.sync}
    ops = []

    def reg(name, a, b, step=1):
        return (name, a, b, step)

    def part(name, a, b):
        name, at = PART.get(name, (name, 0))
        return name, a + at, b + at

    def R(name, a, b, step=1, p=128):
        name, a, b = part(name, a, b)
        t = T[name]
        ap = t[0:p, a:b] if step == 1 else t[0:p, a:b:step]
        return (ap, [reg(name, a, b, step)])

    def N(name, a, n, step=1):
        return R(name, a, a + step * (n - 1) + 1, step if n > 1 else 1)

    def X(name, b, off, oa, ob, a=0):
        name, a, b = part(name, a, b)
        off, oa, ob = part(off, oa, ob)
        return (T[name][:, a:b].indirect(T[off][:, oa:ob]), [reg(name, a, b), reg(off, oa, ob)])

    def K(x):
        return x if isinstance(x, tuple) else (x, [])

    def add_op(q, fn, reads, writes, kind="c", n=1, sem=None):
        rd, wr = [], []
        for x in reads:
            rd += x
        for x in writes:
            wr += x
        ops.append({"q": q, "fn": fn, "r": rd, "w": wr, "kind": kind, "n": n, "sem": sem})

    def split(out):
        return [out[1][0:1]], [out[1][1:]]

    def tt(out, a, b, op):
        w, r = split(out)
        add_op("v", lambda: g.vector.tensor_tensor(out=out[0], in0=a[0], in1=b[0], op=op), [a[1], b[1]] + r, w)

    def ts(out, a, s1, op0, s2=None, op1=None):
        k1, k2 = K(s1), K(s2)
        if op1 is None:
            add_op("v", lambda: g.vector.tensor_scalar(out=out[0], in0=a[0], scalar1=k1[0], scalar2=None, op0=op0), [a[1], k1[1]], [out[1]])
        else:
            add_op("v", lambda: g.vector.tensor_scalar(out=out[0], in0=a[0], scalar1=k1[0], scalar2=k2[0], op0=op0, op1=op1),
                   [a[1], k1[1], k2[1]], [out[1]])

    def cp(out, a):
        w, r = split(out)
        add_op("v", lambda: g.vector.tensor_copy(out=out[0], in_=a[0]), [a[1]] + r, w)

    def fill(name, a, n, step=1, v=0.0):
        out = N(name, a, n, step)
        add_op("v", lambda: g.vector.memset(out[0], v), [], [out[1]])

    def scan(out, d0, d1, first=0.0, op0=O.add, op1=O.max):
        add_op("v", lambda: g.vector.tensor_tensor_scan(out=out[0], data0=d0[0], data1=d1[0], initial=first, op0=op0, op1=op1),
               [d0[1], d1[1]], [out[1]])

    def act(out, a, bias=0.0, scale=1.0, func=AF.Identity):
        kb, ks = K(bias), K(scale)
        add_op("s", lambda: g.scalar.activation(out=out[0], in_=a[0], func=func, bias=kb[0], scale=ks[0]), [a[1], kb[1], ks[1]], [out[1]])

    def const(name, a, n, step=1, v=0.0):
        act(N(name, a, n, step), R("zer", 0, n), v)

    def mm(out, lhsT, rhs, start=True, stop=True):
        add_op("t", lambda: g.tensor.matmul(out=out[0], lhsT=lhsT[0], rhs=rhs[0], start=start, stop=stop), [lhsT[1], rhs[1]], [out[1]])
        ops[-1]["opens"] = not stop

    def turn(out, a):
        add_op("v", lambda: g.vector.transpose(out=out[0], in_=a[0]), [a[1]], [out[1]])

    def load(q, name, src, p=128, a=0, b=None, at=0):
        b = b or SCRATCH[name][1][1]
        o = R(name, at + a, at + b, 1, p)
        add_op(q, lambda: queues[q].dma_start(o[0], src[:, a:b]), [], [o[1]], "dma", 16)

    def iota(out, pattern, base, cm=0):
        if SCRATCH[out[1][0][0]][2] == "float32":
            add_op("g", lambda: g.iota(out[0], pattern, base, cm, allow_small_or_imprecise_dtypes=True), [], [out[1]])
        else:
            add_op("g", lambda: g.iota(out[0], pattern, base, cm), [], [out[1]])

    def gconst(name, a, n, step=1, v=0.0):
        o, z = N(name, a, n, step), R("zer", 0, n)
        if v == 0.0:
            iota(o, [[0, n]], 0)
        else:
            add_op("g", lambda: g.affine_select(o[0], z[0], [[0, n]], O.is_gt, v, 0, 0), [z[1]], [o[1]])

    def message(sb, width, src_at, dst, dst_at, sem, which=(FAR, PLANE, MATE)):
        for k in [order[j] for j in which]:
            rid, pid = topo.addr(cores[k])[:2]
            add_op("g", lambda k=k, rid=rid, pid=pid: g.remote_dma(
                out_ap=T[dst][:, dst_at(k):dst_at(k) + width], in_ap=T[sb][:, src_at(k):src_at(k) + width], remote_sem=T.sem[sem],
                local_sem=T.sem["sent"], pid=pid, routing_id=rid, dma_engine_mask=topo.mask(core, cores[k])),
                [[reg(sb, src_at(k), src_at(k) + width)]], [], "remote", len(topo.engines(core, cores[k])))

    def landing(dst, width, at, sem, senders=others):
        add_op("ext", None, [], [[reg(dst, at(k), at(k) + width) for k in senders]], "ext", sum(len(topo.engines(cores[k], core)) for k in senders), sem)

    def hand_on(i):
        h, engines = helper_of(topo, cores, core)
        rid, pid = topo.addr(h)[:2]
        a = N("pq", LATER[i][1], NR * LATER[i][2])
        add_op("g", lambda: g.remote_dma(out_ap=a[0], in_ap=a[0], remote_sem=T.sem[LATER[i][0]], local_sem=T.sem["sent"], pid=pid,
                                         routing_id=rid, dma_engine_mask=sum(1 << e for e in engines)), [a[1]], [], "remote", len(engines))

    def handed(i):
        landing("lq", LATER[i][2], lambda k: LATER[i][3] + LATER[i][2] * others.index(k), LATER[i][0])

    def win(s, a, b, step=1):
        return R("win%d" % s, a, b, step)

    def pick(s, a, b, off, oa, ob):
        return X("win%d" % s, b, off, oa, ob, a)

    def send(s, w):
        sb, i, a = "sb%d_%d" % (s, w), SENT_AT[w // 2], sent_from(rank) if w else 0
        for j, d in enumerate(order):
            if w:
                (act if j == 1 else cp)(N(sb, MW * j, MW), pick(s, 0, slot_at(w), "l16", i + 4 * d, i + 4 * d + 3))
            else:
                tt(N(sb, MW * j, MW), X("src", C + 8, "lc", 4 * j, 4 * j + 3), R("floor", 0, MW), O.max)
        message(sb, MS if w else MW, lambda k: MW * order.index(k) + a, "win%d" % s, lambda k: slot_at(w) + MW * rank + a, "arr%d_%d" % (s, w))
        b = slot_at(w) + MW * rank + filled_from(rank)
        act(win(s, b, b + NF), N(sb, filled_from(rank), NF))

    def arrival(s, w):
        landing("win%d" % s, MS if w else MW, lambda k: slot_at(w) + MW * k + (sent_from(k) if w else 0), "arr%d_%d" % (s, w))

    def own(s, w, n=1):
        return win(s, own_at(w) + 2, own_at(w + n), 3)

    def terms(w):
        return ("dbo", DO + DB * (w // 2)) if w % 2 else ("dbe", 1)

    def coefs(w):
        return N("cro", 16 + 128 * (w // 2), 128) if w % 2 else N("cre", 64 * w - 128, 128)

    def term_constants(w, make):
        d, a = terms(w)
        make(d, a - 1, 64, 3, -BIG) if w < 3 else make(d, a + 2, 63, 3, -BIG)
        make(d, a + 193, 64, 3, -BIG)
        make(d, a + 194, 64, 3)

    def chain_gather(s, w):
        d, a = terms(w)
        tt(N(d, a, 128, 3), pick(s, 0, slot_at(w), "up16", 8 * w, 8 * w + 8), coefs(w), O.mult)

    def chain_scan(s, w):
        d, a = terms(w)
        scan(win(s, own_at(w), own_at(w) + 192), N(d, a - 1, 192), N(d, a + 192, 192), -BIG)

    def finish_gather(s, x):
        w, i = x - 1, x // 2
        if (s, x) == (0, 1):
            act(N("ebs", 4, NS, 6), pick(0, LP, ZB, "k16", 8, 10))
            a = pick(0, LP, slot_at(1), "ex", 12, 15)
        else:
            if x == 1:
                act(N("ebs", 4, NS, 6), pick(s, slot_at(w), slot_at(x), "lc", 12, 14))
            a = pick(s, slot_at(w), slot_at(x), "ex", 4 * i, 4 * i + 3)
        tt(N("ebs", 2, MW, 3), a, N("ce", MW * i, MW), O.mult)

    def others_base(at, step):
        act(N("ebs", 4, NF, 6), N("lq", at, NF, step))

    def finish_scan(s, x):
        scan(win(s, slot_at(x), slot_at(x) + 143, 2), N("ebs", 0, 72, 2), N("ebs", 5, 72, 2))

    def sent_base(out, x, by=act):
        by(out, X("dbo", terms(x)[1] + 192, "bx", 2 * x, 2 * x + 2))

    def base(w, src, k=0, n=F, by=cp):
        d, a = terms(w) if w else ("dbo", HD + 1)
        o, x = N(d, a + 1 + 3 * k, n, 3), X(src, C, "seq16", 4 * w + k // 16, 4 * w + (k + n) // 16)
        if src == "src":
            by(o, x)
        else:
            tt(o, x, N("rmp", F * w + k, n), O.mult)

    def halves(w, src):
        return [lambda: base(w, src, 0, F // 2), lambda: base(w, src, F // 2, F // 2)]

    def removal(a, b, by=act):
        by(R("rmp", F * a, F * b), X("rmb", C, "seq16", 4 * a, 4 * b))

    def twice_at(w):
        return ("ps", 512 * (w - 1)) if w < 5 else ("pf", 512 * (w - 4))

    def twice(w):
        p, a = twice_at(w)
        for u in range(U):
            mm(N(p, a + 64 * u, F), R("one", 0, 128), N("rmp", F * w, F))

    def added(at, *names):
        for a in names:
            mm(N("pf", at, 48), R("one", 0, 128), R(a, 0, 48), a == names[0], a == names[-1])

    def coef(w):
        tt(coefs(w), N("cob", 128 * w, 128), N(*twice_at(w), 128), O.mult)

    def spread(i):
        act(N("upf", 16 + 128 * i, 128), X("tab", Z + 8, "upr16", 16 * i + 8, 16 * i + 16))

    def sent(name, i, u):
        return X(name, 16 + 128 * (i + 1), "ix", 12 * u + 4 * i + 2, 12 * u + 4 * i + 4)

    def sent_columns(i, u):
        tt(N("fo", 64 * i + u, NS, 2), sent("upf", i, u), N("mskw", u, NS, 2), O.mult)

    def fold(a, n):
        scan(N("cum", a, n), N("anew", 0, n), N("fo", a, n), 0.0, O.mult, O.add)

    def folded(a, n):
        return N("cum", 16 * a + 15, n, 16)

    def sent_lists(i):
        for c in range(2):
            act(N("l16f", SENT_AT[i] + rank % 2 + (c ^ turned), NR, 4), R("zer", 0, NR), N("x3", 48 + 4 * i + c, 1))
        act(N("l16f", SENT_AT[i] + values_at(rank) // 16, NR, 4), folded(4 * i, NR), 0.0, -1.0)

    def scattered(w, n=1):
        cp(X("psic0", 64 + C, "seq16", 4 * w, 4 * (w + n), 64), own(0, w, n))

    def gathered(j, by):
        by(N("psic1", 16 + CB * j, CB), pick(1, 0, own_at(W), "iv", 8 * j, 8 * j + CB // 16))

    def flux(s, j):
        mm(N("pf", 512 * j, 32), N("psic1", CB * j, 128) if s else N("psic0", j, 128, 4), R("mskw", 0, 32), s == 0, s == 1)

    def inverse(a, b):
        cp(X("invs", C, "seq16", 4 * a, 4 * b), R("oc", F * a, F * b))

    def inverse_masked(j):
        tt(N("fo", 128 * j, 128), N("invs", j, 128, 4), N("ps", 0, 128), O.mult)

    def pair(s, x, meanwhile):
        chain_gather(s, x)
        finish_gather(s, x)
        chain_scan(s, x)
        finish_scan(s, x)
        meanwhile[0]()
        chain_gather(s, x + 1)
        meanwhile[1]()
        chain_scan(s, x + 1)
        meanwhile[2]()

    col = lambda k: N("col", k, 1)
    p16, m8 = N("p16", 0, 1), N("p16", 1, 1)
    fu = lambda n: R(n, 0, 48)
    PK = lambda d: NS + MW * d
    up = R("ls", 8, 56)
    twin = rank ^ 1
    turned = int(0 < rank < NR - 1)

    load("y", "ls", T.seq, 128, 0, 28, 68)
    load("s", "ls", T.snd, 128, 0, 12, 56)
    load("y", "scb", T.sc, 16)
    load("s", "ls", T.up, 128, 0, 56)
    load("y", "rmb", T.rm)
    load("y", "qsb", T.qs)
    load("y", "cob", T.co, 128, 128, 256)
    load("y", "cob", T.co, 128, 256)
    iota(R("pi", 0, 2), [[0, 2]], 0, 1)
    iota(R("iot", 0, 128), [[1, 128]], 1024, -1)
    iota(N("tab", C, NS), [[MW, NR], [1, CAP]], ZB - LP + block(rank ^ 2, rank))
    iota(N("tab", C + CAP * twin, CAP), [[1, CAP]], ZB - LP + MW * twin + block(twin, rank))
    iota(N("tab", 0, F), [[-3, F]], -HD - 2)
    for a, b, k in ((0, rank + 1, 0), (rank + 1, NR, rank)) if turned else ((0, NR, -(rank == 0)),):
        iota(N("tab", C + NS + CAP * a, CAP * (b - a)), [[-6, CAP * (b - a)]], -slot_at(1) - 4 - MW * k)
    iota(R("c16", 0, 16), [[16, 16]], 0)
    gconst("win0", LP + 3 * LW + NS + 1, CAP, 6)
    gconst("l16f", 3, 12, 4)
    fill("zer", 0, 128)
    ts(N("pb", 0, 1), N("pi", 0, 1), 15, O.bitwise_and)
    fill("tab", Z, 3, 400)
    cp(p16, N("pb", 0, 1))
    ts(R("iam", 0, 64), R("iot", 0, 64), 15, O.bitwise_and)
    ts(m8, p16, 8.0, O.is_ge)
    ts(R("mskw", 0, 64), R("iam", 0, 64), 0.0, O.is_equal)
    ts(R("one", 0, 128), R("iot", 0, 128), 1024.0, O.is_equal)
    const("anew", 0, 128, 1, 1.0)
    const("dbo", 0, 2, DO)
    const("pk", PK(0) + 4, NS, 6)
    const("anew", 0, 8, 16)
    const("cob", 112, 1)
    const("sq1", 0, 1)
    term_constants(1, const)
    act(col(0), p16, float(LW * rank + NS + 2), 3.0)
    act(col(1), p16, float(MW * rank + values_at(rank)))
    act(R("kz", 0, NR), R("zer", 0, NR), col(0))
    act(col(3), p16, 0.0, 3.0)
    if rank:
        act(R("kz", 0, rank), R("kz", 0, rank), -float(LW))
    act(col(2), p16, NS + 1.0, 6.0)
    act(col(4), p16, 0.0, 2.0)
    act(col(5), m8, col(2), LW - 6.0 * CAP)
    const("win0", 0, 2, 3 * Z + HD + 2)

    ts(N("zf", 48, 12), N("ls", 56, 12), float(Z), O.is_ge, -4096.0, O.mult)
    for c in range(1 + turned):
        ts(N("k0", 4 + c, 2 - turned), N("ls", 56 + (c ^ turned), 2 - turned), 3.0, O.mult, 191.0, O.min)
    tt(N("vz", 48, 12), N("ls", 56, 12), N("zf", 48, 12), O.add)
    cp(R("ls16", 0, 96), R("ls", 0, 96))
    spread(0)
    removal(1, 2)
    twice(1)
    iota(N("tab", F, 4 * F), [[-3, 4 * F]], -HD - 2 - 3 * F)
    for u in range(U):
        ts(N("ix", 12 * u, 12), N("vz", 48, 12), float(64 * u - 48), O.add)
    removal(0, 1, cp)
    act(N("rs", 0, NS), X("rmp", 2 * F, "ix", 2, 4, F - 16))
    act(N("sq1", 16, F), X("qsb", C, "seq16", 4, 8))

    beside = lambda d: PK(d) - NF if slots_before(rank, d) else PK(d) + MW
    outer, inner = sorted((FAR, MATE), key=lambda j: 0 < order[j] < NR - 1)
    filled = lambda k: slot_at(0) + MW * k + filled_from(k)
    place = lambda q, d: LP + LW * (q - (q > d)) + NS
    sent_columns(0, 0)
    sent_columns(0, 1)
    base(0, "qsb")
    fold(0, 64)
    ts(N("pk", beside(order[outer]) - sent_from(rank), NS), X("dbo", DO + 1, "k0", 4, 6, HD + 2), 0.0, O.max)
    message("pk", NF, lambda k: beside(order[outer]), "win0", lambda k: filled(rank), "arr0_0", (PLANE,))
    ts(R("k0", 0, 4), folded(0, 4), -1.0, O.mult)
    removal(2, 4)
    act(N("pk", PK(0) + 2, 64, 3), X("dbo", HD + 192, "k0", 0, 4), 0.0, 1.0, AF.Relu)
    for u in range(U):
        tt(N("pk", PK(0) + 3 * u, NS, 6), X("cob", 256, "ix", 12 * u + 2, 12 * u + 4, 112), N("rs", 0, NS), O.mult)
    tt(N("pk", PK(0) + 4, NR, MW), folded(0, 4), R("kz", 0, NR), O.max)
    tt(N("pk", PK(0) + 1, NS, 6), X("sq1", 16 + F, "ix", 2, 4), N("rs", 0, NS), O.mult)
    cp(fu("vz"), up)
    for w in (2, 4):
        act(N("tab", C + NS * w, NS), N("tab", C, NS), float(LP - ZB))
    for j in (outer, inner):
        if j == inner:
            act(N("pk", beside(order[inner]), NF), N("pk", beside(order[outer]), NF))
        message("pk", MW + NF, lambda k: PK(k) - NF * slots_before(rank, k), "win0", lambda k: place(rank, k) - NF * slots_before(rank, k),
                "pre%d" % j, (j,))
    message("pk", MW, PK, "win0", lambda k: place(rank, k), "pre1", (PLANE,))
    gconst("ebs", 0, 24, 6, -BIG)
    gconst("ebs", 7, 24, 6, -BIG)

    act(N("tab", C, NS), N("tab", C, NS), float(-LP), -1.0)
    act(R("x3", 0, 60), R("vz", 0, 60), float(HD + 2), 3.0)
    spread(1)
    act(fu("zf"), fu("vz"), (1 - C - Z) / 2, 1.0, AF.Abs)
    act(own(0, 0), N("dbo", HD + 2, F, 3), 0.0, 1.0, AF.Relu)
    act(win(0, filled(rank), filled(rank) + NF), N("pk", beside(order[outer]), NF))
    twice(3)
    ts(fu("mq"), up, 0x38, O.bitwise_and)
    ts(fu("mt"), up, 0x27, O.bitwise_and)
    ts(fu("e2"), fu("mq"), 32.0, O.is_ge, 44.0, O.mult)
    ts(fu("e3"), fu("mq"), 32.0 + CAP * rank, O.is_gt, -float(MW), O.mult)
    added(0, "e2", "e3")
    twice(2)
    ts(fu("e1"), fu("mt"), -5.0, O.mult, block(rank ^ 2, rank) + 40.0, O.add)
    ts(fu("e4"), fu("mq"), float(CAP * twin), O.is_equal, float(block(twin, rank) - block(rank ^ 2, rank)), O.mult)
    ts(R("bx", 0, 12), N("vz", 48, 12), 3.0, O.mult, float(HD + 2), O.add)
    coef(3)
    for u in range(U):
        act(N("pq", 2 * u, NS, 4), X("cro", 16 + 256, "ix", 12 * u + 6, 12 * u + 8))
    const("pq", 1, 64, 4)
    const("ebs", 9, 24, 6)
    sent_columns(1, 0)
    sent_columns(1, 1)
    base(3, "qsb")
    sent_base(N("pq", 3, NS, 4), 3)
    act(N("kf", 0, 4), N("c16", 0, 4), col(3), LW / 16)
    act(N("kf", 4, 4), N("c16", 0, 4), col(4), NS / 16)
    act(N("kf", 8, 2), N("c16", 0, 2), col(5), LW / 8)
    fold(64, 64)
    tt(fu("e5"), N("pf", 0, 48), fu("e1"), O.max)
    added(1536, "e4", "x3", "e5")
    ts(N("a1", 4, 4), folded(4, 4), 0.5, O.is_lt, col(1), O.mult)
    ts(fu("gate"), fu("zf"), (Z - C) / 2, O.is_lt)
    tt(N("pq", 1, NR, NS), N("a1", 4, 4), folded(4, 4), O.max)
    hand_on(0)
    term_constants(2, gconst)
    iota(R("idt", 0, 128), [[1, 128]], 0)
    coef(1)
    tt(fu("y2"), N("pf", 1536, 48), fu("gate"), O.mult)
    mm(N("pf", 48, 10), R("one", 0, 128), R("kf", 0, 10))
    added(0, "x3", "y2")
    base(1, "qsb")
    coef(2)
    b2 = halves(2, "qsb")
    b2[0]()
    cp(R("up16", 8, 66), N("pf", 0, 58))
    b2[1]()
    act(N("tab", C + 2 * NS, NS), N("tab", C + 2 * NS, NS), float(-slot_at(2)), -1.0)
    act(N("tab", C + 3 * NS, NS), N("tab", C + NS, NS), -384.0)
    spread(2)
    landing("win0", NF, filled, "arr0_0", [order[PLANE]])
    for j in (MATE, FAR):
        d = order[j]
        landing("win0", MW + NF, lambda k: place(k, rank) - NF * slots_before(k, rank), "pre%d" % j, [d])
        act(win(0, filled(d), filled(d) + NF), N("win0", place(d, rank) + (-NF if slots_before(d, rank) else MW), NF))
    landing("win0", MW, lambda k: place(k, rank), "pre1", [order[PLANE]])
    act(N("ce", 0, MW), pick(0, LP + NS, ZB, "k16", 0, 3))
    cp(N("ex", 12, 3), N("win0", LP + NS + 4, 3, LW))
    chain_gather(0, 1)
    finish_gather(0, 1)
    sent_lists(1)
    chain_scan(0, 1)
    finish_scan(0, 1)
    removal(4, 6)
    twice(5)
    twice(4)
    cp(N("l16", 0, 16), N("l16f", 0, 16))
    chain_gather(0, 2)
    b5 = halves(5, "qsb")
    b5[0]()
    chain_scan(0, 2)
    b5[1]()
    send(0, 2)

    sent_lists(0)
    sent_base(N("pq", 128 + 3, NS, 4), 5)
    act(folded(0, 4), folded(0, 4), float(LP - ZB))
    sent_columns(2, 0)
    sent_columns(2, 1)
    coef(5)
    for u in range(U):
        act(N("pq", 128 + 2 * u, NS, 4), sent("cro", 2, u))
    fold(128, 64)
    coef(4)
    ts(N("a1", 0, 12), folded(0, 12), 0.5, O.is_lt, col(1), O.mult)
    base(4, "qsb")
    tt(N("pq", 128 + 5, NR, NS), N("a1", 0, 4), folded(0, 4), O.max)
    tt(N("pq", 128 + 1, NR, NS), N("a1", 8, 4), folded(8, 4), O.max)
    hand_on(1)
    scattered(0, 2)
    term_constants(3, const)
    sent_lists(2)
    removal(6, 7)
    twice(6)
    const("psic0", 0, 64)
    handed(0)
    act(N("ce", MW, MW), X("lq", 3 * NS, "k16", 4, 7))
    others_base(3, 4)
    cp(N("ex", 4, 3), N("lq", 1, 3, NS))
    act(col(2), m8, p16, -8.0)
    act(col(6), m8, float(1 - rank % 2), float(2 * (rank % 2) - 1))
    act(col(7), col(2), 8.0, 2.0)
    act(col(8), m8, float(rank % 2), float(1 - 2 * (rank % 2)))
    act(col(9), col(7), 0.0, col(6))
    const("sq1", 0, 1, 1, float(C))
    act(col(10), N("x3", 48 + rank // 2, 1), col(9), col(8))
    const("idw", 0, 1, 1, float(C))
    act(N("l16f", SENT_AT[0] + block(rank, rank) // 16, NR, 4), R("c16", 0, NR), col(10), col(6))
    for a, n in ((128, 128), (256, 192)):
        act(N("idt", a, n), N("idt", 0, n), float(a))
    arrival(0, 2)

    pair(0, 3, [lambda: cp(N("l16", 16, 16), N("l16f", 16, 16)), lambda: coef(6), lambda: cp(N("l16", 32, 16), N("l16f", 32, 16))])
    send(0, 4)
    iota(R("oc", 0, C), [[3, C]], HD + 2)
    act(R("mskw", 64, 128), R("mskw", 0, 64))
    act(R("scf", 0, 16, 1, 16), R("scb", 0, 16, 1, 16))
    for i in range(8):
        mm(N("pf", 16 * i, 16), R("mskw", 0, 128, 1, 16), R("scf", 0, 16, 1, 16))
    act(N("sq1", 16, F), X("idt", C, "seq16", 4, 8))
    act(N("idw", HD + 2, F, 3), X("idt", C, "seq16", 0, 4))
    act(N("idw", 8, NS, 2), X("sq1", 16 + F, "ix", 2, 4))
    term_constants(5, const)
    const("floor", 0, MW)
    const("win1", 0, 2, 3 * Z + HD + 2)
    const("src", C, 8)
    const("floor", block(rank, rank), CAP, 1, -BIG)
    at = [float(MW * k + block(k, k)) for k in others]
    act(col(11), m8, col(2), at[1] - at[0])
    act(folded(13, 1), col(2), at[2])
    act(folded(12, 1), col(11), at[0])
    scattered(2, 3)
    base(6, "qsb")
    for j, d in enumerate(order):
        tt(N("fo", 64 * j, MW), X("idw", HD + 192, "l16", SENT_AT[0] + 4 * d, SENT_AT[0] + 4 * d + 3), R("mskw", 0, MW), O.mult)
    handed(1)
    act(N("ce", 2 * MW, MW), X("lq", 6 * NS, "k16", 4, 7, 3 * NS))
    others_base(3 * NS + 3, 4)
    cp(N("ex", 8, 3), N("lq", 3 * NS + 1, 3, NS))
    act(R("screp", 0, 128), R("pf", 0, 128))
    arrival(0, 4)
    pair(0, 5, [lambda: fold(0, 96), lambda: scattered(5), lambda: fold(96, 96)])
    scattered(6)
    cp(R("lc", 0, 14), folded(0, 14))

    blocks = ((0, 192), (192, 128), (320, 64), (384, 64))
    for i, (a, n) in enumerate(blocks):
        mm(N("ps", 512 * i, n), R("screp", 0, 128), N("psic0", 64 + a, n))
    for i, (a, n) in enumerate(blocks):
        tt(N("src", a, n), N("ps", 512 * i, n), N("rmb", a, n), O.mult)
    cp(N("ex", 0, 3), N("lq", 3 * NS + 5, 3, NS))
    send(1, 0)
    for j in range(4):
        flux(0, j)
    ts(own(1, 0), X("src", C, "seq16", 0, 4), 0.0, O.max)
    base(3, "src", 0, F, act)
    base(1, "src")
    sent_base(N("pq", LATER[2][1], NS), 3)
    hand_on(2)
    base(2, "src")
    act(N("ps", 0, 128), R("mskw", 0, 128))
    const("invs", C, 64)
    inverse(0, 3)
    arrival(1, 0)

    pair(1, 1, halves(5, "src") + [lambda: sent_base(N("pq", LATER[3][1], NS), 5, cp)])
    send(1, 2)
    hand_on(3)
    base(4, "src", 0, F, act)
    inverse(3, W)
    for j in range(2):
        inverse_masked(j)
    handed(2)
    others_base(LATER[2][3], 1)
    arrival(1, 2)
    pair(1, 3, [lambda a=a: fold(a, 64) for a in (0, 64, 128)])
    send(1, 4)
    base(6, "src", 0, F, act)
    for j in range(2, 4):
        inverse_masked(j)
    fold(192, 128)
    fold(320, 128)
    cp(R("iv", 0, 16), folded(0, 16))
    handed(3)
    others_base(LATER[3][3], 1)
    arrival(1, 4)
    pair(1, 5, [lambda: fold(448, 64), lambda: cp(N("iv", 16, 16), folded(16, 16)), lambda: fill("psic1", 0, 16)])

    for j in range(4):
        gathered(j, act if j % 2 else cp)
    for j in range(4):
        flux(1, j)
    for j in range(4):
        turn(N("yo", j, 32, 4), N("pf", 512 * j, 32))
    for k in range(4):
        a, b = max(0, 128 * k - 64), 128 * k + 64
        q = "y" if k % 2 == 1 else "s"
        add_op(q, lambda q=q, a=a, b=b, k=k: queues[q].dma_start(T.y[:, a:b], T.yo[32 * k:32 * k + 16, 128 - (b - a):128]),
               [[("yo", 0, 128, 1)]], [[("y", a, b, 1)]], "dma", 16)

    emit(g, T, queues, ops)


def meets(x, y, same):
    if x[0] in PSUM and x[0] == y[0] and not same:
        return x[1] // 512 <= (y[2] - 1) // 512 and y[1] // 512 <= (x[2] - 1) // 512
    if x[0] != y[0] or x[1] >= y[2] or y[1] >= x[2]:
        return False
    if x[3] == 1 and y[3] == 1:
        return True
    return not set(range(x[1], x[2], x[3])).isdisjoint(range(y[1], y[2], y[3]))


def clash(a, b):
    if a["q"] == "t" and b.get("opens"):
        return False
    for x in a["w"]:
        for y in b["r"] + b["w"]:
            if meets(x, y, a["q"] == b["q"]):
                return True
    for x in a["r"]:
        for y in b["w"] + (b["r"] if x[0] in PSUM and a["q"] != b["q"] else []):
            if meets(x, y, a["q"] == b["q"]):
                return True
    return False


def plan_waits(ops, clashes, flagged):
    known, issued, start, waits, new, turn, reader = {}, {}, {}, [], set(flagged), {}, {}
    for i in range(len(ops) - 1, -1, -1):
        for j in clashes[i]:
            if ops[j]["q"] == ops[i]["q"]:
                reader[j] = i
    for i, o in enumerate(ops):
        ws = []
        q = o["q"]
        if o["kind"] == "ext":
            start[i] = 0
            waits.append(ws)
            continue
        k = known.get(q, 0)
        mine = issued.setdefault(q, [[] for r in range(KQ.get(q, 1))])
        for j in clashes[i]:
            if k >> j & 1:
                continue
            p = ops[j]
            if p["kind"] == "remote":
                raise ValueError("a call waits for a message's source")
            if p["q"] == q and p["kind"] == "c" and j not in flagged:
                ws.append(("q", (turn[j], len(mine[turn[j]]))))
                for m in mine[turn[j]]:
                    k |= 1 << m | start[m]
            else:
                ws.append(("u", j))
                k |= 1 << j | start[j]
                if p["kind"] == "c":
                    new.add(j)
        start[i] = k
        known[q] = k
        if o["kind"] == "c" and i not in flagged:
            by_age = sorted(range(len(mine)), key=lambda n: mine[n][-1] if mine[n] else -1)
            free = [n for n in by_age if all(k >> m & 1 or reader.get(m, i) <= i for m in mine[n])]
            turn[i] = (free + by_age)[0]
            mine[turn[i]].append(i)
        waits.append(ws)
    return waits, new, turn, start


def emit(g, T, queues, ops):
    flagged, names = set(), {}
    clashes = [[j for j in range(i - 1, -1, -1) if clash(o, ops[j])] for i, o in enumerate(ops)]
    while True:
        waits, new, turn, start = plan_waits(ops, clashes, flagged)
        if new == flagged:
            break
        flagged = new
    own, total, last = 0, {}, {}
    for i, o in enumerate(ops):
        if o["kind"] == "ext":
            names[i], total[i] = o["sem"], o["n"]
        elif o["kind"] == "dma" or i in flagged:
            free = [x for x in last if o["kind"] == "c" and start[i] >> last[x] & 1]
            names[i] = free[0] if free else "x%d" % own
            total[i] = o["n"] + (total[last[free[0]]] if free else 0)
            own += 0 if free else 1
            if o["kind"] == "c":
                last[names[i]] = i
    count, done, sent, waited = {}, {}, 0, set()
    for i, o in enumerate(ops):
        if o["kind"] == "ext":
            continue
        q = o["q"]
        for kind, v in waits[i]:
            if kind == "q":
                queues[q].wait_ge(T.sem["q_%s%d" % (q, v[0])], v[1])
                done[(q, v[0])] = v[1]
            else:
                queues[q].wait_ge(T.sem[names[v]], total[v])
                waited.add(v)
        x = o["fn"]()
        if o["kind"] == "remote":
            sent += o["n"]
        elif i in names:
            x.then_inc(T.sem[names[i]], o["n"])
        else:
            x.then_inc(T.sem["q_%s%d" % (q, turn[i])], 1)
            count[(q, turn[i])] = count.get((q, turn[i]), 0) + 1
    for q, r in count:
        if done.get((q, r), 0) < count[(q, r)]:
            queues[q].wait_ge(T.sem["q_%s%d" % (q, r)], count[(q, r)])
    g.wait_ge(T.sem["sent"], sent)
    for i in total:
        if i not in waited:
            queues[ops[i]["q"]].wait_ge(T.sem[names[i]], total[i])
